import numpy as np, ml_dtypes
CORES = [48,51,52,55]
N = 4
BF = ml_dtypes.bfloat16
def gentries(a):
    return np.ascontiguousarray(a.reshape(8, 16, -1).transpose(0, 2, 1)).reshape(8, -1)
def gtable(e):
    e = np.asarray(e); return np.ascontiguousarray(e.reshape(8, -1, 16).transpose(0, 2, 1)).reshape(128, -1).astype(np.int32)
def f(rng, *shape):
    return (rng.standard_normal(shape, dtype=np.float32) * np.exp2(rng.integers(-2, 3, shape[:-1] + (1,)))).astype(BF)
def wide(rng, *shape):
    v = f(rng, *shape).astype(np.float32); k = shape[:-2] + (1, shape[-1])
    return (v * np.exp2(rng.integers(-6, 7, k)) * (rng.random(k) > 0.0625)).astype(BF)
W, C, LOOK, RO = 8192, 1024, 5, 3
def cuts(rng, least=3):
    room = W - least * C - W // 16
    e = np.sort(rng.integers(0, room + 1, C - 1))
    return least + np.diff(np.concatenate([np.array([0]), e, np.array([room])])).astype(np.int64)
def laid(rng, le, first):
    o = rng.permutation(C); o = np.concatenate([np.array([first]), o[o != first]])
    st = np.zeros(C, np.int64); st[o] = np.add.accumulate(le[o]) - le[o]
    return st
def walk(le):
    cyc = np.repeat(np.arange(C), le)
    return cyc, np.arange(cyc.size) - np.repeat(np.add.accumulate(le) - le, le)
def rings(s, order, st, le):
    cyc, off = walk(le); a, n = st[cyc], le[cyc]
    s[order[a + off]] = order[a + (off + 1) % n] + order[a + (off + n - 1) % n]
    return s, order[st], np.concatenate([order[st + 1], order[st + le - 1]])
def hang(rng, order, st, le, near, mix):
    kid = np.full(W, -1, np.int64)
    a, b = rng.permutation(np.arange(0, C, 2)), rng.permutation(np.arange(1, C, 2))
    m = np.array(a[:mix]); a[:mix] = b[:mix]; b[:mix] = m
    for par, kids in ((0, b), (1, a)):
        i = np.arange(par, C, 2); w = st[i] + 1
        if not near: w = np.concatenate([w, st[i] + 2, (st[i] + 3)[le[i] > 3]])
        kid[order[rng.permutation(w)[:C // 2]]] = kids
    return kid
def skeleton(rng, near, far=()):
    out = []
    for g in range(N * 8):
        order = rng.permutation(W); le = cuts(rng, 5 if g in far else 3); st = laid(rng, le, int(rng.integers(0, C)))
        s, r, e = rings(rng.integers(1, 2 * W - 2, W), order, st, le); tight = near and g % 2 == 1 and g not in far
        out.append((s, r, e, hang(rng, order, st, le, tight, 0 if tight else C // 8)))
    return out
def items(rng):
    a = np.exp2(rng.integers(-2, 3, (N, 128, 1))).astype(np.float32)
    x = rng.standard_normal((N, 128, W), dtype=np.float32) * a
    h = np.repeat(rng.choice(np.array([-0.7, -0.4, -0.1, 0.2], np.float32), (N, 8, RO * C)), 16, axis=1)
    return x, (np.float32(0.7) * rng.standard_normal((N, 128, RO * C), dtype=np.float32) + h) * a
def pat(rng, u):
    m = rng.choice(np.array([1, 3, 5, 7]), u.shape); sh = rng.integers(0, 16, u.shape)
    return ((np.arange(16)[:, None] * m + sh) & 15) < u
def pack(x, q, out):
    s, r, e, k = [np.stack(a) for a in zip(*out)]
    return {"x": np.ascontiguousarray(x.reshape(N, 128, W)).astype(BF), "nsum": s.reshape(N, 8, W).astype(np.int32), "rho": np.stack([gtable(a) for a in r.reshape(N, 8, C)]),
            "nei": np.stack([gtable(a) for a in e.reshape(N, 8, 2 * C)]), "kid": k.reshape(N, 8, W).astype(np.int32), "dem": np.ascontiguousarray(q.reshape(N, 128, RO * C)).astype(BF)}
def setup_inputs(rng):
    x, q = items(rng)
    return pack(x, q, skeleton(rng, False))
def setup_inputs_corners(rng):
    out = []; fit = np.zeros((N * 8, W), bool)
    for g in range(N * 8):
        if g % 8 == 0: modes = rng.permutation(8)
        mode = int(modes[g % 8]); order = rng.permutation(W)
        le = rng.choice(np.array([3, 4, LOOK + 1, LOOK + 2, 2 * LOOK, 2 * LOOK + 1, 2 * LOOK + 2]), C).astype(np.int64)
        le = np.where(np.add.accumulate(le - 3) > W - 3 * C, 3, le)
        if g % 2 == 1: le[rng.integers(0, C)] += W - np.sum(le)
        st = laid(rng, le, int(rng.integers(0, C))); s, r, e = rings(rng.integers(1, 2 * W - 2, W), order, st, le)
        cyc, p = walk(le); k = rng.choice(np.array([0, 0, 1, 2, 3, 4, 5, 5, 6, 6]), C)[cyc]; n = le[cyc]; back = n - p
        fit[g] = rng.random(W) < 0.5
        fit[g, order[st[cyc] + p]] = (p == 0) | ((k == 0) & ((p == LOOK) | (back == LOOK))) | ((k == 1) & ((p == LOOK + 1) | (back == 1))) | ((k == 2) & (p == n // 2)) | (k == 4) | ((k == 5) & ((p == 1) | (back == 1))) | ((k == 6) & (rng.random(p.size) < 0.5))
        kid = np.full(W, -1, np.int64)
        if mode == 0: kid[order[st + 1]] = (np.arange(C) + 1) % C
        elif mode == 2: kid[order[st]] = rng.permutation(C)
        elif mode == 3: kid[order[st + 1]] = np.arange(C)
        elif mode >= 4: kid = hang(rng, order, st, le, mode < 6, 0 if mode < 6 else C // 8)
        out.append((s, r, e, kid))
    fit = fit.reshape(N, 8, 1, W)
    u = np.where(fit, rng.choice(np.array([9, 16]), fit.shape), rng.choice(np.array([0, 8]), fit.shape))
    x = np.where(pat(rng, u), np.float32(1), np.float32(-1)) * (2 + rng.random((N, 8, 16, W), dtype=np.float32))
    q = 2 * rng.random((N, 8, 16, RO * C), dtype=np.float32) - 1
    return pack(x, q + rng.choice(np.array([0, 8, -8], np.float32), (N, 8, 1, RO * C), p=[0.8, 0.1, 0.1]), out)
def setup_inputs_crowd(rng):
    x, q = items(rng); q = q.reshape(N, 8, 16, RO, C); xv = x.reshape(N * 8, 16, W)
    h = int(rng.integers(0, 8)); k = (h + 1) % 8; deep = []
    for r in range(N):
        for t in range(RO):
            o = rng.permutation(8); i = rng.choice(np.array([0, C - 1, C // 2, C // 2 + 1]), 2)
            if t == 0:
                o = o[(o != h) & (o != k)]
                if r == 0:
                    j = int(np.argmax(o % 2)); o[[1, j]] = o[[j, 1]]
                o = np.concatenate([np.array([h]), o]); deep.append(r * 8 + int(o[4])); q[r, o[4], :, 0] = -72
            q[r, o[0], :, t] = 128; q[r, o[1], :, t] = 128; q[r, o[1], :, t, i[0]] = -128
            q[r, o[2], :, t] = -128; q[r, o[3], :, t] = -128; q[r, o[3], :, t, i[1]] = 128
    q[:, k, :, 0, C - 1] = 128; q[:, k, :, 1, C - 1] = -72
    out = skeleton(rng, True, set(deep) | set(r * 8 + k for r in range(N)))
    for r in range(N):
        for g, e in ((deep[r], np.arange(2 * C)), (r * 8 + k, np.array([C - 1, 2 * C - 1]))):
            a = out[g][2][e]; b = out[g][0][a] - out[g][1][e % C]
            xv[g][:, a] -= 96; xv[g][:, b] -= 48
    return pack(x, q, out)
def setup_inputs_ends(rng):
    zig = np.zeros(W, np.int64); zig[0::2] = np.arange(W // 2); zig[1::2] = W - 1 - np.arange(W // 2)
    out = []
    for g in range(N * 8):
        order = zig if g % 2 == 0 else W - 1 - zig; first = C - 1 if (g // 2) % 2 == 1 else 0
        le = cuts(rng); le[first] = max(int(le[first]), 5); st = laid(rng, le, first)
        s, r, e = rings(rng.choice(np.array([1, 2 * W - 3]), W), order, st, le)
        out.append((s, r, e, hang(rng, order, st, le, False, C // 8)))
    u = rng.choice(np.array([0, 8, 9, 16]), (N, 8, 1, W), p=[0.15, 0.25, 0.35, 0.25])
    u[:, 0::2, 0, 0] = 8; u[:, 0::2, 0, W - 1] = 9; u[:, 1::2, 0, 0] = 9; u[:, 1::2, 0, W - 1] = 8
    m = rng.choice(np.array([0, 8, 16]), (N, 8, 1, RO * C), p=[0.15, 0.25, 0.6])
    for g in range(N * 8):
        if (g // 2) % 2 == 0:
            s, r, e, kd = out[g]; a = int(e[0]); b = int(s[a] - r[0]); c = int(s[b] - a)
            u[g // 8, g % 8, 0, a] = 8; u[g // 8, g % 8, 0, b] = 8; u[g // 8, g % 8, 0, c] = 9; u[g // 8, g % 8, 0, int(e[C])] = 9
            kd[r[0]] = kd[a]; kd[a] = -1
            m[g // 8, g % 8, 0, 0] = 0; m[g // 8, g % 8, 0, C] = 16
    return pack(np.where(pat(rng, u), np.float32(1024), np.float32(-1024)), np.where(pat(rng, m), np.float32(1024), np.float32(-1024)), out)
def setup_inputs_spread(rng):
    return pack(wide(rng, N, 128, W), wide(rng, N, 128, RO * C), skeleton(rng, False))
def setup_inputs_ties(rng):
    a = np.exp2(rng.integers(-2, 3, (1, 1, 16, 1))).astype(np.float32)
    m = rng.integers(0, 4, (N, 8, 16, W)); k = rng.integers(0, 4, (N, 8, 16, RO * C)) + rng.choice(np.array([0, 0, 1]), (N, 8, 1, RO * C))
    return pack(a * (1 + m * np.float32(0.0078125)), a * (1 + k * np.float32(0.0078125)), skeleton(rng, False))
def check_inputs(d):
    bad = []
    for k, lo, hi in (("nsum", 1, 2 * W - 3), ("rho", 0, W - 1), ("nei", 0, W - 1), ("kid", -1, C - 1)):
        if np.min(d[k]) < lo or np.max(d[k]) > hi: bad.append("range of " + k)
    for k in ("x", "dem"):
        a = np.abs(d[k].astype(np.float32))
        if not np.all(np.isfinite(a)): bad.append("numbers of " + k + " finite")
        if np.any((a > 0) & (a < 2.0 ** -126)): bad.append("no subnormal number in " + k)
    kd = np.sort(d["kid"].reshape(N * 8, W), axis=1)
    if np.any((kd[:, 1:] == kd[:, :-1]) & (kd[:, 1:] >= 0)): bad.append("no lane twice in a row of kid")
    if bad: return bad
    s = d["nsum"].astype(np.int64).reshape(-1)
    ro = np.stack([gentries(a) for a in d["rho"]]).astype(np.int64).reshape(-1)
    ne = np.stack([gentries(a) for a in d["nei"]]).astype(np.int64).reshape(N * 8, 2, C)
    cur, last = ne[:, 0].reshape(-1), ne[:, 1].reshape(-1); base = np.repeat(np.arange(N * 8) * W, C); prev = ro
    seen = np.zeros(N * 8 * W, np.int64); np.add.at(seen, base + ro, 1)
    good = bool(np.max(seen) == 1 and np.all(s[base + ro] == cur + last) and np.all(cur != last))
    while good and cur.size:
        at = base + cur; np.add.at(seen, at, 1); nx = s[at] - prev; home = nx == ro
        good = not (np.any(seen[at] > 1) or np.any(nx < 0) or np.any(nx >= W) or np.any(home & (cur != last)))
        go = ~home; prev, cur, ro, last, base = cur[go], nx[go], ro[go], last[go], base[go]
    if not good: bad.append("cycles whole and apart")
    return bad
def reach(a, b):
    return np.sum((a >= b).astype(np.int64), axis=-2) >= 9
def reference(x, nsum, rho, nei, kid, dem):
    xs = x.astype(np.float32).reshape(N * 8, 16, W); s = nsum.astype(np.int64).reshape(N * 8, W); kd = kid.astype(np.int64).reshape(N * 8, W)
    ro = np.stack([gentries(a) for a in rho]).astype(np.int64).reshape(N * 8, C)
    ne = np.stack([gentries(a) for a in nei]).astype(np.int64).reshape(N * 8, 2, C)
    q = dem.astype(np.float32).reshape(N * 8, 16, RO, C); lane = np.arange(C)
    live = np.ones((N * 8, C), bool); z = q[:, :, 0]
    for t in range(RO):
        w, pv, emb = [], [], live
        for side in range(2):
            prev, cur = ro, ne[:, side] + 0; stop = ~live; hit = np.zeros((N * 8, C), bool)
            for k in range(LOOK):
                home = cur == ro; fit = reach(np.take_along_axis(xs, cur[:, None, :], 2), z) & ~home
                hit = hit | (fit & ~stop); go = ~(stop | fit | home); stop = ~go
                nxt = np.take_along_axis(s, cur, 1) - prev
                prev, cur = np.where(go, cur, prev), np.where(go, nxt, cur)
            w.append(cur); pv.append(prev); emb = emb & hit
        emb = emb & (w[0] != w[1])
        g, i = np.nonzero(emb)
        for side in range(2):
            s[g, w[side][g, i]] += ro[g, i] - pv[side][g, i]
            ne[g, side, i] = w[side][g, i]
        s[g, ro[g, i]] = w[0][g, i] + w[1][g, i]
        j = np.take_along_axis(kd, w[0], 1); jj = np.maximum(j, 0)
        g, i = np.nonzero(emb & (lane % 2 == t % 2) & (j >= 0) & (jj % 2 != lane % 2) & np.take_along_axis(emb, jj, 1))
        h = jj[g, i]; v = w[0][g, i]; b = s[g, v] - ro[g, i]
        c, d = ne[g, 0, h], ne[g, 1, h]
        keep = np.sum((xs[g, :, c] >= xs[g, :, d]).astype(np.int64), axis=1) >= 9
        c, d = np.where(keep, c, d), np.where(keep, d, c)
        s[g, v] += c - b
        s[g, c] += v - ro[g, h]
        s[g, d] += b - ro[g, h]
        s[g, b] += d - v
        live = live & True; live[g, h] = False
        if t < RO - 1:
            fl = np.roll((~emb).reshape(N, 8, C), 1, axis=0); zc = np.roll(z.reshape(N, 8, 16, C), 1, axis=0)
            fl = np.where(lane % 2 == 1, np.roll(fl, 1, axis=1), fl); zc = np.where(lane % 2 == 1, np.roll(zc, 1, axis=1), zc)
            z = np.where(fl[:, :, None, :], zc, q[:, :, t + 1].reshape(N, 8, 16, C)).reshape(N * 8, 16, C)
    return {"ys": s.reshape(N, 8, W).astype(np.float32), "yn": ne.reshape(N, 8, 2 * C).astype(np.float32), "yl": live.reshape(N, 8, C).astype(np.float32)}

@@ -1,0 +1,680 @@
+from concourse.mybir import AluOpType as OP, ActivationFunctionType as AF
+
+W = 8192
+WD = W + 512
+BF, F32, I32, U16 = "bfloat16", "float32", "int32", "uint16"
+SB = {
+    "X": (W, BF), "A0": (W, BF), "KW": (W, BF), "A": (WD, F32), "B": (WD, F32),
+    "D0": (1024, BF), "ZW1": (3072, BF), "ZW2": (3072, BF), "Z1": (1024, BF), "Z2": (1024, BF),
+    "NS": (512, I32), "NH": (512, BF), "NL": (512, BF), "NHF": (512, F32), "NLF": (512, F32),
+    "KD": (512, I32), "ZN": (512, F32), "BN": (512, F32),
+    "RN": (192, I32), "RNF": (192, F32), "PM": (512, F32), "EO": (512, F32), "I32P": (128, F32), "I32N": (128, F32),
+    "IB": (128 * 10, BF), "ZS": (16 * 144, BF), "ZP": (5 * 144, BF), "ONE": (48, BF),
+    "PI": (2, I32), "PF": (4, F32), "ST": (32 * 10, F32),
+    "C": (6 * 384 + 256, F32), "U": (6 * 384 + 256, U16), "R": (64, F32), "RU": (64, U16), "RH": (128, BF),
+    "GS": (4096, BF), "CM": (4096, BF), "SG": (256, BF), "OV": (192, BF), "DD": (64 * 4, BF),
+    "M": (256, F32), "MN": (256, I32), "WN": (256, I32), "M2": (384, I32), "M3": (384, I32),
+    "E": (192, F32), "NE": (64, BF), "FS": (128, U16), "FO": (128, U16),
+    "VC": (64, F32), "VH": (64, BF), "VL": (64, BF), "WS": (2048, F32), "WE": (1024, F32),
+    "UB": (96, U16), "GK": (1024, BF), "PT": (32 * 6, F32), "LH": (128, BF), "LT": (1024, BF),
+    "LL": (128, BF), "LO": (32, U16), "LS": (512, BF), "LW": (1536, BF), "LI": (128, F32),
+    "Q": (32 * 20, F32), "QO": (64, U16), "GX": (512, BF), "CK": (512, BF), "V4": (128, F32), "H4": (128, BF),
+    "L4": (128, BF), "RV": (64, F32), "RVH": (64, BF), "RVL": (64, BF), "OB": (256, F32),
+}
+SCRATCH = {k: ("sbuf", [128, v[0]], v[1]) for k, v in SB.items()}
+for _i in range(8):
+    SCRATCH["P%d" % _i] = ("psum", [128, 512], "float32")
+SEMAPHORES = ["ev", "es", "et", "eg", "sent"] + ["d%d" % i for i in range(40)] + ["a%d" % i for i in range(6)]
+
+CY, PCY, GA, SC, HOP = 1.04, 0.52, 1.56, 3.8, 70.0
+PARAM = {'delta': 30, 'flexv': 1, 'iters': 4, 'split': 0, 'roots': 'sv', 'boost': [700.0, 39600.0, -1300.0, 0.0, -3300.0, 1600.0, 4000.0, -200.0, 6700.0, 1100.0, 7100.0, 0.0, 0.0, 0.0, 100.0, 4700.0, 400.0, 2700.0, 1800.0, -2500.0, 10500.0, 12300.0, 18500.0], 'noise': 0, 'seed': 11}
+
+
+def meet(a, b):
+    if len(a) > 3 and len(b) > 3 and a[3] == b[3] and (a[1] - b[1]) % a[3]:
+        return False
+    return a[1] < b[2] and b[1] < a[2]
+
+
+def build():
+    ops = []
+    acc = {}
+    tag = [0]
+
+    def sz(a):
+        return (a[2] - a[1] + (a[3] if len(a) > 3 else 1) - 1) // (a[3] if len(a) > 3 else 1)
+
+    def ps(a):
+        return a[0][0] == "P" and a[0][1:].isdigit()
+
+    def add(alts, rd, wr, after=(), lat=0.0, kind="c", pri=0.0):
+        o = {"n": len(ops), "alts": alts, "rd": rd, "wr": wr, "lat": lat, "kind": kind, "pri": pri, "tag": tag[0]}
+        dep = set(x["n"] for x in after)
+        for a, w in [(a, 0) for a in rd] + [(a, 1) for a in wr]:
+            if a[0] in ("A", "B"):
+                continue
+            for (n, a2, w2) in acc.get(a[0], ()):
+                if (w or w2) and meet(a, a2):
+                    dep.add(n)
+        for a, w in [(a, 0) for a in rd] + [(a, 1) for a in wr]:
+            acc.setdefault(a[0], []).append((o["n"], a, w))
+        o["dep"] = dep
+        ops.append(o)
+        return o
+
+    def two(*aps):
+        return all((not ps(a)) and SB[a[0]][1] in (BF, U16) for a in aps)
+
+    def vc(n):
+        return 50.0 + max(64, n) * CY
+
+    def tt(out, a, b, op):
+        n = sz(out) * (1 if ps(a) or ps(b) else 2)
+        return add([("v", vc(n), lambda q, T, r: [q.tensor_tensor(r(out), r(a), r(b), op)])], [a, b], [out])
+
+    def ts(out, a, s1, s2, op0, op1=None):
+        n = sz(out) * (0.5 if two(out, a) else 1)
+        rd = [a] + [s for s in (s1, s2) if isinstance(s, tuple)]
+
+        def em(q, T, r):
+            x1 = r(s1) if isinstance(s1, tuple) else s1
+            if op1 is None:
+                return [q.tensor_scalar(r(out), r(a), x1, None, op0)]
+            return [q.tensor_scalar(r(out), r(a), x1, r(s2) if isinstance(s2, tuple) else s2, op0, op1)]
+        return add([("v", vc(n), em)], rd, [out])
+
+    def cp(out, a):
+        n = sz(out) * (0.5 if two(out, a) else 1)
+        return add([("v", vc(n), lambda q, T, r: [q.tensor_copy(r(out), r(a))])], [a], [out])
+
+    def ms(out, val, pri=0.0):
+        n = sz(out) * (0.5 if two(out) else 1)
+        return add([("v", vc(n), lambda q, T, r: [q.memset(r(out), val)])], [], [out], pri=pri)
+
+    def flex(out, a, bias=0.0, engs="sv", scale=1.0):
+        n = sz(out)
+        col = isinstance(bias, tuple)
+        alts = []
+        if "s" in engs:
+            alts.append(("s", 15.0 + vc(n), lambda q, T, r: [q.activation(r(out), r(a), AF.Identity, bias=r(bias) if col else bias, scale=scale)]))
+        if "v" in engs:
+            alts.append(("v", vc(n), lambda q, T, r: [q.tensor_scalar(r(out), r(a), r(bias) if col else bias, None, OP.add)]))
+        return add(alts, [a] + ([bias] if col else []), [out])
+
+    def gat(out, win, off, engs="s", after=()):
+        n = sz(out)
+        alts = []
+        if "s" in engs:
+            alts.append(("s", 65.0 + n * GA * CY, lambda q, T, r: [q.activation(r(out), r(win).indirect(r(off)), AF.Copy)]))
+        if "v" in engs:
+            alts.append(("v", 50.0 + n * GA * CY, lambda q, T, r: [q.tensor_copy(r(out), r(win).indirect(r(off)))]))
+        return add(alts, [win, off], [out], after)
+
+    def cmpg(out, off, z):
+        return add([("v", 50.0 + sz(out) * GA * CY, lambda q, T, r: [q.tensor_tensor(r(out), r(("X", 0, W)).indirect(r(off)), r(z), OP.is_ge)])],
+                   [("X", 0, W), off, z], [out])
+
+    def scat(win, off, src, eng, after=()):
+        if eng == "s":
+            em = lambda q, T, r: [q.activation(r(win).indirect(r(off)), r(src), AF.Silu)]
+        else:
+            em = lambda q, T, r: [q.tensor_copy(r(win).indirect(r(off)), r(src))]
+        return add([(eng, 60.0 + sz(src) * SC * CY, em)], [off, src], [win], after)
+
+    def pe(groups, first=True, last=True):
+        cost, rd, wr = 60.0, [], []
+        for grp in groups:
+            for (o, l, x) in grp:
+                cost += max(64, sz(x)) * PCY * (4 if SB[x[0]][1] == F32 else 1)
+                for lst, a in ((rd, l), (rd, x[:3]), (wr, o)):
+                    if a not in lst:
+                        lst.append(a)
+
+        def em(q, T, r):
+            res = []
+            for grp in groups:
+                for i, (o, l, x) in enumerate(grp):
+                    res.append(q.matmul(r(o), r(l), r(x), first and i == 0, last and i == len(grp) - 1))
+            return res
+        return add([("t", cost, em)], rd, wr)
+
+    def pew(groups, per):
+        for i in range(0, len(groups), per):
+            pe(groups[i:i + per])
+
+    def zero(a):
+        return add([("g", 130.0 + 2 * sz(a) * CY, lambda q, T, r: [q.iota(r(a), [[0, sz(a)]], 0, 0, allow_small_or_imprecise_dtypes=True)])], [], [a])
+
+    def gp(n, em, rd, wr, pri=0.0):
+        return add([("g", 170.0 + 2 * n * CY, em)], rd, wr, pri=pri)
+
+    def dma(pairs, rd, wr, nbytes, after=(), q="y", pri=0.0):
+        return add([(q, 100.0 * len(pairs), lambda e, T, r: [e.dma_start(a(T), b(T)) for a, b in pairs])], rd, wr, after,
+                   lat=2000.0 + nbytes / 200.0, kind="d", pri=pri)
+
+    def send(src, dst, k):
+        s = add([("g", 300.0, (src, dst, k))], [src], [], kind="s")
+        return add([("n", 0.0, k)], [], [dst], [s], lat=2200.0 + sz(src) * 256 / 150.0, kind="r")
+
+    def sel(buf, base, r):
+        return (buf, base + 15 - r, base + 143 - r)
+
+    def to_list(out, wide, zset):
+        return [(out, sel("ZP", 144 * zset, r), (wide[0], wide[1] + r, wide[2], 16)) for r in range(16)]
+
+    def to_wide(bank, lists):
+        return [[((bank, r, 512, 16), sel("ZS", 144 * r, row), a) for a, row in lists] for r in range(16)]
+
+    def b32(name, i, n=1):
+        return (name, 32 * i, 32 * (i + n))
+
+    ALL = 4
+    IBM = lambda i: ("IB", 128 * i, 128 * i + 128)
+    IP, IN = ("I32P", 0, 128), ("I32N", 0, 128)
+    UF, DUM, LDUM = b32("ST", 0), b32("ST", 1), b32("ST", 3)
+    LN = [b32("ST", 4), b32("ST", 5)]
+    BA = ("PF", 1, 2)
+
+    def slot(t, h):
+        return (t * 2 + h) * 384 if t < 3 else 6 * 384 + 128 * h
+
+    def Cc(t, h, k, s=None):
+        o = slot(t, h) + (k - 1) * 64
+        return ("C", o, o + 64) if s is None else ("C", o + 32 * s, o + 32 * s + 32)
+
+    def Uu(t, h, k, s=None):
+        o = slot(t, h) + (0 if k == 1 else 64 if k == 0 else k * 64)
+        return ("U", o, o + 64) if s is None else ("U", o + 32 * s, o + 32 * s + 32)
+
+    dma([(lambda T: T.RN[:, 0:64], lambda T: T.rho[:]), (lambda T: T.RN[:, 64:192], lambda T: T.nei[:])], [], [("RN", 0, 192)], 98304, pri=9e5)
+    dma([(lambda T: T.NS[:], lambda T: T.nsum[:])], [], [("NS", 0, 512)], 262144, q="s", pri=9e5)
+    dma([(lambda T: T.KD[:], lambda T: T.kid[:])], [], [("KD", 0, 512)], 524288, q="s", pri=8.5e5)
+    lx = dma([(lambda T: T.X[:], lambda T: T.x[:])], [], [("X", 0, W)], 2400000, pri=8e5)
+    ld = dma([(lambda T: T.D0[:], lambda T: T.dem[:, 0:1024])], [], [("D0", 0, 1024)], 600000, q="s", pri=8e5)
+    ms(("ZN", 0, 512), 0.0, 9e5)
+    for i in range(2):
+        zero(("ZS", 1152 * i, 1152 * i + 1152))
+    ms(("ZP", 0, 720), 0.0)
+    ms(("ONE", 0, 48), 1.0)
+    for i in range(5):
+        ms(("A0", 1024 * i, 1024 * i + 1024), 0.0)
+    for i in range(10, 16):
+        flex(("A0", 512 * i, 512 * i + 512), ("ZN", 0, 512), 0.0, "s")
+
+    def diag(out, src, pat, fill, base, cm=1):
+        return gp(sz(out), lambda q, T, r: [q.affine_select(r(out), r(src), pat, OP.not_equal, fill, base, cm)], [src], [out])
+
+    def band(out, src, pat, base, cm):
+        return gp(sz(out), lambda q, T, r: [q.affine_select(r(out), r(src), pat, OP.is_ge, 0.0, base, cm)], [src], [out])
+
+    z128 = ("ZN", 0, 128)
+    for h in range(2):
+        for b in range(2):
+            diag(("PM", 128 * (2 * h + b), 128 * (2 * h + b + 1)), z128, [[-16, 8], [1024, 2], [-2, 8]], 1.0, -h - 1024 * b)
+    diag(IN, z128, [[-1, 128]], -1.0, 0)
+    diag(IP, z128, [[-1, 128]], 1.0, 0)
+    zp4, zpa = ("ZP", 15, 576, 16), ("ZP", 591, 720, 16)
+    band(zp4, ("ONE", 0, 36), [[-2, 4], [-16, 9]], 0, 1)
+    band(zp4, zp4, [[2, 4], [16, 9]], 1, -1)
+    band(zpa, ("ONE", 0, 9), [[-16, 9]], 0, 1)
+    band(zpa, zpa, [[16, 9]], 15, -1)
+    zs = ("ZS", 15, 2304, 16)
+    diag(zs, zs, [[-1, 16], [-16, 9]], 1.0, 0)
+    for k in range(5):
+        flex(IBM(k), IP, 0.0, "s", float(2 ** 18 * (5 - k)))
+    flex(IBM(5), IP, 0.0, "s", -64.0)
+    flex(IBM(6), IP, 0.0, "s", float(2 ** 21))
+    flex(("IB", 896 + 16, 1024), ("I32P", 0, 112), 0.0, "s", 2048.0)
+    flex(("IB", 896, 896 + 16), ("I32P", 112, 128), 0.0, "s", 2048.0)
+    flex(IBM(8), IP, 0.0, "s", 1024.0)
+    flex(("IB", 1152, 1154), ("ZN", 0, 2), 0.0, "s")
+    flex(("IB", 1154, 1280), ("I32P", 0, 126), 0.0, "s")
+    for h in range(2):
+        diag(("EO", 256 * h, 256 * h + 256), ("ZN", 0, 256), [[-16, 8], [-1, 16], [1024, 2]], 1.0, -1024 * h)
+    gp(1, lambda q, T, r: [q.iota(r(("PI", 0, 1)), [[0, 1]], 0, 1)], [], [("PI", 0, 1)])
+    gp(32, lambda q, T, r: [q.iota(r(b32("ST", 8)), [[16, 32]], 0, 0, allow_small_or_imprecise_dtypes=True)], [], [b32("ST", 8)])
+    ts(("PI", 1, 2), ("PI", 0, 1), 15, None, OP.bitwise_and)
+    cp(("PF", 0, 1), ("PI", 1, 2))
+    ts(BA, ("PF", 0, 1), 1.0, 128.0, OP.is_equal, OP.mult)
+    ts(UF, b32("ST", 8), ("PF", 0, 1), None, OP.add)
+    ts(DUM, UF, float(W), None, OP.add)
+    ts(b32("ST", 2), UF, float(W), None, OP.add)
+    ts(LDUM, UF, 1024.0, None, OP.add)
+    for h in range(2):
+        ts(LN[h], UF, 2.0, float(h), OP.mult, OP.add)
+
+    ts(("NH", 0, 512), ("NS", 0, 512), 64.0, None, OP.add)
+    tt(("NL", 0, 512), ("NS", 0, 512), ("NH", 0, 512), OP.subtract)
+    wa = dma([(lambda T: T.A0[0:128:16, :], lambda T: T.NH[:]), (lambda T: T.A0[1:128:16, :], lambda T: T.NL[:])],
+             [("NH", 0, 512), ("NL", 0, 512)], [("A0", 0, W)], 262144)
+    flex(("NHF", 0, 512), ("NH", 0, 512), 0.0, "s")
+    flex(("NLF", 0, 512), ("NL", 0, 512), 128.0, "s")
+    za = []
+    for i in range(8):
+        a = ("A", 1024 * i, 1024 * i + 1024)
+        za.append(zero(a))
+    ia = dma([(lambda T: T.A[0:128:16, 0:W], lambda T: T.NHF[:]), (lambda T: T.A[1:128:16, 0:W], lambda T: T.NLF[:])],
+             [("NHF", 0, 512), ("NLF", 0, 512)], [("A", 0, W)], 524288, za)
+    late_loads = [lx, ld, wa]
+    dma([(lambda T: T.KW[:], lambda T: T.x[:])], [], [("KW", 0, W)], 2600000, late_loads)
+    dma([(lambda T: T.ZW1[:, 0:1024], lambda T: T.dem[:, 1024:2048]), (lambda T: T.ZW2[:, 0:1024], lambda T: T.dem[:, 2048:3072])],
+        [], [("ZW1", 0, 1024), ("ZW2", 0, 1024)], 3000000, late_loads)
+    ib = dma([(lambda T: T.B[0:128:16, 0:W], lambda T: T.ZN[:])], [("ZN", 0, 512)], [("B", 0, W)], 3200000, late_loads)
+    ts(("KD", 0, 512), ("KD", 0, 512), 2047, None, OP.bitwise_and)
+    cp(("CK", 0, 512), ("KD", 0, 512))
+    tt(("GX", 0, 512), ("KD", 0, 512), ("CK", 0, 512), OP.subtract)
+    dma([(lambda T: T.KW[0:128:16, :], lambda T: T.CK[:]), (lambda T: T.KW[1:128:16, :], lambda T: T.GX[:])],
+        [("CK", 0, 512), ("GX", 0, 512)], [("KW", 0, W)], 262144)
+
+    cp(("RNF", 0, 192), ("RN", 0, 192))
+    for h in range(2):
+        bk = "P%d" % (4 + h)
+        pe([[((bk, 0, 96), ("PM", 128 * (2 * h + b), 128 * (2 * h + b + 1)), ("RNF", b, 192, 2)) for b in range(2)]])
+        cp(Uu(0, h, 1), (bk, 32, 96))
+        flex(Cc(0, h, 1), (bk, 32, 96))
+        flex(b32("R", h), (bk, 0, 32))
+    cp(("RU", 0, 64), ("R", 0, 64))
+    flex(("RH", 0, 64), ("RNF", 0, 64))
+    tt(("RH", 64, 128), ("RNF", 0, 64), ("RH", 0, 64), OP.subtract)
+    for i in range(2):
+        bk = "P%d" % (6 + i)
+        pew(to_wide(bk, [(b32("RH", i), 0), (b32("RH", 2 + i), 1), (b32("RH", i), 6), (b32("RH", 2 + i), 7)]), 4)
+        flex(("LT", 512 * i, 512 * i + 512), (bk, 0, 512))
+
+    send(("D0", 0, 1024), ("ZW1", 1024, 2048), 0)
+    dma([(lambda T: T.ZW1[16:128, 2048:3072], lambda T: T.ZW1[0:112, 1024:2048]), (lambda T: T.ZW1[0:16, 2048:3072], lambda T: T.ZW1[112:128, 1024:2048])],
+        [("ZW1", 1024, 2048)], [("ZW1", 2048, 3072)], 262144)
+
+    wbank = [0]
+
+    def nb_():
+        wbank[0] ^= 1
+        return "P%d" % (6 + wbank[0])
+
+    def write_a(hh, ll, off, stage, after):
+        bk = nb_()
+        pew(to_wide(bk, [(hh, 0), (ll, 1)]), 8)
+        flex(stage, (bk, 0, 512), BA)
+        return scat(("A", 0, WD), off, stage, "s", after)
+
+    def write_b(hh, ll, off, stage, after):
+        bk = nb_()
+        pew(to_wide(bk, [(hh, 0), (ll, 0)]), 8)
+        flex(stage, (bk, 0, 512), 32896.0)
+        return scat(("B", 0, WD), off, stage, "v", after)
+
+    early, late, bw = {}, {-1: []}, []
+    dead = [b32("DD", 0), b32("DD", 1)]
+
+    def walks(t, h):
+        isp = h == t % 2
+        old = t == 0 or (t == 1 and isp)
+        win, off = (("A0", 0, W), 0.0) if old else (("A", 0, W), -128.0)
+        after = [] if old else [ia] if isp else early[t - 1] + late[t - 1]
+        sb, cb, kb = "P%d" % h, "P%d" % (2 + h), "P%d" % (4 + h)
+        z = ("Z%d" % t if t else "D0", h, 1024, 2)
+        m = ("M", 128 * h, 128 * h + 128)
+        for k in range(1, 6):
+            if t > 0 and not isp and PARAM["split"]:
+                for s in range(2):
+                    o_ = 2048 * h + 1024 * (k % 2) + 512 * s
+                    sp = ("P%d" % s, 32 * s, 32 * s + 32)
+                    gat(("GS", o_, o_ + 512), win, Uu(t, h, k, s), "s", after[:4] if k == 1 else after)
+                    pe([to_list(sp, ("GS", o_, o_ + 512), 0) + [(sp, IN, Cc(t, h, k - 1, s) if k > 1 else b32("R", h))]])
+                    if k < 5:
+                        ts(Uu(t, h, k + 1, s), sp, off, float(W - 1), OP.add, OP.min)
+                    flex(Cc(t, h, k + 1, s), sp, off)
+            elif k > 1 or t == 0 or not isp:
+                g_ = ("GS", 2048 * h + 1024 * (k % 2), 2048 * h + 1024 * (k % 2) + 1024)
+                gat(g_, win, Uu(t, h, k), "sv" if old else "s", after[:4] if k == 1 else after)
+                prev = [((sb, 0, 64), IN, Cc(t, h, k - 1))] if k > 1 else [((sb, 32 * s, 32 * s + 32), IN, b32("R", h)) for s in range(2)]
+                pe([to_list((sb, 0, 64), g_, 0) + prev])
+                if k < 5:
+                    ts(Uu(t, h, k + 1), (sb, 0, 64), off, float(W - 1), OP.add, OP.min)
+                flex(Cc(t, h, k + 1), (sb, 0, 64), off)
+            if 2 <= k <= 4:
+                tt(b32("OV", 3 * h + k - 2), Cc(t, h, k, 0), Cc(t, h, 1, 1), OP.is_equal)
+            c_ = 2048 * h + 1024 * (k % 2)
+            for s in range(2):
+                cmpg(("CM", c_ + 512 * s, c_ + 512 * s + 512), Uu(t, h, k, s), z)
+            blk = [b32("OV", 3 * h + j - 2) for j in range(2, k)] + ([dead[h]] if t > 1 or (t == 1 and isp) else [])
+            pe([to_list((cb, 0, 64), ("CM", c_, c_ + 1024), ALL) + [((cb, 0, 32), IBM(5), a) for a in blk]])
+            sg = ("SG", 128 * h + 64 * (k % 2), 128 * h + 64 * (k % 2) + 64)
+            add([("s", 15.0 + vc(64), lambda q, T, r, sg=sg: [q.activation(r(sg), r((cb, 0, 64)), AF.Sign, bias=-8.5)])], [(cb, 0, 64)], [sg])
+            ck = Cc(t, h, k)
+            pe([[((kb, 0, 128), IP, ("C", ck[1], ck[1] + 128)), ((kb, 0, 64), IBM(k - 1), sg), ((kb, 64, 128), IBM(k - 1), sg)]])
+            if k == 1:
+                flex(m, (kb, 0, 128))
+            else:
+                tt(m if k < 5 else ("MN", 128 * h, 128 * h + 128), (kb, 0, 128), m, OP.max)
+
+    def embed(t, h):
+        isp = h == t % 2
+        kb = "P%d" % (4 + h)
+        mn = lambda i, n=1: b32("MN", 4 * h + i, n)
+        wn = lambda i, n=1: b32("WN", 4 * h + i, n)
+        ne = b32("NE", h)
+        ts(wn(0, 4), mn(0, 4), 16383, None, OP.bitwise_and)
+        tt(b32("E", 3 * h), mn(0), mn(1), OP.min)
+        tt(b32("E", 3 * h + 1), wn(0), wn(1), OP.not_equal)
+        tt(b32("E", 3 * h + 2), b32("E", 3 * h), b32("E", 3 * h + 1), OP.min)
+        ts(ne, b32("E", 3 * h + 2), 0.5, None, OP.is_lt)
+        parts = [(Cc(t, h, 1), mn(0, 2)), (b32("ST", 1, 2), mn(0, 2))] + ([(Cc(t, h, 2), mn(2, 2))] if not isp and t < 2 else [])
+        pe([[((kb, 64 * i, 64 * i + 64), IP, a)] + [((kb, 64 * i + 32 * s, 64 * i + 32 * s + 32), IBM(6), ne) for s in range(2)]
+            for i, (a, _) in enumerate(parts)])
+        o = 192 * h
+        for i, (_, mm) in enumerate(parts):
+            tt(("M2", o + 64 * i, o + 64 * i + 64), (kb, 64 * i, 64 * i + 64), mm, OP.max)
+        ts(("M3", o, o + 64 * len(parts)), ("M2", o, o + 64 * len(parts)), 16383, None, OP.bitwise_and)
+        u1 = Uu(t + 1, h, 1)
+        cp(("U", u1[1], u1[1] + 128), ("M3", o, o + 128))
+        cp(Cc(t + 1, h, 1), ("M3", o, o + 64))
+        if len(parts) == 3:
+            ts(Uu(t + 1, h, 2), ("M3", o + 128, o + 192), float(W - 1), None, OP.min)
+            cp(Cc(t + 1, h, 2), ("M3", o + 128, o + 192))
+        if t < 2:
+            src = ("P%d" % (2 + h), 64, 96)
+            pe([[(src, IP, LN[h]), (src, IBM(8 - h), ne)]])
+            cp(b32("FS", 2 * t + h), src)
+            send(b32("FS", 2 * t + h), b32("FO", 2 * t + h), 2 + 2 * t + h)
+            gat(("Z%d" % (t + 1), h, 1024, 2), ("ZW%d" % (t + 1), 0, 3072), b32("FO", 2 * t + h), "sv")
+
+    def roots(h):
+        tt(b32("RV", h), Cc(3, h, 1, 0), Cc(3, h, 1, 1), OP.add)
+        flex(b32("RVH", h), b32("RV", h), 64.0)
+        tt(b32("RVL", h), b32("RV", h), b32("RVH", h), OP.subtract)
+        st = ("BN" if h else "PM", 0, 512)
+        if PARAM["roots"][h] == "v":
+            bw.append(write_b(b32("RVH", h), b32("RVL", h), b32("RU", h), st, [ib]))
+        else:
+            early[2].append(write_a(b32("RVH", h), b32("RVL", h), b32("RU", h), st, late[1]))
+
+    def parents(t):
+        h = t % 2
+        q_ = 1 - h
+        wn = lambda i, n=1: b32("WN", 4 * h + i, n)
+        R, ne, sb = b32("R", h), b32("NE", h), "P%d" % h
+        pt = lambda i: b32("PT", i)
+        old = t < 2
+        ts(("UB", 0, 96), wn(0, 3), float(W - 1), None, OP.min)
+        gat(("GK", 512, 1024), ("A0", 0, W) if old else ("A", 0, W), b32("UB", 2), "sv" if old else "s")
+        gat(("GK", 0, 512), ("KW", 0, W), b32("UB", 0), "sv")
+        pe([to_list((sb, 96, 128), ("GK", 512, 1024), 0) + ([] if old else [((sb, 96, 128), IBM(5), ("ONE", 0, 32))] * 2)])
+        pe([to_list((sb, 64, 96), ("GK", 0, 512), 0) + [((sb, 64, 96), IBM(6), ne)]])
+        tt(pt(0), (sb, 96, 128), wn(0), OP.subtract)
+        tt(pt(1), wn(2), wn(1), OP.is_equal)
+        tt(pt(2), R, pt(0), OP.subtract)
+        tt(pt(3), pt(2), pt(1), OP.mult)
+        tt(pt(4), pt(3), pt(0), OP.add)
+        flex(b32("LH", 3), pt(4))
+        tt(b32("LL", 3), pt(4), b32("LH", 3), OP.subtract)
+        cp(b32("LH", 0, 3), wn(0, 3))
+        tt(b32("LL", 0, 3), wn(0, 3), b32("LH", 0, 3), OP.subtract)
+        tt(pt(5), (sb, 64, 96), LDUM, OP.min)
+        cp(("LO", 0, 32), pt(5))
+        bk = nb_()
+        mm = [((bk, 0, 512), IBM(9), ("LT", h, 1024, 2))]
+        for lists in ([(b32("LH", 0), 0), (b32("LL", 0), 1)], [(b32("LH", 2), 6), (b32("LL", 2), 7)], [(b32("LH", 3), 4), (b32("LL", 3), 5)]):
+            mm += [x for grp in to_wide(bk, lists) for x in grp]
+        cuts = [0, 1, 17, 33, 49, 65, 81, 97]
+        for i in range(7):
+            pe([mm[cuts[i]:cuts[i + 1]]], i == 0, i == 6)
+        flex(("LS", 0, 512), (bk, 0, 512))
+        dma([(lambda T: T.LW[:, 0:1024], lambda T: T.LT[:])], [("LT", 0, 1024)], [("LW", 0, 1024)], 262144)
+        scat(("LW", 0, 1536), ("LO", 0, 32), ("LS", 0, 512), "v")
+        for i in range(4):
+            pe([[((sb, 128 + 32 * i, 160 + 32 * i), sel("ZP", 144 * i, r), ("LW", 2 * r + q_, 1024, 32)) for r in range(16)]])
+        flex(("LI", 0, 128), (sb, 128, 256))
+        tag[0] += 1
+        for s in range(2):
+            tt(b32("VC", s), wn(2 + s), R, OP.add)
+        flex(("VH", 0, 64), ("VC", 0, 64), 64.0)
+        tt(("VL", 0, 64), ("VC", 0, 64), ("VH", 0, 64), OP.subtract)
+        early[t] = [write_a(b32("VH", s), b32("VL", s), Uu(t + 1, h, 0, s), ("WE", 512 * s, 512 * s + 512), [ia] + late[t - 1]) for s in range(2)]
+        Q = lambda i, n=1: b32("Q", i, n)
+        li = lambda i: b32("LI", i)
+        tt(Q(1), li(0), b32("R", q_), OP.is_equal)
+        tt(Q(6), li(0), li(3), OP.subtract)
+
+    def children(t):
+        h = 1 - t % 2
+        wn = lambda i, n=1: b32("WN", 4 * h + i, n)
+        Q = lambda i, n=1: b32("Q", i, n)
+        li = lambda i: b32("LI", i)
+        ne, cb = b32("NE", h), "P%d" % (2 + h)
+        n0, n1 = Cc(t + 1, h, 1, 0), Cc(t + 1, h, 1, 1)
+        gat(("GX", 0, 512), ("X", 0, W), Uu(t + 1, h, 1, 1), "sv")
+        cmpg(("CK", 0, 512), Uu(t + 1, h, 1, 0), ("GX", 0, 512))
+        pe([to_list((cb, 96, 128), ("CK", 0, 512), ALL)])
+        tt(Q(7), n0, n1, OP.subtract)
+        tt(Q(11), wn(2), li(3), OP.add)
+        tt(Q(12), li(1), n1, OP.add)
+        tt(Q(13), wn(3), li(0), OP.add)
+        tt(Q(14), li(2), n0, OP.add)
+        ns = Cc(3, 0, 2, 0) if t == 1 else Q(18)
+        tt(ns, Q(1), ne, OP.max)
+        tt(Q(15), ns, DUM, OP.mult)
+        tt(Q(16), li(0), Q(15), OP.max)
+        tt(Q(17), li(3), Q(15), OP.max)
+        cp(("QO", 0, 64), Q(16, 2))
+        if t < 2:
+            ts(dead[h], ns, -1.0, 1.0, OP.mult, OP.add)
+        else:
+            tt(Cc(3, 1, 2, 0), ns, dead[h], OP.is_gt)
+        ts(Q(19), (cb, 96, 128), 9.0, None, OP.is_ge)
+        tt(Q(6), Q(6), Q(19), OP.mult)
+        tt(Q(7), Q(7), Q(19), OP.mult)
+        tt(("V4", 0, 64), Q(11, 2), Q(6, 2), OP.add)
+        tt(("V4", 64, 128), Q(13, 2), Q(6, 2), OP.subtract)
+        for i in range(2):
+            flex(b32("H4", 2 * i, 2), b32("V4", 2 * i, 2), 64.0)
+            tt(b32("L4", 2 * i, 2), b32("V4", 2 * i, 2), b32("H4", 2 * i, 2), OP.subtract)
+        offs = [Uu(t + 1, h, 0, 0), b32("QO", 0), Uu(t + 1, h, 0, 1), b32("QO", 1)]
+        late[t] = []
+        for i in ((1, 3, 0, 2) if t < 2 else (1, 0, 3, 2)):
+            st = ("WS", 512 * i, 512 * i + 512)
+            if t == 2 and i % 2 == 1:
+                bw.append(write_b(b32("H4", i), b32("L4", i), offs[i], st, [ib]))
+            else:
+                late[t].append(write_a(b32("H4", i), b32("L4", i), offs[i], st, [ia] + (early[t] if i % 2 == 1 else [])))
+
+    for t in range(3):
+        p_ = t % 2
+        tag[0] = 1 + 7 * t
+        walks(t, p_)
+        tag[0] += 1
+        walks(t, 1 - p_)
+        tag[0] += 1
+        embed(t, p_)
+        tag[0] += 1
+        parents(t)
+        if t == 2:
+            roots(p_)
+        tag[0] += 1
+        embed(t, 1 - p_)
+        if t == 2:
+            roots(1 - p_)
+        tag[0] += 1
+        children(t)
+        tag[0] += 1
+        if t == 0:
+            send(("Z1", 0, 1024), ("ZW2", 1024, 2048), 1)
+            dma([(lambda T: T.ZW2[16:128, 2048:3072], lambda T: T.ZW2[0:112, 1024:2048]), (lambda T: T.ZW2[0:16, 2048:3072], lambda T: T.ZW2[112:128, 1024:2048])],
+                [("ZW2", 1024, 2048)], [("ZW2", 2048, 3072)], 262144)
+
+    lo = [Cc(3, h, 1)[1] for h in range(2)]
+    add([("t", 60.0 + 2048 * PCY, lambda q, T, r: [q.matmul(T.P2[0:96, 256:512], T.C[:, lo[h]:lo[h] + 96], T.EO[:, 256 * h:256 * h + 256], h == 0, h == 1) for h in range(2)])],
+        [("C", lo[0], lo[0] + 96), ("C", lo[1], lo[1] + 96), ("EO", 0, 512)], [("P2", 256, 512)])
+    add([("s", 15.0 + vc(256), lambda q, T, r: [q.activation(T.OB[0:96, :], T.P2[0:96, 256:512], AF.Copy)]),
+         ("v", vc(256), lambda q, T, r: [q.tensor_copy(T.OB[0:96, :], T.P2[0:96, 256:512])])], [("P2", 256, 512)], [("OB", 0, 256)])
+    prs = []
+    for g_ in range(8):
+        prs.append((lambda T, g_=g_: T.yn[g_, :], lambda T, g_=g_: T.OB[0:64, 32 * g_:32 * g_ + 32]))
+        prs.append((lambda T, g_=g_: T.yl[g_, :], lambda T, g_=g_: T.OB[64:96, 32 * g_:32 * g_ + 32]))
+    dma(prs, [("OB", 0, 256)], [], 98304)
+    dma([(lambda T: T.NHF[:], lambda T: T.A[0:128:16, 0:W]), (lambda T: T.NLF[:], lambda T: T.A[1:128:16, 0:W])],
+        [("A", 0, W)], [("NHF", 0, 512), ("NLF", 0, 512)], 524288, early[2] + late[2] + late[1], q="s")
+    dma([(lambda T: T.BN[:], lambda T: T.B[0:128:16, 0:W])], [("B", 0, W)], [("BN", 0, 512)], 262144, bw)
+    for i in range(2):
+        cs = lambda nm: (nm, 256 * i, 256 * i + 256)
+        bk = ("P%d" % i, 256, 512)
+        pe([[(bk, IP, cs("NHF")), (bk, IP, cs("NLF"))]])
+        tt(cs("NS"), bk, cs("BN"), OP.max)
+        ts(cs("KD"), cs("NS"), 32767, None, OP.bitwise_and)
+        ts(cs("ZN"), cs("KD"), -128.0, None, OP.add)
+    dma([(lambda T: T.ys[:], lambda T: T.ZN[:])], [("ZN", 0, 512)], [], 262144)
+    return ops
+
+
+def isps(a):
+    return a[0][0] == "P" and a[0][1:].isdigit()
+
+
+def schedule(ops, par):
+    n = len(ops)
+    pred = [sorted(o["dep"]) for o in ops]
+    succ = [[] for _ in range(n)]
+    for o in ops:
+        o["lk"] = sorted(set((x[0], w, isps(x)) for x, w in [(x, 0) for x in o["rd"]] + [(x, 1) for x in o["wr"]] if isps(x) or x[0] in ("A", "B")))
+        for d in o["dep"]:
+            succ[d].append(o["n"])
+    pri = [0.0] * n
+    for o in reversed(ops):
+        i = o["n"]
+        pri[i] = min(a[1] for a in o["alts"]) + o["lat"] + HOP + max([pri[j] for j in succ[i]] + [0.0])
+    best = None
+    seed = par.get("seed", 0)
+    for _ in range(par["iters"]):
+        p = []
+        for i in range(n):
+            seed = (seed * 1103515245 + 12345) % 2147483648
+            p.append(pri[i] + ops[i]["pri"] + par["boost"][ops[i]["tag"]] + par.get("noise", 0.0) * seed / 2147483648.0)
+        fw = one_pass(ops, par, p, pred, succ, None)
+        span = max(x[3] for x in fw)
+        if best is None or span < best[0]:
+            best = (span, fw)
+        fixed, back = {}, [0.0] * n
+        for (i, a, s_, e_) in fw:
+            fixed[i] = a
+            back[i] = e_
+        for (i, a, s_, e_) in one_pass(ops, par, back, succ, pred, fixed):
+            pri[i] = e_
+    return best[1]
+
+
+def one_pass(ops, par, pri, pred, succ, fixed):
+    n = len(ops)
+    left = [len(p) for p in pred]
+    rdy = [0.0] * n
+    ready = [i for i in range(n) if not pred[i]]
+    free = {}
+    lock = {}
+    order = []
+    while ready:
+        cand = []
+        for i in ready:
+            best = None
+            o = ops[i]
+            for a in (o["alts"] if fixed is None else [fixed[i]]):
+                s = max(rdy[i], free.get(a[0], 0.0))
+                for nm, w, bank in o["lk"]:
+                    for (e, w2), end in lock.get(nm, {}).items():
+                        if end + HOP > s and ((bank and e != a[0]) or (not bank and (w or w2))):
+                            s = end + HOP
+                f = s + a[1] + (par["flexv"] * a[1] if a[0] == "v" else 0.0)
+                if best is None or f < best[0]:
+                    best = (f, s, a)
+            cand.append((best[1], i, best[2]))
+        s0, _, a0 = min(cand, key=lambda c: (c[0], -pri[c[1]]))
+        s, i, a = max([c for c in cand if c[0] <= s0 + par["delta"] and c[2][0] == a0[0]], key=lambda c: (pri[c[1]], -c[1]))
+        o = ops[i]
+        end = s + a[1] + o["lat"]
+        if a[0] != "n":
+            free[a[0]] = s + a[1]
+        for nm, w, bank in o["lk"]:
+            d = lock.setdefault(nm, {})
+            d[(a[0], w)] = max(d.get((a[0], w), 0.0), end)
+        order.append((i, a, s, end))
+        ready.remove(i)
+        for j in succ[i]:
+            rdy[j] = max(rdy[j], end + HOP)
+            left[j] -= 1
+            if left[j] == 0:
+                ready.append(j)
+    return order
+
+
+PLAN = []
+
+
+def rank_program(g, core, T, topo):
+    rank = T.rank_of(core)
+    if rank is None:
+        return
+    if not PLAN:
+        ops = build()
+        PLAN.append(ops)
+        PLAN.append(schedule(ops, PARAM))
+    ops, order = PLAN
+    nxt = T.cores[(rank + 1) % len(T.cores)]
+    rid, pid = topo.addr(nxt)[0:2]
+    mask = topo.mask(core, nxt)
+    nen = len(topo.engines(core, nxt))
+    queue = {"v": g.vector, "s": g.scalar, "t": g.tensor, "g": g, "y": g.sync}
+    count = {}
+    token = {}
+    waited = {}
+    hist = {}
+    place = {}
+    known = {}
+    nd = [0]
+
+    def r(a):
+        return T[a[0]][:, a[1]:a[2]:a[3]] if len(a) > 3 else T[a[0]][:, a[1]:a[2]]
+
+    def wait(e, sem, val):
+        if waited.get((e, sem), 0) < val:
+            queue[e].wait_ge(T.sem[sem], val)
+            waited[(e, sem)] = val
+
+    for (i, a, _, _) in order:
+        o = ops[i]
+        e = a[0]
+        place[i] = len(place)
+        accs = [(x, 0) for x in o["rd"]] + [(x, 1) for x in o["wr"]]
+        prev = set(o["dep"])
+        for x, w in accs:
+            bank = isps(x)
+            for (j, e2, x2, w2) in hist.get(x[0], ()):
+                if ((w or w2) and meet(x, x2)) or (bank and e2 != e):
+                    prev.add(j)
+        for x, w in accs:
+            hist.setdefault(x[0], []).append((i, e, x, w))
+        if o["kind"] == "r":
+            token[i] = ("a%d" % a[2], nen)
+            count[token[i][0]] = nen
+            continue
+        for j in sorted(prev, key=lambda j: -place[j]):
+            if token[j] is not None and waited.get((e, token[j][0]), 0) < token[j][1]:
+                wait(e, token[j][0], token[j][1])
+                for sem, val in known.get(j, ()):
+                    waited[(e, sem)] = max(waited.get((e, sem), 0), val)
+        known[i] = [(k[1], v) for k, v in waited.items() if k[0] == e]
+        if o["kind"] == "s":
+            src, dst, k = a[2]
+            g.remote_dma(r(dst), r(src), T.sem["a%d" % k], T.sem.sent, pid, rid, mask)
+            count["sent"] = count.get("sent", 0) + nen
+            token[i] = None
+            continue
+        ins = a[2](queue[e], T, r)
+        if o["kind"] == "d":
+            sem, inc = "d%d" % nd[0], 16
+            nd[0] += 1
+        else:
+            sem, inc = "e" + e, 1
+        for x in ins:
+            x.then_inc(T.sem[sem], inc)
+            count[sem] = count.get(sem, 0) + inc
+        token[i] = (sem, count[sem])
+    for sem in sorted(count):
+        g.wait_ge(T.sem[sem], count[sem])

@@ -4,30 +4,36 @@ W = 8192
 WD = W + 512
 BF, F32, I32, U16 = "bfloat16", "float32", "int32", "uint16"
 SB = {
-    "X": (W, BF), "A0": (W, BF), "KW": (W, BF), "A": (WD, F32), "B": (WD, F32),
-    "D0": (1024, BF), "ZW1": (3072, BF), "ZW2": (3072, BF), "Z1": (1024, BF), "Z2": (1024, BF),
-    "NS": (512, I32), "NH": (512, BF), "NL": (512, BF), "NHF": (512, F32), "NLF": (512, F32),
-    "KD": (512, I32), "ZN": (512, F32), "BN": (512, F32),
-    "RN": (192, I32), "RNF": (192, F32), "PM": (512, F32), "EO": (512, F32), "I32P": (128, F32), "I32N": (128, F32),
-    "IB": (128 * 10, BF), "ZS": (16 * 144, BF), "ZP": (5 * 144, BF), "ONE": (48, BF),
-    "PI": (2, I32), "PF": (4, F32), "ST": (32 * 10, F32),
-    "C": (6 * 384 + 256, F32), "U": (6 * 384 + 256, U16), "R": (64, F32), "RU": (64, U16), "RH": (128, BF),
-    "GS": (4096, BF), "CM": (4096, BF), "SG": (256, BF), "OV": (192, BF), "DD": (64 * 4, BF),
-    "M": (256, F32), "MN": (256, I32), "WN": (256, I32), "M2": (384, I32), "M3": (384, I32),
-    "E": (192, F32), "NE": (64, BF), "FS": (128, U16), "FO": (128, U16),
-    "VC": (64, F32), "VH": (64, BF), "VL": (64, BF), "WS": (2048, F32), "WE": (1024, F32),
-    "UB": (96, U16), "GK": (1024, BF), "PT": (32 * 6, F32), "LH": (128, BF), "LT": (1024, BF),
-    "LL": (128, BF), "LO": (32, U16), "LS": (512, BF), "LW": (1536, BF), "LI": (128, F32),
-    "Q": (32 * 20, F32), "QO": (64, U16), "GX": (512, BF), "CK": (512, BF), "V4": (128, F32), "H4": (128, BF),
-    "L4": (128, BF), "RV": (64, F32), "RVH": (64, BF), "RVL": (64, BF), "OB": (256, F32),
+    "X": (W, BF), "A0": (W, BF), "KW": (W, BF), "A": (WD, F32), "D1": (WD, F32),
+    "D0": (2048, BF), "ZW1": (3072, BF), "ZW2": (3072, BF), "Z1": (1024, BF), "Z2": (1024, BF),
+    "NS": (512, I32), "KD": (512, I32), "NH": (512, BF), "NM": (512, BF),
+    "NHF": (512, F32), "NLF": (512, F32), "DN1": (512, F32), "DN2": (512, F32),
+    "RN": (192, I32), "EO": (512, F32), "IF": (512, F32), "ZN": (256, F32),
+    "IB": (128 * 6, BF), "ZS": (16 * 144, BF), "ZP": (7 * 144, BF), "ONE": (256, BF), "CR": (64 * 8 + 352 + 160 + 256, BF),
+    "PI": (2, I32), "PF": (12, F32), "ST": (32 * 8, F32),
+    "K0": (386, F32), "K1": (386, F32), "K2": (450, F32), "K3": (450, F32), "SC0": (1120, F32), "SC1": (896, F32),
+    "U": (8 * 384, U16), "R": (64, F32), "RU": (64, U16), "NI": (128, F32),
+    "GS": (4096, BF), "CM": (4096, BF), "OV": (192, BF), "SP": (96, BF),
+    "MN": (320, I32), "WN": (320, I32), "E": (128, F32), "EM": (64, BF), "TM": (256, F32), "NE": (384, F32),
+    "FS": (128, U16), "FO": (128, U16), "UB": (320, U16), "G1": (512, BF), "G2": (512, BF), "GR": (512, BF),
+    "PT": (128, F32), "LO": (96, U16), "LW": (1536, BF), "LI": (128, F32),
+    "RW": (1536, F32), "WS": (2048, F32),
+    "Q": (32 * 10, F32), "QO": (64, U16), "GX": (512, BF), "CK": (512, BF), "H5": (160, BF), "L5": (160, BF),
+    "HP": (128, BF), "LP": (128, BF), "LV": (64, F32),
 }
 SCRATCH = {k: ("sbuf", [128, v[0]], v[1]) for k, v in SB.items()}
 for _i in range(8):
     SCRATCH["P%d" % _i] = ("psum", [128, 512], "float32")
 SEMAPHORES = ["ev", "es", "et", "eg", "sent"] + ["d%d" % i for i in range(40)] + ["a%d" % i for i in range(6)]
 
-CY, PCY, GA, SC, HOP = 1.04, 0.52, 1.56, 3.8, 70.0
-PARAM = {'delta': 30, 'flexv': 1, 'iters': 4, 'split': 0, 'roots': 'sv', 'boost': [700.0, 39600.0, -1300.0, 0.0, -3300.0, 1600.0, 4000.0, -200.0, 6700.0, 1100.0, 7100.0, 0.0, 0.0, 0.0, 100.0, 4700.0, 400.0, 2700.0, 1800.0, -2500.0, 10500.0, 12300.0, 18500.0], 'noise': 0, 'seed': 11}
+COST = {"cy": 0.85, "pe": 0.43, "ga": 1.4, "sc": 3.3, "hop": 80.0, "dma": 2000.0, "bw": 200.0, "mm": 0.0}
+PARAM = {"flexv": 2.0, "flex0": 0.0, "xl": 13000.0, "iters": 10, "moves": 12000, "noise": 300.0, "seed": 5, "split": 0, "last": "ssss",
+         "fill": 10, "kwv": 3, "kwd": 1, "pair": 1, "roots": 1,
+         "boost": [5e5] + [0.0] * 21 + [1e5, 0.0, 0.0, 0.0]}
+KEY = 2.0 ** -20
+WT = [(5 - k) * 65536.0 for k in range(7)]
+MAGIC = 1.5 * 2 ** 23
+BIG = 16384.0
 
 
 def meet(a, b):
@@ -36,22 +42,24 @@ def meet(a, b):
     return a[1] < b[2] and b[1] < a[2]
 
 
-def build():
+def isps(a):
+    return a[0][0] == "P" and a[0][1:].isdigit()
+
+
+def build(par, c):
     ops = []
     acc = {}
     tag = [0]
+    CY, PCY, GA, SC = c["cy"], c["pe"], c["ga"], c["sc"]
 
     def sz(a):
         return (a[2] - a[1] + (a[3] if len(a) > 3 else 1) - 1) // (a[3] if len(a) > 3 else 1)
-
-    def ps(a):
-        return a[0][0] == "P" and a[0][1:].isdigit()
 
     def add(alts, rd, wr, after=(), lat=0.0, kind="c", pri=0.0):
         o = {"n": len(ops), "alts": alts, "rd": rd, "wr": wr, "lat": lat, "kind": kind, "pri": pri, "tag": tag[0]}
         dep = set(x["n"] for x in after)
         for a, w in [(a, 0) for a in rd] + [(a, 1) for a in wr]:
-            if a[0] in ("A", "B"):
+            if a[0] in ("A", "D1"):
                 continue
             for (n, a2, w2) in acc.get(a[0], ()):
                 if (w or w2) and meet(a, a2):
@@ -63,70 +71,80 @@ def build():
         return o
 
     def two(*aps):
-        return all((not ps(a)) and SB[a[0]][1] in (BF, U16) for a in aps)
+        return all((not isps(a)) and SB[a[0]][1] in (BF, U16) for a in aps)
 
     def vc(n):
         return 50.0 + max(64, n) * CY
 
+    def val(r, x):
+        return r(x) if isinstance(x, tuple) else x
+
+    def cols(*xs):
+        return [x for x in xs if isinstance(x, tuple)]
+
     def tt(out, a, b, op):
-        n = sz(out) * (1 if ps(a) or ps(b) else 2)
+        n = sz(out) * (1 if isps(a) or isps(b) else 2)
         return add([("v", vc(n), lambda q, T, r: [q.tensor_tensor(r(out), r(a), r(b), op)])], [a, b], [out])
 
     def ts(out, a, s1, s2, op0, op1=None):
         n = sz(out) * (0.5 if two(out, a) else 1)
-        rd = [a] + [s for s in (s1, s2) if isinstance(s, tuple)]
 
         def em(q, T, r):
-            x1 = r(s1) if isinstance(s1, tuple) else s1
             if op1 is None:
-                return [q.tensor_scalar(r(out), r(a), x1, None, op0)]
-            return [q.tensor_scalar(r(out), r(a), x1, r(s2) if isinstance(s2, tuple) else s2, op0, op1)]
-        return add([("v", vc(n), em)], rd, [out])
+                return [q.tensor_scalar(r(out), r(a), val(r, s1), None, op0)]
+            return [q.tensor_scalar(r(out), r(a), val(r, s1), val(r, s2), op0, op1)]
+        return add([("v", vc(n), em)], [a] + cols(s1, s2), [out])
 
     def cp(out, a):
         n = sz(out) * (0.5 if two(out, a) else 1)
         return add([("v", vc(n), lambda q, T, r: [q.tensor_copy(r(out), r(a))])], [a], [out])
 
-    def ms(out, val, pri=0.0):
+    def ms(out, v, pri=0.0):
         n = sz(out) * (0.5 if two(out) else 1)
-        return add([("v", vc(n), lambda q, T, r: [q.memset(r(out), val)])], [], [out], pri=pri)
+        return add([("v", vc(n), lambda q, T, r: [q.memset(r(out), v)])], [], [out], pri=pri)
+
+    def scan(out, p, k):
+        return add([("v", vc(sz(out)), lambda q, T, r: [q.tensor_tensor_scan(r(out), r(p), r(k), 0.0, OP.max, OP.min)])], [p, k], [out])
 
     def flex(out, a, bias=0.0, engs="sv", scale=1.0):
         n = sz(out)
-        col = isinstance(bias, tuple)
         alts = []
         if "s" in engs:
-            alts.append(("s", 15.0 + vc(n), lambda q, T, r: [q.activation(r(out), r(a), AF.Identity, bias=r(bias) if col else bias, scale=scale)]))
+            alts.append(("s", 15.0 + vc(n), lambda q, T, r: [q.activation(r(out), r(a), AF.Identity, bias=val(r, bias), scale=val(r, scale))]))
         if "v" in engs:
-            alts.append(("v", vc(n), lambda q, T, r: [q.tensor_scalar(r(out), r(a), r(bias) if col else bias, None, OP.add)]))
-        return add(alts, [a] + ([bias] if col else []), [out])
+            alts.append(("v", vc(n), lambda q, T, r: [q.tensor_scalar(r(out), r(a), val(r, scale), val(r, bias), OP.mult, OP.add)]))
+        return add(alts, [a] + cols(bias, scale), [out])
 
-    def gat(out, win, off, engs="s", after=()):
+    def gat(out, win, off, engs="sv", after=(), scale=None, bias=0.0):
         n = sz(out)
-        alts = []
-        if "s" in engs:
-            alts.append(("s", 65.0 + n * GA * CY, lambda q, T, r: [q.activation(r(out), r(win).indirect(r(off)), AF.Copy)]))
-        if "v" in engs:
-            alts.append(("v", 50.0 + n * GA * CY, lambda q, T, r: [q.tensor_copy(r(out), r(win).indirect(r(off)))]))
-        return add(alts, [win, off], [out], after)
+        if scale is None:
+            es = lambda q, T, r: [q.activation(r(out), r(win).indirect(r(off)), AF.Copy)]
+            ev = lambda q, T, r: [q.tensor_copy(r(out), r(win).indirect(r(off)))]
+        else:
+            es = lambda q, T, r: [q.activation(r(out), r(win).indirect(r(off)), AF.Identity, bias=val(r, bias), scale=r(scale))]
+            ev = lambda q, T, r: [q.tensor_scalar(r(out), r(win).indirect(r(off)), r(scale), val(r, bias), OP.mult, OP.add)]
+        alts = [x for x in (("s", 65.0 + n * GA * CY, es), ("v", 50.0 + n * GA * CY, ev)) if x[0] in engs]
+        return add(alts, [win, off] + cols(scale, bias), [out], after)
 
     def cmpg(out, off, z):
         return add([("v", 50.0 + sz(out) * GA * CY, lambda q, T, r: [q.tensor_tensor(r(out), r(("X", 0, W)).indirect(r(off)), r(z), OP.is_ge)])],
                    [("X", 0, W), off, z], [out])
 
-    def scat(win, off, src, eng, after=()):
-        if eng == "s":
+    def scat(win, off, src, eng, after=(), src2=None):
+        if src2 is not None:
+            em = lambda q, T, r: [q.tensor_tensor(r(win).indirect(r(off)), r(src), r(src2), OP.add)]
+        elif eng == "s":
             em = lambda q, T, r: [q.activation(r(win).indirect(r(off)), r(src), AF.Silu)]
         else:
             em = lambda q, T, r: [q.tensor_copy(r(win).indirect(r(off)), r(src))]
-        return add([(eng, 60.0 + sz(src) * SC * CY, em)], [off, src], [win], after)
+        return add([(eng, 60.0 + sz(src) * SC * CY, em)], [off, src] + cols(src2), [win], after)
 
-    def pe(groups, first=True, last=True):
-        cost, rd, wr = 60.0, [], []
+    def pe(groups, first=True, last=True, hold=None):
+        cost, rd, wr = 60.0, [], [(hold, 0, 512)] if hold else []
         for grp in groups:
             for (o, l, x) in grp:
-                cost += max(64, sz(x)) * PCY * (4 if SB[x[0]][1] == F32 else 1)
-                for lst, a in ((rd, l), (rd, x[:3]), (wr, o)):
+                cost += max(64, sz(x)) * PCY * (4 if SB[x[0]][1] == F32 else 1) + c["mm"]
+                for lst, a in ((rd, l), (rd, x if x[0][0] == "K" else x[:3]), (wr, o)):
                     if a not in lst:
                         lst.append(a)
 
@@ -138,23 +156,22 @@ def build():
             return res
         return add([("t", cost, em)], rd, wr)
 
-    def pew(groups, per):
-        for i in range(0, len(groups), per):
-            pe(groups[i:i + per])
+    def gp(n, em, rd, wr, pri=0.0, after=()):
+        return add([("g", 170.0 + 2 * n * CY, em)], rd, wr, after, pri=pri)
 
-    def zero(a):
-        return add([("g", 130.0 + 2 * sz(a) * CY, lambda q, T, r: [q.iota(r(a), [[0, sz(a)]], 0, 0, allow_small_or_imprecise_dtypes=True)])], [], [a])
+    def iota(a, pat, base, cm, pri=0.0):
+        return gp(sz(a), lambda q, T, r: [q.iota(r(a), pat, base, cm, allow_small_or_imprecise_dtypes=True)], [], [a], pri)
 
-    def gp(n, em, rd, wr, pri=0.0):
-        return add([("g", 170.0 + 2 * n * CY, em)], rd, wr, pri=pri)
+    def zero(a, v=0):
+        return iota(a, [[0, sz(a)]], v, 0)
 
     def dma(pairs, rd, wr, nbytes, after=(), q="y", pri=0.0):
         return add([(q, 100.0 * len(pairs), lambda e, T, r: [e.dma_start(a(T), b(T)) for a, b in pairs])], rd, wr, after,
-                   lat=2000.0 + nbytes / 200.0, kind="d", pri=pri)
+                   lat=c["dma"] + nbytes / c["bw"], kind="d", pri=pri)
 
     def send(src, dst, k):
         s = add([("g", 300.0, (src, dst, k))], [src], [], kind="s")
-        return add([("n", 0.0, k)], [], [dst], [s], lat=2200.0 + sz(src) * 256 / 150.0, kind="r")
+        return add([("n", 0.0, k)], [], [dst], [s], lat=200.0 + c["dma"] + sz(src) * 256 / c["bw"], kind="r")
 
     def sel(buf, base, r):
         return (buf, base + 15 - r, base + 143 - r)
@@ -162,44 +179,58 @@ def build():
     def to_list(out, wide, zset):
         return [(out, sel("ZP", 144 * zset, r), (wide[0], wide[1] + r, wide[2], 16)) for r in range(16)]
 
-    def to_wide(bank, lists):
-        return [[((bank, r, 512, 16), sel("ZS", 144 * r, row), a) for a, row in lists] for r in range(16)]
-
     def b32(name, i, n=1):
         return (name, 32 * i, 32 * (i + n))
 
-    ALL = 4
+    def sub(a, i, n=1):
+        s = a[3] if len(a) > 3 else 1
+        return (a[0], a[1] + 32 * i * s, a[1] + 32 * (i + n) * s) + a[3:]
+
+    def const(out, i):
+        a = i if isinstance(i, tuple) else ("CR", 64 * i, 64 * i + sz(out))
+        o = 0 if i in (4, 5, 6) else 128
+        return (out, ("ONE", o, o + 128, 1, 1), a + (1, 1))
+
+    ALL = 6
     IBM = lambda i: ("IB", 128 * i, 128 * i + 128)
-    IP, IN = ("I32P", 0, 128), ("I32N", 0, 128)
-    UF, DUM, LDUM = b32("ST", 0), b32("ST", 1), b32("ST", 3)
+    IP, IN, KP, KN = [("IF", 128 * i, 128 * i + 128) for i in range(4)]
+    DUM, LDUM, UF = b32("ST", 0, 2), b32("ST", 2), b32("ST", 3)
     LN = [b32("ST", 4), b32("ST", 5)]
-    BA = ("PF", 1, 2)
+    PC = lambda i: ("PF", i, i + 1)
+    BA, M1, M2, B2 = PC(1), PC(2), PC(3), PC(4)
+    CE, CV, CG = ("CR", 512, 864), ("CR", 864, 1024), ("CR", 1024, 1280)
+    NE = lambda h, i, n=1: b32("NE", 6 * h + i, n)
+    R = lambda h: b32("R", h)
+    EM = lambda h: b32("EM", h)
+    UW = lambda h, i, n=1: b32("UB", 5 * h + i, n)
 
-    def slot(t, h):
-        return (t * 2 + h) * 384 if t < 3 else 6 * 384 + 128 * h
+    def blk(t):
+        return 7 if t == 2 else 6
 
-    def Cc(t, h, k, s=None):
-        o = slot(t, h) + (k - 1) * 64
-        return ("C", o, o + 64) if s is None else ("C", o + 32 * s, o + 32 * s + 32)
+    def Kk(t, h, k):
+        o = 7 - k
+        return ("K%d" % (h + (2 if t == 2 else 0)), o, o + 64 * blk(t) - blk(t) + 1, blk(t))
 
-    def Uu(t, h, k, s=None):
-        o = slot(t, h) + (0 if k == 1 else 64 if k == 0 else k * 64)
-        return ("U", o, o + 64) if s is None else ("U", o + 32 * s, o + 32 * s + 32)
+    def Uu(t, h, k):
+        o = (2 * t + h) * 384 + 64 * (2 if k == 0 else k - 1 if k < 3 else k)
+        return ("U", o, o + 64)
 
-    dma([(lambda T: T.RN[:, 0:64], lambda T: T.rho[:]), (lambda T: T.RN[:, 64:192], lambda T: T.nei[:])], [], [("RN", 0, 192)], 98304, pri=9e5)
-    dma([(lambda T: T.NS[:], lambda T: T.nsum[:])], [], [("NS", 0, 512)], 262144, q="s", pri=9e5)
-    dma([(lambda T: T.KD[:], lambda T: T.kid[:])], [], [("KD", 0, 512)], 524288, q="s", pri=8.5e5)
+    def key(t, h, k, src, out=None):
+        return flex(out or Kk(t, h, k), src, WT[k] * KEY, "sv", KEY)
+
+    dma([(lambda T: T.NS[:], lambda T: T.nsum[:])], [], [("NS", 0, 512)], 262144, pri=9.5e5)
+    dma([(lambda T: T.RN[:, 0:64], lambda T: T.rho[:]), (lambda T: T.RN[:, 64:192], lambda T: T.nei[:])], [], [("RN", 0, 192)], 98304, q="s", pri=9e5)
     lx = dma([(lambda T: T.X[:], lambda T: T.x[:])], [], [("X", 0, W)], 2400000, pri=8e5)
-    ld = dma([(lambda T: T.D0[:], lambda T: T.dem[:, 0:1024])], [], [("D0", 0, 1024)], 600000, q="s", pri=8e5)
-    ms(("ZN", 0, 512), 0.0, 9e5)
-    for i in range(2):
-        zero(("ZS", 1152 * i, 1152 * i + 1152))
-    ms(("ZP", 0, 720), 0.0)
-    ms(("ONE", 0, 48), 1.0)
-    for i in range(5):
-        ms(("A0", 1024 * i, 1024 * i + 1024), 0.0)
-    for i in range(10, 16):
-        flex(("A0", 512 * i, 512 * i + 512), ("ZN", 0, 512), 0.0, "s")
+    ld = dma([(lambda T, i=i: T.D0[:, 1024 * i:1024 * i + 1024], lambda T: T.dem[:, 0:1024]) for i in range(2)], [], [("D0", 0, 2048)], 600000, q="s", pri=8e5)
+    dma([(lambda T: T.KD[:], lambda T: T.kid[:])], [], [("KD", 0, 512)], 800000, q="s", pri=7e5)
+    ms(("ZN", 0, 256), 0.0, 9e5)
+    ms(("ONE", 0, 128), 1.0, 9e5)
+    ms(("ZP", 0, 1008), 0.0, 9e5)
+    nv = par["fill"]
+    for i in range(0, nv, 2):
+        ms(("A0", 512 * i, 512 * i + 1024), 32768.0, 5e5)
+    for i in range(2 * nv, 32):
+        flex(("A0", 256 * i, 256 * i + 256), ("ZN", 0, 256), 32768.0, "s")["pri"] = 5e5
 
     def diag(out, src, pat, fill, base, cm=1):
         return gp(sz(out), lambda q, T, r: [q.affine_select(r(out), r(src), pat, OP.not_equal, fill, base, cm)], [src], [out])
@@ -207,277 +238,329 @@ def build():
     def band(out, src, pat, base, cm):
         return gp(sz(out), lambda q, T, r: [q.affine_select(r(out), r(src), pat, OP.is_ge, 0.0, base, cm)], [src], [out])
 
+    ts(("NH", 0, 512), ("NS", 0, 512), 64.0, None, OP.add)["pri"] = 6e5
+    tt(("CK", 0, 512), ("NS", 0, 512), ("NH", 0, 512), OP.subtract)["pri"] = 6e5
+    flex(("NM", 0, 512), ("CK", 0, 512), 128.0)["pri"] = 6e5
+    wa = dma([(lambda T: T.A0[0:128:16, :], lambda T: T.NH[:]), (lambda T: T.A0[1:128:16, :], lambda T: T.NM[:])],
+             [("NH", 0, 512), ("NM", 0, 512)], [("A0", 0, W)], 262144, pri=6e5)
+    late_loads = [lx, ld, wa]
+
     z128 = ("ZN", 0, 128)
     for h in range(2):
         for b in range(2):
-            diag(("PM", 128 * (2 * h + b), 128 * (2 * h + b + 1)), z128, [[-16, 8], [1024, 2], [-2, 8]], 1.0, -h - 1024 * b)
-    diag(IN, z128, [[-1, 128]], -1.0, 0)
+            diag(("DN2", 128 * (2 * h + b), 128 * (2 * h + b + 1)), z128, [[-16, 8], [1024, 2], [-2, 8]], 1.0, -h - 1024 * b)
     diag(IP, z128, [[-1, 128]], 1.0, 0)
-    zp4, zpa = ("ZP", 15, 576, 16), ("ZP", 591, 720, 16)
-    band(zp4, ("ONE", 0, 36), [[-2, 4], [-16, 9]], 0, 1)
-    band(zp4, zp4, [[2, 4], [16, 9]], 1, -1)
-    band(zpa, ("ONE", 0, 9), [[-16, 9]], 0, 1)
+    zp6, zp0, zpa = ("ZP", 15, 864, 16), ("ZP", 15, 144, 16), ("ZP", 879, 1008, 16)
+    band(zp6, ("ONE", 0, 54), [[-2, 6], [-16, 9]], 0, 1)
+    band(zp6, zp6, [[2, 6], [16, 9]], 1, -1)
+    diag(zp0, zp0, [[-16, 9]], -2.0 ** -8, -2)
+    ms(("EM", 0, 9), 2.0)
+    band(zpa, ("EM", 0, 9), [[-16, 9]], 0, 1)
     band(zpa, zpa, [[16, 9]], 15, -1)
-    zs = ("ZS", 15, 2304, 16)
-    diag(zs, zs, [[-1, 16], [-16, 9]], 1.0, 0)
-    for k in range(5):
-        flex(IBM(k), IP, 0.0, "s", float(2 ** 18 * (5 - k)))
-    flex(IBM(5), IP, 0.0, "s", -64.0)
-    flex(IBM(6), IP, 0.0, "s", float(2 ** 21))
-    flex(("IB", 896 + 16, 1024), ("I32P", 0, 112), 0.0, "s", 2048.0)
-    flex(("IB", 896, 896 + 16), ("I32P", 112, 128), 0.0, "s", 2048.0)
-    flex(IBM(8), IP, 0.0, "s", 1024.0)
-    flex(("IB", 1152, 1154), ("ZN", 0, 2), 0.0, "s")
-    flex(("IB", 1154, 1280), ("I32P", 0, 126), 0.0, "s")
+    for i, s in ((1, -1.0), (2, 1 / KEY), (3, -1 / KEY)):
+        flex(("IF", 128 * i, 128 * i + 128), IP, 0.0, "s", s)
+    for i, s in enumerate((-64.0, -BIG, BIG, -4096.0, -1024.0)):
+        flex(IBM(i), IP, 0.0, "s", s)
+    flex(("IB", 640 + 16, 768), ("IF", 0, 112), 0.0, "s", -2048.0)
+    flex(("IB", 640, 640 + 16), ("IF", 112, 128), 0.0, "s", -2048.0)
+    ms(("ONE", 128, 256), 65536.0)
+    iota(("CR", 0, 256), [[-1, 4], [0, 64]], 4, 0)
+    iota(("CR", 256, 448), [[16, 3], [0, 64]], -17, 0)
+    iota(("CR", 512, 768), [[0, 2], [1, 2], [0, 64]], -4, 0)
+    ms(("CR", 768, 992), 0.0)
+    ms(("CR", 992, 1024), -128.0 / 65536.0)
+    iota(CG, [[0, 256]], int(MAGIC) // 65536, 0)
     for h in range(2):
-        diag(("EO", 256 * h, 256 * h + 256), ("ZN", 0, 256), [[-16, 8], [-1, 16], [1024, 2]], 1.0, -1024 * h)
+        ms(("K%d" % h, 0, 386, 385), 0.0)
+        ms(("K%d" % (2 + h), 0, 450, 7), 0.0)
+        ms(("K%d" % (2 + h), 1, 450, 7), WT[6] * KEY)
     gp(1, lambda q, T, r: [q.iota(r(("PI", 0, 1)), [[0, 1]], 0, 1)], [], [("PI", 0, 1)])
-    gp(32, lambda q, T, r: [q.iota(r(b32("ST", 8)), [[16, 32]], 0, 0, allow_small_or_imprecise_dtypes=True)], [], [b32("ST", 8)])
+    iota(b32("ST", 6), [[16, 32]], 0, 0)
     ts(("PI", 1, 2), ("PI", 0, 1), 15, None, OP.bitwise_and)
-    cp(("PF", 0, 1), ("PI", 1, 2))
-    ts(BA, ("PF", 0, 1), 1.0, 128.0, OP.is_equal, OP.mult)
-    ts(UF, b32("ST", 8), ("PF", 0, 1), None, OP.add)
-    ts(DUM, UF, float(W), None, OP.add)
-    ts(b32("ST", 2), UF, float(W), None, OP.add)
-    ts(LDUM, UF, 1024.0, None, OP.add)
+    cp(PC(0), ("PI", 1, 2))
+    ts(PC(5), PC(0), 1.0, 128.0, OP.is_equal, OP.mult)
+    ts(PC(6), PC(0), 2.0, 32768.0, OP.is_ge, OP.mult)
+    ts(PC(7), PC(0), 4.0, -32768.0, OP.is_ge, OP.mult)
+    ts(BA, PC(5), PC(6), PC(7), OP.add, OP.add)
+    ts(M1, PC(0), 6.0, None, OP.is_lt)
+    ts(PC(9), PC(0), 6.0, None, OP.is_ge)
+    ts(M2, PC(0), 10.0, PC(9), OP.is_lt, OP.mult)
+    ts(B2, PC(0), 10.0, -1.0, OP.is_equal, OP.mult)
+    ts(PC(8), ("PI", 0, 1), PC(0), -512.0, OP.subtract, OP.mult)
+    ts(UF, b32("ST", 6), PC(0), None, OP.add)
+    for s in range(2):
+        ts(sub(DUM, s), UF, float(W), None, OP.add)
+    ts(LDUM, UF, 1024.0 - 4096.0, None, OP.add)
     for h in range(2):
-        ts(LN[h], UF, 2.0, float(h), OP.mult, OP.add)
+        ts(LN[h], UF, 2.0, float(h + 1024 * (h + 1)), OP.mult, OP.add)
 
-    ts(("NH", 0, 512), ("NS", 0, 512), 64.0, None, OP.add)
-    tt(("NL", 0, 512), ("NS", 0, 512), ("NH", 0, 512), OP.subtract)
-    wa = dma([(lambda T: T.A0[0:128:16, :], lambda T: T.NH[:]), (lambda T: T.A0[1:128:16, :], lambda T: T.NL[:])],
-             [("NH", 0, 512), ("NL", 0, 512)], [("A0", 0, W)], 262144)
-    flex(("NHF", 0, 512), ("NH", 0, 512), 0.0, "s")
-    flex(("NLF", 0, 512), ("NL", 0, 512), 128.0, "s")
-    za = []
-    for i in range(8):
-        a = ("A", 1024 * i, 1024 * i + 1024)
-        za.append(zero(a))
-    ia = dma([(lambda T: T.A[0:128:16, 0:W], lambda T: T.NHF[:]), (lambda T: T.A[1:128:16, 0:W], lambda T: T.NLF[:])],
-             [("NHF", 0, 512), ("NLF", 0, 512)], [("A", 0, W)], 524288, za)
-    late_loads = [lx, ld, wa]
-    dma([(lambda T: T.KW[:], lambda T: T.x[:])], [], [("KW", 0, W)], 2600000, late_loads)
-    dma([(lambda T: T.ZW1[:, 0:1024], lambda T: T.dem[:, 1024:2048]), (lambda T: T.ZW2[:, 0:1024], lambda T: T.dem[:, 2048:3072])],
-        [], [("ZW1", 0, 1024), ("ZW2", 0, 1024)], 3000000, late_loads)
-    ib = dma([(lambda T: T.B[0:128:16, 0:W], lambda T: T.ZN[:])], [("ZN", 0, 512)], [("B", 0, W)], 3200000, late_loads)
-    ts(("KD", 0, 512), ("KD", 0, 512), 2047, None, OP.bitwise_and)
-    cp(("CK", 0, 512), ("KD", 0, 512))
-    tt(("GX", 0, 512), ("KD", 0, 512), ("CK", 0, 512), OP.subtract)
-    dma([(lambda T: T.KW[0:128:16, :], lambda T: T.CK[:]), (lambda T: T.KW[1:128:16, :], lambda T: T.GX[:])],
-        [("CK", 0, 512), ("GX", 0, 512)], [("KW", 0, W)], 262144)
-
-    cp(("RNF", 0, 192), ("RN", 0, 192))
+    cp(("TM", 0, 192), ("RN", 0, 192))
     for h in range(2):
         bk = "P%d" % (4 + h)
-        pe([[((bk, 0, 96), ("PM", 128 * (2 * h + b), 128 * (2 * h + b + 1)), ("RNF", b, 192, 2)) for b in range(2)]])
+        pe([[((bk, 0, 96), ("DN2", 128 * (2 * h + b), 128 * (2 * h + b + 1)), ("TM", b, 192, 2)) for b in range(2)]])
         cp(Uu(0, h, 1), (bk, 32, 96))
-        flex(Cc(0, h, 1), (bk, 32, 96))
-        flex(b32("R", h), (bk, 0, 32))
+        key(0, h, 1, (bk, 32, 96))
+        flex(R(h), (bk, 0, 32))
+        flex(b32("NI", 2 * h, 2), (bk, 32, 96))
     cp(("RU", 0, 64), ("R", 0, 64))
-    flex(("RH", 0, 64), ("RNF", 0, 64))
-    tt(("RH", 64, 128), ("RNF", 0, 64), ("RH", 0, 64), OP.subtract)
-    for i in range(2):
-        bk = "P%d" % (6 + i)
-        pew(to_wide(bk, [(b32("RH", i), 0), (b32("RH", 2 + i), 1), (b32("RH", i), 6), (b32("RH", 2 + i), 7)]), 4)
-        flex(("LT", 512 * i, 512 * i + 512), (bk, 0, 512))
-
+    for h in range(2):
+        for s in range(2):
+            key(2, h, 0, R(h), sub(Kk(2, h, 0), s))
     send(("D0", 0, 1024), ("ZW1", 1024, 2048), 0)
-    dma([(lambda T: T.ZW1[16:128, 2048:3072], lambda T: T.ZW1[0:112, 1024:2048]), (lambda T: T.ZW1[0:16, 2048:3072], lambda T: T.ZW1[112:128, 1024:2048])],
-        [("ZW1", 1024, 2048)], [("ZW1", 2048, 3072)], 262144)
 
-    wbank = [0]
+    def rotate(z):
+        dma([(lambda T: T[z][16:128, 2048:3072], lambda T: T[z][0:112, 1024:2048]), (lambda T: T[z][0:16, 2048:3072], lambda T: T[z][112:128, 1024:2048])],
+            [(z, 1024, 2048)], [(z, 2048, 3072)], 262144)
+    rotate("ZW1")
 
-    def nb_():
-        wbank[0] ^= 1
-        return "P%d" % (6 + wbank[0])
+    tag[0] = 22
+    if par["kwd"]:
+        dma([(lambda T, i=i: T.KW[i:128:16, :], lambda T, i=i: T.A0[i:128:16, :]) for i in (0, 1, 10, 11, 12, 13, 14, 15)],
+            [("A0", 0, W)], [("KW", 0, 1)], 1048576, late_loads)
+    for i in range(0 if par["kwd"] else par["kwv"]):
+        ms(("KW", 1024 * i, 1024 * i + 1024), 0.0)
+    for i in range(16 if par["kwd"] else 2 * par["kwv"], 16):
+        flex(("KW", 512 * i, 512 * i + 512), ("ZP", 0, 512), 0.0, "s", 0.0)
+    ts(("KD", 0, 512), ("KD", 0, 512), 2047, None, OP.bitwise_and)
+    cp(("G1", 0, 512), ("KD", 0, 512))
+    tt(("G2", 0, 512), ("KD", 0, 512), ("G1", 0, 512), OP.subtract)
+    iota(("NHF", 0, 512), [[32, 16], [0, 32]], 0, 512)
+    flex(("GR", 0, 512), ("NHF", 0, 512), PC(8))
+    iota(("GX", 0, 512), [[0, 16], [1, 32]], 0, 0)
+    rows = [(2, "G1"), (3, "G2"), (4, "GR"), (5, "GX"), (8, "GR"), (9, "GX"), (6, "NH"), (7, "NM")]
+    dma([(lambda T, i=i: T.KW[i:128:16, :], lambda T, n=n: T[n][:]) for i, n in rows], [(n, 0, 512) for _, n in rows],
+        [("KW", par["kwd"], W)], 1048576 * (1 + par["kwd"]), late_loads)
+    dma([(lambda T: T.ZW1[:, 0:1024], lambda T: T.dem[:, 1024:2048]), (lambda T: T.ZW2[:, 0:1024], lambda T: T.dem[:, 2048:3072])],
+        [], [("ZW1", 0, 1024), ("ZW2", 0, 1024)], 1500000, late_loads)
+    for i in range(2):
+        ms(("ZS", 1152 * i, 1152 * i + 1152), 0.0)
+    zs = ("ZS", 15, 2304, 16)
+    diag(zs, zs, [[-1, 16], [-16, 9]], 1.0, 0)
+    zero(("LW", 0, 1024))
+    tag[0] = 24
+    ia = []
+    for i in range(8):
+        a, b = ("A", 1024 * i, 1024 * i + 1024), ("A0", 1024 * i, 1024 * i + 1024)
+        ia.append(gp(1024, lambda q, T, r, a=a, b=b: [q.affine_select(r(a), r(b), [[0, 1024]], OP.is_ge, 0.0, 0, 0)], [b], [a]))
+    for i in range(3):
+        zero(("RW", 512 * i, 512 * i + 512))
+    tag[0] = 23
+    zero(("DN1", 0, 512), -int(MAGIC) - 32896)
+    idl = dma([(lambda T: T.D1[0:128:16, 0:W], lambda T: T.DN1[:])], [("DN1", 0, 512)], [("D1", 0, W)], 262144, late_loads)
+    for h in range(2):
+        diag(("EO", 256 * h, 256 * h + 256), ("ZN", 0, 256), [[-16, 8], [-1, 16], [1024, 2]], 1.0, -1024 * h)
 
-    def write_a(hh, ll, off, stage, after):
-        bk = nb_()
-        pew(to_wide(bk, [(hh, 0), (ll, 1)]), 8)
-        flex(stage, (bk, 0, 512), BA)
-        return scat(("A", 0, WD), off, stage, "s", after)
+    turn = [0, 0]
 
-    def write_b(hh, ll, off, stage, after):
-        bk = nb_()
-        pew(to_wide(bk, [(hh, 0), (ll, 0)]), 8)
-        flex(stage, (bk, 0, 512), 32896.0)
-        return scat(("B", 0, WD), off, stage, "v", after)
+    def write(lists, off, engs, after, stage=None, banks=None):
+        n = sz(lists[0][0]) // 32
+        if stage is None:
+            turn[1] ^= 1
+            stage = ("WS", 1024 * turn[1], 1024 * turn[1] + 512 * n)
+        for b in range(n):
+            turn[0] ^= 1
+            bk = banks[b] if banks else "P%d" % (6 + turn[0])
+            rs = list(range(b, 16, n))
+            grp = [[((bk, i, 512, len(rs)), sel("ZS", 144 * r, row), a) for a, row in lists] for i, r in enumerate(rs)]
+            per = 16 // len(lists)
+            for i in range(0, len(grp), per):
+                pe(grp[i:i + per])
+            flex(stage if n == 1 else (stage[0], stage[1] + b, stage[2], 2), (bk, 0, 512), BA if engs[0] == "s" else -MAGIC - 32896.0)
+        return [scat(("A" if engs[0] == "s" else "D1", 0, WD), sub(off, b), stage if n == 1 else sub(stage, 16 * b, 16), engs[0], after) for b in range(n)]
 
-    early, late, bw = {}, {-1: []}, []
-    dead = [b32("DD", 0), b32("DD", 1)]
+    def pairs(hh, ll, rows, off, eng, after, banks=None):
+        if par["pair"] and sz(hh) == 64:
+            return write([(hh, rows[0]), (ll, rows[1])], off, eng, after, None, banks)
+        return [x for s in range(sz(hh) // 32) for x in write([(sub(hh, s), rows[0]), (sub(ll, s), rows[1])], sub(off, s), eng, after)]
+
+    aw, pw, ga, d1w, d2w, base = {-1: ia}, {-1: []}, [], [], [], []
+
+    def delta(hh, ll, off, eng, banks=None):
+        if eng == "s":
+            d2w.extend(pairs(hh, ll, (3, 3), off, "s", base + ga, banks))
+        else:
+            d1w.extend(pairs(hh, ll, (0, 0), off, "v", [idl], banks))
 
     def walks(t, h):
         isp = h == t % 2
         old = t == 0 or (t == 1 and isp)
-        win, off = (("A0", 0, W), 0.0) if old else (("A", 0, W), -128.0)
-        after = [] if old else [ia] if isp else early[t - 1] + late[t - 1]
-        sb, cb, kb = "P%d" % h, "P%d" % (2 + h), "P%d" % (4 + h)
+        win = ("A0", 0, W) if old else ("A", 0, W)
+        after = [] if old else aw[0] if isp else aw[t - 1]
+        sb, pb, n = "P%d" % h, "P%d" % (2 + h), blk(t)
         z = ("Z%d" % t if t else "D0", h, 1024, 2)
-        m = ("M", 128 * h, 128 * h + 128)
+        slot = lambda k: (pb, 6 - k, 64 * n, n)
         for k in range(1, 6):
-            if t > 0 and not isp and PARAM["split"]:
-                for s in range(2):
+            if (k > 1 or t == 0) and (k < 5 or t < 2 or isp):
+                sides = [(0, 1)] if t == 2 and k == 5 else [(0, 1), (1, 1)] if par["split"] and t > 0 and not isp else [(0, 2)]
+                for s, m in sides:
                     o_ = 2048 * h + 1024 * (k % 2) + 512 * s
-                    sp = ("P%d" % s, 32 * s, 32 * s + 32)
-                    gat(("GS", o_, o_ + 512), win, Uu(t, h, k, s), "s", after[:4] if k == 1 else after)
-                    pe([to_list(sp, ("GS", o_, o_ + 512), 0) + [(sp, IN, Cc(t, h, k - 1, s) if k > 1 else b32("R", h))]])
+                    g_ = ("GS", o_, o_ + 512 * m)
+                    sp = (sb, 32 * s, 32 * (s + m))
+                    x = gat(g_, win, sub(Uu(t, h, k), s, m), "sv", after)
+                    if not old:
+                        ga.append(x)
+                    prev = [(sp, KN, sub(Kk(t, h, k - 1), s, m)), const(sp, k - 2)] if k > 1 else [(sub(sp, s), IN, R(h)) for s in range(2)]
+                    pe([to_list(sp, g_, 0) + prev])
                     if k < 5:
-                        ts(Uu(t, h, k + 1, s), sp, off, float(W - 1), OP.add, OP.min)
-                    flex(Cc(t, h, k + 1, s), sp, off)
-            elif k > 1 or t == 0 or not isp:
-                g_ = ("GS", 2048 * h + 1024 * (k % 2), 2048 * h + 1024 * (k % 2) + 1024)
-                gat(g_, win, Uu(t, h, k), "sv" if old else "s", after[:4] if k == 1 else after)
-                prev = [((sb, 0, 64), IN, Cc(t, h, k - 1))] if k > 1 else [((sb, 32 * s, 32 * s + 32), IN, b32("R", h)) for s in range(2)]
-                pe([to_list((sb, 0, 64), g_, 0) + prev])
-                if k < 5:
-                    ts(Uu(t, h, k + 1), (sb, 0, 64), off, float(W - 1), OP.add, OP.min)
-                flex(Cc(t, h, k + 1), (sb, 0, 64), off)
-            if 2 <= k <= 4:
-                tt(b32("OV", 3 * h + k - 2), Cc(t, h, k, 0), Cc(t, h, 1, 1), OP.is_equal)
+                        ts(sub(Uu(t, h, k + 1), s, m), sp, float(W - 1), None, OP.min)
+                    key(t, h, k + 1, sp, sub(Kk(t, h, k + 1), s, m))
+                    if t > 0 and k < 4 and s == 0:
+                        tt(b32("OV", 3 * h + k - 1), sub(sp, 0), NE(h, 1), OP.is_equal)
             c_ = 2048 * h + 1024 * (k % 2)
-            for s in range(2):
-                cmpg(("CM", c_ + 512 * s, c_ + 512 * s + 512), Uu(t, h, k, s), z)
-            blk = [b32("OV", 3 * h + j - 2) for j in range(2, k)] + ([dead[h]] if t > 1 or (t == 1 and isp) else [])
-            pe([to_list((cb, 0, 64), ("CM", c_, c_ + 1024), ALL) + [((cb, 0, 32), IBM(5), a) for a in blk]])
-            sg = ("SG", 128 * h + 64 * (k % 2), 128 * h + 64 * (k % 2) + 64)
-            add([("s", 15.0 + vc(64), lambda q, T, r, sg=sg: [q.activation(r(sg), r((cb, 0, 64)), AF.Sign, bias=-8.5)])], [(cb, 0, 64)], [sg])
-            ck = Cc(t, h, k)
-            pe([[((kb, 0, 128), IP, ("C", ck[1], ck[1] + 128)), ((kb, 0, 64), IBM(k - 1), sg), ((kb, 64, 128), IBM(k - 1), sg)]])
-            if k == 1:
-                flex(m, (kb, 0, 128))
-            else:
-                tt(m if k < 5 else ("MN", 128 * h, 128 * h + 128), (kb, 0, 128), m, OP.max)
+            if t == 0:
+                cmpg(("CM", c_, c_ + 1024), Uu(t, h, k), ("D0", h, 2048, 2))
+            for s in range(2 if t else 0):
+                cmpg(("CM", c_ + 512 * s, c_ + 512 * s + 512), sub(Uu(t, h, k), s), z)
+            stop = [b32("OV", 3 * h + j - 2) for j in range(2, k)] if t else []
+            stop += [b32("SP", j) for j in range(t) if j % 2 != h]
+            ends = [[const(slot(6), 6)]] + ([[const(slot(0), 5)]] if t == 2 else []) if k == 1 else []
+            pe([to_list(slot(k), ("CM", c_, c_ + 1024), ALL) + [const(slot(k), 4)] + [(sub(slot(k), 0), IBM(0), a) for a in stop]] + ends)
 
     def embed(t, h):
         isp = h == t % 2
-        kb = "P%d" % (4 + h)
-        mn = lambda i, n=1: b32("MN", 4 * h + i, n)
-        wn = lambda i, n=1: b32("WN", 4 * h + i, n)
-        ne = b32("NE", h)
-        ts(wn(0, 4), mn(0, 4), 16383, None, OP.bitwise_and)
-        tt(b32("E", 3 * h), mn(0), mn(1), OP.min)
-        tt(b32("E", 3 * h + 1), wn(0), wn(1), OP.not_equal)
-        tt(b32("E", 3 * h + 2), b32("E", 3 * h), b32("E", 3 * h + 1), OP.min)
-        ts(ne, b32("E", 3 * h + 2), 0.5, None, OP.is_lt)
-        parts = [(Cc(t, h, 1), mn(0, 2)), (b32("ST", 1, 2), mn(0, 2))] + ([(Cc(t, h, 2), mn(2, 2))] if not isp and t < 2 else [])
-        pe([[((kb, 64 * i, 64 * i + 64), IP, a)] + [((kb, 64 * i + 32 * s, 64 * i + 32 * s + 32), IBM(6), ne) for s in range(2)]
-            for i, (a, _) in enumerate(parts)])
-        o = 192 * h
-        for i, (_, mm) in enumerate(parts):
-            tt(("M2", o + 64 * i, o + 64 * i + 64), (kb, 64 * i, 64 * i + 64), mm, OP.max)
-        ts(("M3", o, o + 64 * len(parts)), ("M2", o, o + 64 * len(parts)), 16383, None, OP.bitwise_and)
-        u1 = Uu(t + 1, h, 1)
-        cp(("U", u1[1], u1[1] + 128), ("M3", o, o + 128))
-        cp(Cc(t + 1, h, 1), ("M3", o, o + 64))
-        if len(parts) == 3:
-            ts(Uu(t + 1, h, 2), ("M3", o + 128, o + 192), float(W - 1), None, OP.min)
-            cp(Cc(t + 1, h, 2), ("M3", o + 128, o + 192))
+        sb, pb, n = "P%d" % h, "P%d" % (2 + h), blk(t)
+        kb, sc = Kk(t, h, 1)[0], "SC%d" % h
+        lo, hi, lw, fs = (sb, 64, 192), (sb, 192, 320), (sb, 320, 384), (sb, 384, 416)
+        pe([[const((sb, 64, 416), CE)] + [(sub(a, 2 * i, 2), KP, Kk(t, h, 1 + i)) for a in (lo, hi) for i in range(2)]
+            + [(lw, IP, DUM), (fs, IP, LN[h])]], True, False, sb)
+        m = 64 * n
+        scan((sc, 0, m), (pb, 0, m), (kb, 1, m + 1))
+        o = 2 if t == 2 else 0
+        scan((sc, m, 2 * m), (pb, 0, m), (kb, o, m + o))
+        nf = 4
+        if t == 2 and isp:
+            scan((sc, 2 * m, 2 * m + m // 2), (pb, 0, m // 2), (kb, 0, m // 2))
+            nf = 5
+        fin = (sc, 5, 5 + 32 * nf * n - n + 1, n)
+        mn, wn = b32("MN", 5 * h, nf), b32("WN", 5 * h, nf)
+        tt(b32("E", 2 * h + 1), sub(fin, 0), sub(fin, 1), OP.min)
+        ts(mn, fin, 1 / KEY, None, OP.mult)
+        ts(wn, mn, W - 1, None, OP.bitwise_and)
+        cp(UW(h, 0, nf), wn)
+        tt(b32("E", 2 * h), sub(wn, 0), sub(wn, 1), OP.is_equal)
+        tt(EM(h), b32("E", 2 * h), b32("E", 2 * h + 1), OP.is_le)
+        pe([[(fs, IBM(4 + h), EM(h))] + [(sub(a, i), IBM(j), EM(h)) for a, j in ((lo, 1), (hi, 2), (lw, 1)) for i in range(sz(a) // 32)]], False, True, sb)
         if t < 2:
-            src = ("P%d" % (2 + h), 64, 96)
-            pe([[(src, IP, LN[h]), (src, IBM(8 - h), ne)]])
-            cp(b32("FS", 2 * t + h), src)
+            cp(b32("FS", 2 * t + h), fs)
             send(b32("FS", 2 * t + h), b32("FO", 2 * t + h), 2 + 2 * t + h)
-            gat(("Z%d" % (t + 1), h, 1024, 2), ("ZW%d" % (t + 1), 0, 3072), b32("FO", 2 * t + h), "sv")
+        tt(b32("TM", 4 * h, 4), lo, sub(wn, 0, 4), OP.max)
+        tt(NE(h, 0, 4), hi, b32("TM", 4 * h, 4), OP.min)
+        tt(NE(h, 4, 2), lw, sub(wn, 0, 2), OP.max)
+        u1 = Uu(t + 1, h, 1)
+        cp(("U", u1[1], u1[1] + 192), NE(h, 0, 6))
+        if t < 2:
+            key(t + 1, h, 1, NE(h, 0, 2))
+            if not isp:
+                key(t + 1, h, 2, NE(h, 2, 2))
+                tt(b32("OV", 3 * h), NE(h, 2), NE(h, 1), OP.is_equal)
+            gat(("Z%d" % (t + 1), h, 1024, 2), ("ZW%d" % (t + 1), 0, 3072), b32("FO", 2 * t + h))
 
-    def roots(h):
-        tt(b32("RV", h), Cc(3, h, 1, 0), Cc(3, h, 1, 1), OP.add)
-        flex(b32("RVH", h), b32("RV", h), 64.0)
-        tt(b32("RVL", h), b32("RV", h), b32("RVH", h), OP.subtract)
-        st = ("BN" if h else "PM", 0, 512)
-        if PARAM["roots"][h] == "v":
-            bw.append(write_b(b32("RVH", h), b32("RVL", h), b32("RU", h), st, [ib]))
-        else:
-            early[2].append(write_a(b32("RVH", h), b32("RVL", h), b32("RU", h), st, late[1]))
+    def told(out, st, h):
+        return [(out, sel("ZP", 144 * st, r), ("LW", 2 * r + h, 1024, 32)) for r in range(16)]
+
+    def digits(hh, ll, src):
+        flex(hh, src, 64.0)
+        tt(ll, src, hh, OP.subtract)
+
+    def root(out, h):
+        return [(out, IP, NE(h, 0)), (out, IP, NE(h, 1)), (out, IN, b32("NI", 2 * h)), (out, IN, b32("NI", 2 * h + 1))]
 
     def parents(t):
         h = t % 2
         q_ = 1 - h
-        wn = lambda i, n=1: b32("WN", 4 * h + i, n)
-        R, ne, sb = b32("R", h), b32("NE", h), "P%d" % h
-        pt = lambda i: b32("PT", i)
-        old = t < 2
-        ts(("UB", 0, 96), wn(0, 3), float(W - 1), None, OP.min)
-        gat(("GK", 512, 1024), ("A0", 0, W) if old else ("A", 0, W), b32("UB", 2), "sv" if old else "s")
-        gat(("GK", 0, 512), ("KW", 0, W), b32("UB", 0), "sv")
-        pe([to_list((sb, 96, 128), ("GK", 512, 1024), 0) + ([] if old else [((sb, 96, 128), IBM(5), ("ONE", 0, 32))] * 2)])
-        pe([to_list((sb, 64, 96), ("GK", 0, 512), 0) + [((sb, 64, 96), IBM(6), ne)]])
-        tt(pt(0), (sb, 96, 128), wn(0), OP.subtract)
-        tt(pt(1), wn(2), wn(1), OP.is_equal)
-        tt(pt(2), R, pt(0), OP.subtract)
-        tt(pt(3), pt(2), pt(1), OP.mult)
-        tt(pt(4), pt(3), pt(0), OP.add)
-        flex(b32("LH", 3), pt(4))
-        tt(b32("LL", 3), pt(4), b32("LH", 3), OP.subtract)
-        cp(b32("LH", 0, 3), wn(0, 3))
-        tt(b32("LL", 0, 3), wn(0, 3), b32("LH", 0, 3), OP.subtract)
-        tt(pt(5), (sb, 64, 96), LDUM, OP.min)
-        cp(("LO", 0, 32), pt(5))
-        bk = nb_()
-        mm = [((bk, 0, 512), IBM(9), ("LT", h, 1024, 2))]
-        for lists in ([(b32("LH", 0), 0), (b32("LL", 0), 1)], [(b32("LH", 2), 6), (b32("LL", 2), 7)], [(b32("LH", 3), 4), (b32("LL", 3), 5)]):
-            mm += [x for grp in to_wide(bk, lists) for x in grp]
-        cuts = [0, 1, 17, 33, 49, 65, 81, 97]
-        for i in range(7):
-            pe([mm[cuts[i]:cuts[i + 1]]], i == 0, i == 6)
-        flex(("LS", 0, 512), (bk, 0, 512))
-        dma([(lambda T: T.LW[:, 0:1024], lambda T: T.LT[:])], [("LT", 0, 1024)], [("LW", 0, 1024)], 262144)
-        scat(("LW", 0, 1536), ("LO", 0, 32), ("LS", 0, 512), "v")
-        for i in range(4):
-            pe([[((sb, 128 + 32 * i, 160 + 32 * i), sel("ZP", 144 * i, r), ("LW", 2 * r + q_, 1024, 32)) for r in range(16)]])
-        flex(("LI", 0, 128), (sb, 128, 256))
+        gat(("G1", 0, 512), ("KW", 0, W), UW(h, 0), scale=M1)
+        gat(("G2", 0, 512), ("KW", 0, W), UW(h, 2 if t < 2 else 4), scale=M2, bias=B2)
+        kb = ("P%d" % (2 + h), 448, 480)
+        pe([to_list(kb, ("G1", 0, 512), 1)], True, False, kb[0])
+        pe([[(kb, IBM(3), EM(h))]], False, True, kb[0])
+        tt(b32("PT", 0), kb, LDUM, OP.min)
+        ts(b32("LO", t), b32("PT", 0), 4096.0, None, OP.add)
+        scat(("LW", 0, 1536), b32("LO", t), ("G1", 0, 512), "v", src2=("G2", 0, 512))
+        for i, st in enumerate((4, 2, 5)):
+            o = ("P4", 32 * i, 32 + 32 * i)
+            pe([told(o, st, q_) + ([(o, ("ONE", 0, 128, 1, 1), ("ONE", 0, 32, 1, 1))] if st == 5 else [])])
+        flex(b32("LI", 0, 3), ("P4", 0, 96))
+        tt(b32("Q", 0), b32("LI", 2), R(q_), OP.mult)
         tag[0] += 1
-        for s in range(2):
-            tt(b32("VC", s), wn(2 + s), R, OP.add)
-        flex(("VH", 0, 64), ("VC", 0, 64), 64.0)
-        tt(("VL", 0, 64), ("VC", 0, 64), ("VH", 0, 64), OP.subtract)
-        early[t] = [write_a(b32("VH", s), b32("VL", s), Uu(t + 1, h, 0, s), ("WE", 512 * s, 512 * s + 512), [ia] + late[t - 1]) for s in range(2)]
-        Q = lambda i, n=1: b32("Q", i, n)
-        li = lambda i: b32("LI", i)
-        tt(Q(1), li(0), b32("R", q_), OP.is_equal)
-        tt(Q(6), li(0), li(3), OP.subtract)
+        if t < 2:
+            tt(b32("PT", 1), NE(h, 2), NE(h, 1), OP.is_equal)
+        else:
+            sb = "P%d" % h
+            pe([[((sb, 0, 64), IN, NE(h, 2, 2))] + [((sb, 32 * s, 32 * s + 32), IP, R(h)) for s in range(2)], root((sb, 64, 96), h)])
+            digits(b32("HP", 0, 3), b32("LP", 0, 3), (sb, 0, 96))
+            delta(b32("HP", 0, 2), b32("LP", 0, 2), Uu(3, h, 0), par["last"][0])
+            if not par["roots"]:
+                delta(b32("HP", 2), b32("LP", 2), b32("RU", h), par["last"][1])
 
     def children(t):
         h = 1 - t % 2
-        wn = lambda i, n=1: b32("WN", 4 * h + i, n)
+        p_ = 1 - h
         Q = lambda i, n=1: b32("Q", i, n)
-        li = lambda i: b32("LI", i)
-        ne, cb = b32("NE", h), "P%d" % (2 + h)
-        n0, n1 = Cc(t + 1, h, 1, 0), Cc(t + 1, h, 1, 1)
-        gat(("GX", 0, 512), ("X", 0, W), Uu(t + 1, h, 1, 1), "sv")
-        cmpg(("CK", 0, 512), Uu(t + 1, h, 1, 0), ("GX", 0, 512))
-        pe([to_list((cb, 96, 128), ("CK", 0, 512), ALL)])
-        tt(Q(7), n0, n1, OP.subtract)
-        tt(Q(11), wn(2), li(3), OP.add)
-        tt(Q(12), li(1), n1, OP.add)
-        tt(Q(13), wn(3), li(0), OP.add)
-        tt(Q(14), li(2), n0, OP.add)
-        ns = Cc(3, 0, 2, 0) if t == 1 else Q(18)
-        tt(ns, Q(1), ne, OP.max)
-        tt(Q(15), ns, DUM, OP.mult)
-        tt(Q(16), li(0), Q(15), OP.max)
-        tt(Q(17), li(3), Q(15), OP.max)
-        cp(("QO", 0, 64), Q(16, 2))
+        li = lambda i, n=1: b32("LI", i, n)
+        cb, spl = ("P%d" % (2 + h), 448, 480), b32("SP", t)
+        gat(("GX", 0, 512), ("X", 0, W), UW(h, 1))
+        cmpg(("CK", 0, 512), UW(h, 0), ("GX", 0, 512))
+        pe([to_list(cb, ("CK", 0, 512), ALL)])
+        tt(spl, EM(h), li(2), OP.is_gt)
+        t3 = lambda i, n=1: ("P4", 160 + 32 * i, 160 + 32 * (i + n))
+        dif = lambda o, a, b: [(o, IP, a), (o, IN, b)]
+        cross = lambda o: [(o, IP, NE(h, 0, 2)), (sub(o, 0), IN, li(1)), (sub(o, 1), IN, li(0))]
+        nq = 1 if t < 2 else 2
+        pe([dif(t3(0), NE(h, 0), NE(h, 1))])
+        pe([dif(t3(1), li(1), li(0))])
         if t < 2:
-            ts(dead[h], ns, -1.0, 1.0, OP.mult, OP.add)
+            pe([cross(t3(2, 2))])
+        pe([[(t3(4, nq), IP, sub(DUM, 0, nq))] + [(t3(4 + i), IBM(1), spl) for i in range(nq)]])
+        tt(Q(1, nq), t3(4, nq), li(0, nq), OP.max)
+        cp(b32("QO", 0, nq), Q(1, nq))
+        v = lambda i, n=1: ("P5", 32 * i, 32 * (i + n))
+        pe([[const(v(0, 5), CV)] + (told(v(4), 3, h) if t < 2 else [])], True, False, "P5")
+        pe([[(v(0), IP, Q(0)), (v(1), IP, Q(0)), (v(0, 2), IP, li(0, 2))]], False, False, "P5")
+        if t < 2:
+            for i in range(2):
+                zero(("LW", 512 * i, 512 * i + 512))
+            for i, j in ((3, 0), (4, 2), (5, 3)):
+                tt(Q(i), t3(j), spl, OP.mult)
+            pe([[(v(0, 2), IP, NE(h, 2, 2)), (v(2, 2), IP, Q(4, 2)), (v(4), IP, Q(4))]], False, False, "P5")
         else:
-            tt(Cc(3, 1, 2, 0), ns, dead[h], OP.is_gt)
-        ts(Q(19), (cb, 96, 128), 9.0, None, OP.is_ge)
-        tt(Q(6), Q(6), Q(19), OP.mult)
-        tt(Q(7), Q(7), Q(19), OP.mult)
-        tt(("V4", 0, 64), Q(11, 2), Q(6, 2), OP.add)
-        tt(("V4", 64, 128), Q(13, 2), Q(6, 2), OP.subtract)
-        for i in range(2):
-            flex(b32("H4", 2 * i, 2), b32("V4", 2 * i, 2), 64.0)
-            tt(b32("L4", 2 * i, 2), b32("V4", 2 * i, 2), b32("H4", 2 * i, 2), OP.subtract)
-        offs = [Uu(t + 1, h, 0, 0), b32("QO", 0), Uu(t + 1, h, 0, 1), b32("QO", 1)]
-        late[t] = []
-        for i in ((1, 3, 0, 2) if t < 2 else (1, 0, 3, 2)):
-            st = ("WS", 512 * i, 512 * i + 512)
-            if t == 2 and i % 2 == 1:
-                bw.append(write_b(b32("H4", i), b32("L4", i), offs[i], st, [ib]))
-            else:
-                late[t].append(write_a(b32("H4", i), b32("L4", i), offs[i], st, [ia] + (early[t] if i % 2 == 1 else [])))
+            pe([[(v(0, 2), IN, NE(h, 2, 2))] + cross(v(2, 2))], False, False, "P5")
+        ts(Q(6), cb, 17.0, None, OP.is_ge)
+        tt(Q(7), t3(1), Q(6), OP.mult)
+        tt(Q(8), Q(3) if t < 2 else t3(0), Q(6), OP.mult)
+        pe([[(v(0), IP, Q(7)), (v(1, 2), IN, Q(7, 2)), (v(3), IP, Q(8))] + ([(v(4), IN, Q(8))] if t < 2 else [])], False, True, "P5")
+        nv_ = 5 if t < 2 else 4
+        digits(b32("H5", 0, nv_), b32("L5", 0, nv_), v(0, nv_))
+        hl = lambda i, row: [(b32("H5", i), row), (b32("L5", i), row + 1)]
+        if t == 2:
+            delta(b32("H5", 2, 2), b32("L5", 2, 2), ("QO", 0, 64), "v" if par["last"][0] == "s" else "s")
+            delta(b32("H5", 0, 2), b32("L5", 0, 2), Uu(3, h, 0), par["last"][3], ("P5", "P4"))
+            ts(b32("LV", 0), b32("SP", 1), 0.0, None, OP.is_equal)
+            tt(b32("LV", 1), b32("SP", 0), spl, OP.is_equal)
+            return
+        aft = aw[-1] + pw[t - 1]
+        aw[t] = pairs(b32("H5", 0, 2), b32("L5", 0, 2), (0, 1), Uu(t + 1, h, 0), "s", aft)
+        wb = write(hl(4, 0) + hl(3, 4) + hl(2, 6), b32("QO", 0), "s", aft, ("RW", h, 1024, 2), ("P5",))
+        aw[t] += wb
+        tag[0] += 1
+        sb = "P%d" % p_
+        gat(("GR", 0, 512), ("RW", 0, 1536), b32("LO", t))
+        if t == 0:
+            zero(("RW", h, 1024, 2))
+        pe([to_list((sb, 128, 160), ("GR", 0, 512), 3)])
+        tt(b32("PT", 2), (sb, 128, 160), b32("PT", 1), OP.mult)
+        pe([[((sb, 0, 64), IP, NE(p_, 2, 2))] + to_list((sb, 0, 32), ("GR", 0, 512), 2)], True, False, sb)
+        pe([[((sb, 32, 64), IP, b32("PT", 2))]], False, True, sb)
+        ts(Uu(t + 1, p_, 2), (sb, 0, 64), float(W - 1), None, OP.min)
+        key(t + 1, p_, 2, (sb, 0, 64))
+        tt(b32("OV", 3 * p_), (sb, 0, 32), NE(p_, 1), OP.is_equal)
+        tag[0] = 25
+        vb = ("P4", 448, 512)
+        pe([[(vb, KP, Kk(t + 1, p_, 2)), const(vb, ("CR", 576, 640))] + [(sub(vb, s), IP, R(p_)) for s in range(2)]])
+        digits(b32("HP", 0, 2), b32("LP", 0, 2), vb)
+        pw[t] = pairs(b32("HP", 0, 2), b32("LP", 0, 2), (0, 1), Uu(t + 1, p_, 0), "s", wb)
 
+    fb = lambda i: ("P%d" % (2 * i), 256, 512)
+    cs = lambda nm, i: (nm, 256 * i, 256 * i + 256)
     for t in range(3):
         p_ = t % 2
         tag[0] = 1 + 7 * t
@@ -486,70 +569,172 @@ def build():
         walks(t, 1 - p_)
         tag[0] += 1
         embed(t, p_)
-        tag[0] += 1
+        if t == 2:
+            base.append(dma([(lambda T: T.NHF[:], lambda T: T.A[0:128:16, 0:W]), (lambda T: T.NLF[:], lambda T: T.A[1:128:16, 0:W])],
+                            [("A", 0, W)], [("NHF", 0, 512), ("NLF", 0, 512)], 524288, aw[1] + pw[1]))
         parents(t)
         if t == 2:
-            roots(p_)
+            for i in range(2):
+                pe([[(fb(i), IP, cs("NHF", i)), (fb(i), IP, cs("NLF", i)), const(fb(i), CG)]], True, False, fb(i)[0])
         tag[0] += 1
         embed(t, 1 - p_)
         if t == 2:
-            roots(1 - p_)
+            pe([root(("P1", 0, 32), 1)])
+            digits(b32("HP", 3), b32("LP", 3), ("P1", 0, 32))
+            i = 2 if par["roots"] else 3
+            delta(b32("HP", i, 4 - i), b32("LP", i, 4 - i), b32("RU", i - 2, 4 - i), par["last"][2])
         tag[0] += 1
         children(t)
-        tag[0] += 1
         if t == 0:
+            tag[0] = 23
             send(("Z1", 0, 1024), ("ZW2", 1024, 2048), 1)
-            dma([(lambda T: T.ZW2[16:128, 2048:3072], lambda T: T.ZW2[0:112, 1024:2048]), (lambda T: T.ZW2[0:16, 2048:3072], lambda T: T.ZW2[112:128, 1024:2048])],
-                [("ZW2", 1024, 2048)], [("ZW2", 2048, 3072)], 262144)
+            rotate("ZW2")
 
-    lo = [Cc(3, h, 1)[1] for h in range(2)]
-    add([("t", 60.0 + 2048 * PCY, lambda q, T, r: [q.matmul(T.P2[0:96, 256:512], T.C[:, lo[h]:lo[h] + 96], T.EO[:, 256 * h:256 * h + 256], h == 0, h == 1) for h in range(2)])],
-        [("C", lo[0], lo[0] + 96), ("C", lo[1], lo[1] + 96), ("EO", 0, 512)], [("P2", 256, 512)])
-    add([("s", 15.0 + vc(256), lambda q, T, r: [q.activation(T.OB[0:96, :], T.P2[0:96, 256:512], AF.Copy)]),
-         ("v", vc(256), lambda q, T, r: [q.tensor_copy(T.OB[0:96, :], T.P2[0:96, 256:512])])], [("P2", 256, 512)], [("OB", 0, 256)])
-    prs = []
-    for g_ in range(8):
-        prs.append((lambda T, g_=g_: T.yn[g_, :], lambda T, g_=g_: T.OB[0:64, 32 * g_:32 * g_ + 32]))
-        prs.append((lambda T, g_=g_: T.yl[g_, :], lambda T, g_=g_: T.OB[64:96, 32 * g_:32 * g_ + 32]))
-    dma(prs, [("OB", 0, 256)], [], 98304)
-    dma([(lambda T: T.NHF[:], lambda T: T.A[0:128:16, 0:W]), (lambda T: T.NLF[:], lambda T: T.A[1:128:16, 0:W])],
-        [("A", 0, W)], [("NHF", 0, 512), ("NLF", 0, 512)], 524288, early[2] + late[2] + late[1], q="s")
-    dma([(lambda T: T.BN[:], lambda T: T.B[0:128:16, 0:W])], [("B", 0, W)], [("BN", 0, 512)], 262144, bw)
+    tag[0] = 21
+    for nm, n, bk, ob in (("yn", 64, "P1", "RW"), ("yl", 32, "P3", "TM")):
+        a = [NE(h, 0, 2) if nm == "yn" else b32("LV", h) for h in range(2)]
+        add([("t", 60.0 + 2048 * PCY, lambda q, T, r, a=a, n=n, bk=bk: [q.matmul(T[bk][0:n, 256:512], r(a[h]), T.EO[:, 256 * h:256 * h + 256], h == 0, h == 1) for h in range(2)])],
+            a + [("EO", 0, 512)], [(bk, 256, 512)])
+        add([("s", 15.0 + vc(256), lambda q, T, r, n=n, bk=bk, ob=ob: [q.activation(T[ob][0:n, 0:256], T[bk][0:n, 256:512], AF.Copy)]),
+             ("v", vc(256), lambda q, T, r, n=n, bk=bk, ob=ob: [q.tensor_copy(T[ob][0:n, 0:256], T[bk][0:n, 256:512])])], [(bk, 256, 512)], [(ob, 0, 256)])
+        dma([(lambda T, g_=g_, nm=nm: T[nm][g_, :], lambda T, g_=g_, n=n, ob=ob: T[ob][0:n, 32 * g_:32 * g_ + 32]) for g_ in range(8)], [(ob, 0, 256)], [], 65536)
+    dma([(lambda T: T.DN2[:], lambda T: T.A[3:128:16, 0:W])], [("A", 0, W)], [("DN2", 0, 512)], 262144, d2w, q="s")
+    dma([(lambda T: T.DN1[:], lambda T: T.D1[0:128:16, 0:W])], [("D1", 0, W)], [("DN1", 0, 512)], 262144, d1w)
     for i in range(2):
-        cs = lambda nm: (nm, 256 * i, 256 * i + 256)
-        bk = ("P%d" % i, 256, 512)
-        pe([[(bk, IP, cs("NHF")), (bk, IP, cs("NLF"))]])
-        tt(cs("NS"), bk, cs("BN"), OP.max)
-        ts(cs("KD"), cs("NS"), 32767, None, OP.bitwise_and)
-        ts(cs("ZN"), cs("KD"), -128.0, None, OP.add)
-    dma([(lambda T: T.ys[:], lambda T: T.ZN[:])], [("ZN", 0, 512)], [], 262144)
+        pe([[(fb(i), IP, cs("DN2", i))]], False, True, fb(i)[0])
+        tt(cs("NLF", i), fb(i), cs("DN1", i), OP.add)
+    dma([(lambda T: T.ys[:], lambda T: T.NLF[:])], [("NLF", 0, 512)], [], 262144)
     return ops
 
 
-def isps(a):
-    return a[0][0] == "P" and a[0][1:].isdigit()
-
-
-def schedule(ops, par):
+def place(ops, pri, pred, succ, fixed, hop, par):
     n = len(ops)
-    pred = [sorted(o["dep"]) for o in ops]
+    left = [len(p) for p in pred]
+    rdy = [0.0] * n
+    todo = sorted(range(n), key=lambda j: (pri[j], -j))
+    passed = [False] * n
+    late = []
+    busy = {e: [] for e in "vstgyn"}
+    lock, out = {}, []
+    while todo or late:
+        if late:
+            i = max(late, key=lambda j: (pri[j], -j))
+            late.remove(i)
+        else:
+            i = todo.pop()
+            if left[i]:
+                passed[i] = True
+                continue
+        o = ops[i]
+        lk, lat = o["lk"], o["lat"] + hop
+        best = None
+        for a in (o["alts"] if fixed is None else (fixed[i],)):
+            e, d = a[0], a[1]
+            s = rdy[i]
+            iv = busy[e]
+            k = len(iv)
+            while k and iv[k - 1][1] > s:
+                k -= 1
+            while True:
+                while k < len(iv) and iv[k][0] < s + d:
+                    if iv[k][1] > s:
+                        s = iv[k][1]
+                    k += 1
+                s0 = s
+                for nm, w, bank in lk:
+                    lv = lock.get(nm, ())
+                    m = len(lv)
+                    while m and lv[m - 1][0] > s - (2500.0 if bank else 9000.0):
+                        m -= 1
+                    while m < len(lv) and lv[m][0] < s + d + lat:
+                        x = lv[m]
+                        if x[1] > s and ((x[2] != e) if bank else (w or x[3])):
+                            s = x[1]
+                        m += 1
+                if s == s0:
+                    break
+            if fixed is not None:
+                best = (s, s, a, k)
+            else:
+                f = s + d + (par["flex0" if s + d < par["xl"] else "flexv"] * d if e == "v" else 0.0)
+                if best is None or f < best[0]:
+                    best = (f, s, a, k)
+        _, s, a, k = best
+        end = s + a[1] + lat
+        if a[0] != "n":
+            busy[a[0]].insert(k, (s, s + a[1]))
+        for nm, w, bank in lk:
+            lv = lock.setdefault(nm, [])
+            m = len(lv)
+            while m and lv[m - 1][0] > s:
+                m -= 1
+            lv.insert(m, (s, end, a[0], w))
+        out.append((i, a, s, end - hop))
+        for j in succ[i]:
+            if end > rdy[j]:
+                rdy[j] = end
+            left[j] -= 1
+            if left[j] == 0 and passed[j]:
+                late.append(j)
+    out.sort(key=lambda x: (x[2], x[0]))
+    return out
+
+
+def blocks(ops, plan, pred, hop):
+    at, last, before = {}, {}, {}
+    for (i, a, s, e) in plan:
+        at[i] = (a, s, e)
+        before[i] = [last.get(a[0])] + [last.get(nm) for nm, w, bank in ops[i]["lk"]]
+        for k in [a[0]] + [nm for nm, w, bank in ops[i]["lk"]]:
+            last[k] = i
+    i = max(at, key=lambda j: at[j][2])
+    out = []
+    while True:
+        s = at[i][1]
+        dep = [j for j in pred[i] if at[j][2] + hop >= s - 0.5]
+        if dep:
+            i = dep[0]
+            continue
+        cand = [j for j in before[i] if j is not None]
+        if s < 0.5 or not cand:
+            return out
+        j = max(cand, key=lambda k: at[k][1] + at[k][0][1] if at[k][0][0] == at[i][0][0] else at[k][2] + hop)
+        out.append((j, i))
+        i = j
+
+
+def schedule(ops, par, c):
+    n = len(ops)
+    pred, above = [], []
+    for o in ops:
+        far = 0
+        for d in o["dep"]:
+            far |= above[d]
+        pred.append(sorted(d for d in o["dep"] if not far >> d & 1))
+        for d in o["dep"]:
+            far |= 1 << d
+        above.append(far)
     succ = [[] for _ in range(n)]
     for o in ops:
-        o["lk"] = sorted(set((x[0], w, isps(x)) for x, w in [(x, 0) for x in o["rd"]] + [(x, 1) for x in o["wr"]] if isps(x) or x[0] in ("A", "B")))
-        for d in o["dep"]:
+        lk = {}
+        for x, w in [(x, 0) for x in o["rd"]] + [(x, 1) for x in o["wr"]]:
+            if isps(x) or x[0] in ("A", "D1"):
+                lk[x[0]] = max(lk.get(x[0], 0), w)
+        o["lk"] = [(k, v, k[0] == "P") for k, v in sorted(lk.items())]
+        for d in pred[o["n"]]:
             succ[d].append(o["n"])
     pri = [0.0] * n
     for o in reversed(ops):
         i = o["n"]
-        pri[i] = min(a[1] for a in o["alts"]) + o["lat"] + HOP + max([pri[j] for j in succ[i]] + [0.0])
+        pri[i] = min(a[1] for a in o["alts"]) + o["lat"] + c["hop"] + max([pri[j] for j in succ[i]] + [0.0])
     best = None
-    seed = par.get("seed", 0)
+    seed = par["seed"]
     for _ in range(par["iters"]):
         p = []
         for i in range(n):
             seed = (seed * 1103515245 + 12345) % 2147483648
-            p.append(pri[i] + ops[i]["pri"] + par["boost"][ops[i]["tag"]] + par.get("noise", 0.0) * seed / 2147483648.0)
-        fw = one_pass(ops, par, p, pred, succ, None)
+            p.append(pri[i] + ops[i]["pri"] + par["boost"][ops[i]["tag"]] + par["noise"] * seed / 2147483648.0)
+        fw = place(ops, p, pred, succ, None, c["hop"], par)
         span = max(x[3] for x in fw)
         if best is None or span < best[0]:
             best = (span, fw)
@@ -557,51 +742,62 @@ def schedule(ops, par):
         for (i, a, s_, e_) in fw:
             fixed[i] = a
             back[i] = e_
-        for (i, a, s_, e_) in one_pass(ops, par, back, succ, pred, fixed):
+        for (i, a, s_, e_) in place(ops, back, succ, pred, fixed, c["hop"], par):
             pri[i] = e_
+    state = [seed]
+
+    def rnd():
+        state[0] = (state[0] * 1103515245 + 12345) % 2147483648
+        return state[0] / 2147483648.0
+    span, cur = best
+    either = [i for i in range(n) if len(ops[i]["alts"]) > 1]
+    fixed, tight = {}, []
+    for (i, a, s_, e_) in cur:
+        pri[i], fixed[i] = -s_, a
+    for it in range(par["moves"]):
+        p, f, x = list(pri), dict(fixed), rnd()
+        if x < 0.45:
+            if not tight:
+                tight.extend(blocks(ops, cur, pred, c["hop"]))
+            i, j = tight[int(rnd() * len(tight))]
+            if x < 0.15:
+                p[i] = p[j] - 1.0
+            elif x < 0.3:
+                p[j] = p[i] + 1.0
+                for k in pred[j]:
+                    p[k] = max(p[k], p[j] + 1.0)
+            else:
+                for k in (i, j):
+                    if len(ops[k]["alts"]) > 1 and rnd() < 0.7:
+                        f[k] = [a for a in ops[k]["alts"] if a is not f[k]][0]
+        elif x < 0.55:
+            i = either[int(rnd() * len(either))]
+            f[i] = [a for a in ops[i]["alts"] if a is not f[i]][0]
+        elif x < 0.8:
+            i, d, up = int(rnd() * n), rnd() * rnd() * 8000.0, rnd() < 0.5
+            seen, edge = {i}, [i]
+            for _ in range(1 + int(rnd() * 8)):
+                edge = [k for j in edge for k in (pred[j] if up else succ[j]) if k not in seen and abs(p[k] - p[i]) < 9000.0]
+                seen.update(edge)
+            for k in seen:
+                p[k] += d if up else -d
+        elif x < 0.9:
+            tg, lo, d = 1 + int(rnd() * 25), -rnd() * span, (rnd() + rnd() - 1) * 6000.0
+            for i in range(n):
+                if ops[i]["tag"] == tg and lo - 6000.0 < p[i] < lo:
+                    p[i] += d
+        else:
+            for _ in range(1 + int(rnd() * rnd() * 8)):
+                p[int(rnd() * n)] += (rnd() + rnd() - 1) * 3500.0
+        new = place(ops, p, pred, succ, f, c["hop"], par)
+        s = max(y[3] for y in new)
+        if s <= span + 300.0 * rnd() * rnd() * (1.0 - it / par["moves"]):
+            span, fixed, cur, tight = s, f, new, []
+            for (i, a, s_, e_) in new:
+                pri[i] = -s_
+            if s < best[0]:
+                best = (s, new)
     return best[1]
-
-
-def one_pass(ops, par, pri, pred, succ, fixed):
-    n = len(ops)
-    left = [len(p) for p in pred]
-    rdy = [0.0] * n
-    ready = [i for i in range(n) if not pred[i]]
-    free = {}
-    lock = {}
-    order = []
-    while ready:
-        cand = []
-        for i in ready:
-            best = None
-            o = ops[i]
-            for a in (o["alts"] if fixed is None else [fixed[i]]):
-                s = max(rdy[i], free.get(a[0], 0.0))
-                for nm, w, bank in o["lk"]:
-                    for (e, w2), end in lock.get(nm, {}).items():
-                        if end + HOP > s and ((bank and e != a[0]) or (not bank and (w or w2))):
-                            s = end + HOP
-                f = s + a[1] + (par["flexv"] * a[1] if a[0] == "v" else 0.0)
-                if best is None or f < best[0]:
-                    best = (f, s, a)
-            cand.append((best[1], i, best[2]))
-        s0, _, a0 = min(cand, key=lambda c: (c[0], -pri[c[1]]))
-        s, i, a = max([c for c in cand if c[0] <= s0 + par["delta"] and c[2][0] == a0[0]], key=lambda c: (pri[c[1]], -c[1]))
-        o = ops[i]
-        end = s + a[1] + o["lat"]
-        if a[0] != "n":
-            free[a[0]] = s + a[1]
-        for nm, w, bank in o["lk"]:
-            d = lock.setdefault(nm, {})
-            d[(a[0], w)] = max(d.get((a[0], w), 0.0), end)
-        order.append((i, a, s, end))
-        ready.remove(i)
-        for j in succ[i]:
-            rdy[j] = max(rdy[j], end + HOP)
-            left[j] -= 1
-            if left[j] == 0:
-                ready.append(j)
-    return order
 
 
 PLAN = []
@@ -612,9 +808,9 @@ def rank_program(g, core, T, topo):
     if rank is None:
         return
     if not PLAN:
-        ops = build()
+        ops = build(PARAM, COST)
         PLAN.append(ops)
-        PLAN.append(schedule(ops, PARAM))
+        PLAN.append(schedule(ops, PARAM, COST))
     ops, order = PLAN
     nxt = T.cores[(rank + 1) % len(T.cores)]
     rid, pid = topo.addr(nxt)[0:2]
@@ -625,12 +821,14 @@ def rank_program(g, core, T, topo):
     token = {}
     waited = {}
     hist = {}
-    place = {}
+    place_ = {}
     known = {}
     nd = [0]
 
     def r(a):
-        return T[a[0]][:, a[1]:a[2]:a[3]] if len(a) > 3 else T[a[0]][:, a[1]:a[2]]
+        if len(a) > 4:
+            return T[a[0]][0:a[4], a[1]:a[2]]
+        return T[a[0]][:, a[1]:a[2] - (a[2] - a[1] - 1) % a[3]:a[3]] if len(a) > 3 else T[a[0]][:, a[1]:a[2]]
 
     def wait(e, sem, val):
         if waited.get((e, sem), 0) < val:
@@ -640,7 +838,7 @@ def rank_program(g, core, T, topo):
     for (i, a, _, _) in order:
         o = ops[i]
         e = a[0]
-        place[i] = len(place)
+        place_[i] = len(place_)
         accs = [(x, 0) for x in o["rd"]] + [(x, 1) for x in o["wr"]]
         prev = set(o["dep"])
         for x, w in accs:
@@ -654,7 +852,7 @@ def rank_program(g, core, T, topo):
             token[i] = ("a%d" % a[2], nen)
             count[token[i][0]] = nen
             continue
-        for j in sorted(prev, key=lambda j: -place[j]):
+        for j in sorted(prev, key=lambda j: -place_[j]):
             if token[j] is not None and waited.get((e, token[j][0]), 0) < token[j][1]:
                 wait(e, token[j][0], token[j][1])
                 for sem, val in known.get(j, ()):

@@ -4,32 +4,37 @@ W = 8192
 WD = W + 512
 BF, F32, I32, U16 = "bfloat16", "float32", "int32", "uint16"
 SB = {
-    "X": (W, BF), "A0": (W, BF), "KW": (W, BF), "A": (WD, F32), "D1": (WD, F32),
-    "D0": (2048, BF), "ZW1": (3072, BF), "ZW2": (3072, BF), "Z1": (1024, BF), "Z2": (1024, BF),
+    "X": (W, BF), "A0": (WD, BF), "KW": (W, BF), "A": (WD, F32), "D1": (WD, F32),
+    "D0": (2048, BF), "ZW1": (3072, BF), "ZW2": (3072, BF), "Z1": (2048, BF),
     "NS": (512, I32), "KD": (512, I32), "NH": (512, BF), "NM": (512, BF),
-    "NHF": (512, F32), "NLF": (512, F32), "DN1": (512, F32), "DN2": (512, F32),
-    "RN": (192, I32), "EO": (512, F32), "IF": (512, F32), "ZN": (256, F32),
-    "IB": (128 * 6, BF), "ZS": (16 * 144, BF), "ZP": (7 * 144, BF), "ONE": (256, BF), "CR": (64 * 8 + 352 + 160 + 256, BF),
-    "PI": (2, I32), "PF": (12, F32), "ST": (32 * 8, F32),
+    "NHF": (512, F32), "NLF": (512, F32), "DN2": (512, F32),
+    "RN": (192, I32), "WT": (1024, F32), "TB": (256, F32), "IF": (512, F32), "ZN": (768, BF),
+    "IB": (128 * 9, BF), "CE": (2 * 384, BF), "LT": (1024, BF), "ZS": (16 * 144, BF), "ZP": (7 * 144, BF), "ONE": (256, BF),
+    "CR": (64 * 7 + 160 + 256 + 128, BF),
+    "PI": (2, I32), "PF": (12, F32), "ST": (32 * 5, F32),
     "K0": (386, F32), "K1": (386, F32), "K2": (450, F32), "K3": (450, F32), "SC0": (1120, F32), "SC1": (896, F32),
-    "U": (8 * 384, U16), "R": (64, F32), "RU": (64, U16), "NI": (128, F32),
+    "U": (4 * 384, U16), "R": (192, F32), "RU": (64, U16),
     "GS": (4096, BF), "CM": (4096, BF), "OV": (192, BF), "SP": (96, BF),
-    "MN": (320, I32), "WN": (320, I32), "E": (128, F32), "EM": (64, BF), "TM": (256, F32), "NE": (384, F32),
+    "MN": (320, I32), "E": (128, F32), "EM": (64, BF), "TM": (256, F32), "NE": (384, F32),
     "FS": (128, U16), "FO": (128, U16), "UB": (320, U16), "G1": (512, BF), "G2": (512, BF), "GR": (512, BF),
     "PT": (128, F32), "LO": (96, U16), "LW": (1536, BF), "LI": (128, F32),
     "RW": (1536, F32), "WS": (2048, F32),
-    "Q": (32 * 10, F32), "QO": (64, U16), "GX": (512, BF), "CK": (512, BF), "H5": (160, BF), "L5": (160, BF),
-    "HP": (128, BF), "LP": (128, BF), "LV": (64, F32),
+    "Q": (32 * 9, F32), "QO": (64, U16), "GX": (512, BF), "H5": (160, BF), "L5": (160, BF),
+    "LV": (64, BF),
 }
 SCRATCH = {k: ("sbuf", [128, v[0]], v[1]) for k, v in SB.items()}
 for _i in range(8):
     SCRATCH["P%d" % _i] = ("psum", [128, 512], "float32")
-SEMAPHORES = ["ev", "es", "et", "eg", "sent"] + ["d%d" % i for i in range(40)] + ["a%d" % i for i in range(6)]
+SEMAPHORES = ["ev", "es", "et", "eg"] + ["d%d" % i for i in range(40)] + [s + str(i) for s in "al" for i in range(6)]
 
-COST = {"cy": 0.85, "pe": 0.43, "ga": 1.4, "sc": 3.3, "hop": 80.0, "dma": 2000.0, "bw": 200.0, "mm": 0.0}
-PARAM = {"flexv": 2.0, "flex0": 0.0, "xl": 13000.0, "iters": 10, "moves": 12000, "noise": 300.0, "seed": 5, "split": 0, "last": "ssss",
-         "fill": 10, "kwv": 3, "kwd": 1, "pair": 1, "roots": 1,
-         "boost": [5e5] + [0.0] * 21 + [1e5, 0.0, 0.0, 0.0]}
+COST = {"cy": 0.85, "pe": 0.43, "ga": 1.4, "sc": 3.3, "hop": 80.0, "dma": 1300.0, "bw": 380.0, "call": 700.0, "once": 3500.0,
+        "mm": 0.0, "row": 3.0, "f": 1.0}
+SLOW = dict(COST, ga=1.6, sc=3.8, f=1.2, hop=160.0, dma=1700.0, bw=280.0, row=6.0, call=1200.0, once=6000.0)
+PARAM = {"head": 10000.0, "pull": 0.01, "seed": 5, "last": "ss",
+         "dup": 1, "fill": 7, "kw": [5, 7, 6], "cut": [0, 0], "half": [0, 0, 0, 0, 1, 0],
+         "search": [(20000, 500.0, 0.3, 2.0, (1.0, 0.0), 0.0, 0.4), (100000, 900.0, 0.3, 0.3, (1.0, 0.0), 0.0, 1.0),
+                    (15000, 500.0, 0.1, 0.05, (0.6, 0.45), 0.55, 1.0), (45000, 450.0, 0.1, 0.05, (0.6, 0.45), 0.0, 1.0),
+                    (30000, 400.0, 0.05, 0.03, (0.6, 0.45), 0.2, 0.65), (35000, 400.0, 0.05, 0.03, (0.6, 0.45), 0.6, 1.0)]}
 KEY = 2.0 ** -20
 WT = [(5 - k) * 65536.0 for k in range(7)]
 MAGIC = 1.5 * 2 ** 23
@@ -46,6 +51,10 @@ def isps(a):
     return a[0][0] == "P" and a[0][1:].isdigit()
 
 
+def window(a):
+    return a[0] in ("A", "D1") or a == ("A0", 0, WD)
+
+
 def build(par, c):
     ops = []
     acc = {}
@@ -55,11 +64,18 @@ def build(par, c):
     def sz(a):
         return (a[2] - a[1] + (a[3] if len(a) > 3 else 1) - 1) // (a[3] if len(a) > 3 else 1)
 
-    def add(alts, rd, wr, after=(), lat=0.0, kind="c", pri=0.0):
-        o = {"n": len(ops), "alts": alts, "rd": rd, "wr": wr, "lat": lat, "kind": kind, "pri": pri, "tag": tag[0]}
+    def add(alts, rd, wr, after=(), lat=0.0, kind="c", pri=0.0, drop=0, move=0.0):
+        if drop:
+            del ops[-drop:]
+            for lst in acc.values():
+                while lst and lst[-1][0] >= len(ops):
+                    lst.pop()
+        else:
+            alts = [(e, d * (c["f"] if kind == "c" else 1.0), em) for e, d, em in alts]
+        o = {"n": len(ops), "alts": alts, "rd": rd, "wr": wr, "lat": lat, "move": move, "kind": kind, "pri": pri, "tag": tag[0]}
         dep = set(x["n"] for x in after)
         for a, w in [(a, 0) for a in rd] + [(a, 1) for a in wr]:
-            if a[0] in ("A", "D1"):
+            if window(a):
                 continue
             for (n, a2, w2) in acc.get(a[0], ()):
                 if (w or w2) and meet(a, a2):
@@ -108,12 +124,9 @@ def build(par, c):
 
     def flex(out, a, bias=0.0, engs="sv", scale=1.0):
         n = sz(out)
-        alts = []
-        if "s" in engs:
-            alts.append(("s", 15.0 + vc(n), lambda q, T, r: [q.activation(r(out), r(a), AF.Identity, bias=val(r, bias), scale=val(r, scale))]))
-        if "v" in engs:
-            alts.append(("v", vc(n), lambda q, T, r: [q.tensor_scalar(r(out), r(a), val(r, scale), val(r, bias), OP.mult, OP.add)]))
-        return add(alts, [a] + cols(bias, scale), [out])
+        alts = {"s": ("s", 15.0 + vc(n), lambda q, T, r: [q.activation(r(out), r(a), AF.Identity, bias=val(r, bias), scale=val(r, scale))]),
+                "v": ("v", vc(n), lambda q, T, r: [q.tensor_scalar(r(out), r(a), val(r, scale), val(r, bias), OP.mult, OP.add)])}
+        return add([alts[e] for e in engs], [a] + cols(bias, scale), [out])
 
     def gat(out, win, off, engs="sv", after=(), scale=None, bias=0.0):
         n = sz(out)
@@ -131,20 +144,18 @@ def build(par, c):
                    [("X", 0, W), off, z], [out])
 
     def scat(win, off, src, eng, after=(), src2=None):
+        em = {"s": lambda q, T, r: [q.activation(r(win).indirect(r(off)), r(src), AF.Silu)],
+              "v": lambda q, T, r: [q.tensor_copy(r(win).indirect(r(off)), r(src))]}
         if src2 is not None:
-            em = lambda q, T, r: [q.tensor_tensor(r(win).indirect(r(off)), r(src), r(src2), OP.add)]
-        elif eng == "s":
-            em = lambda q, T, r: [q.activation(r(win).indirect(r(off)), r(src), AF.Silu)]
-        else:
-            em = lambda q, T, r: [q.tensor_copy(r(win).indirect(r(off)), r(src))]
-        return add([(eng, 60.0 + sz(src) * SC * CY, em)], [off, src] + cols(src2), [win], after)
+            em["v"] = lambda q, T, r: [q.tensor_tensor(r(win).indirect(r(off)), r(src), r(src2), OP.add)]
+        return add([(e, 60.0 + sz(src) * SC * CY, em[e]) for e in ("sv" if eng == "s" else "v")], [off, src] + cols(src2), [win], after)
 
     def pe(groups, first=True, last=True, hold=None):
         cost, rd, wr = 60.0, [], [(hold, 0, 512)] if hold else []
         for grp in groups:
             for (o, l, x) in grp:
                 cost += max(64, sz(x)) * PCY * (4 if SB[x[0]][1] == F32 else 1) + c["mm"]
-                for lst, a in ((rd, l), (rd, x if x[0][0] == "K" else x[:3]), (wr, o)):
+                for lst, a in ((rd, l), (rd, x if x[0][0] == "K" else x[:3]), (wr, o[:4])):
                     if a not in lst:
                         lst.append(a)
 
@@ -157,21 +168,42 @@ def build(par, c):
         return add([("t", cost, em)], rd, wr)
 
     def gp(n, em, rd, wr, pri=0.0, after=()):
-        return add([("g", 170.0 + 2 * n * CY, em)], rd, wr, after, pri=pri)
+        return add([("g", 200.0 + 2.3 * n * CY, em)], rd, wr, after, pri=pri)
 
     def iota(a, pat, base, cm, pri=0.0):
         return gp(sz(a), lambda q, T, r: [q.iota(r(a), pat, base, cm, allow_small_or_imprecise_dtypes=True)], [], [a], pri)
 
+    def fill(a, v=0, engs="sv", pri=0.0):
+        n, z = sz(a), ("ZN", 0, sz(a), 1) + a[4:]
+        alts = {"s": ("s", 15.0 + vc(n), lambda q, T, r: [q.activation(r(a), r(z), AF.Identity, bias=float(v), scale=1.0)]),
+                "v": ("v", vc(n * (0.5 if two(a) else 1)), lambda q, T, r: [q.memset(r(a), float(v))]),
+                "g": ("g", 160.0 + 2.3 * n * CY, lambda q, T, r: [q.iota(r(a), [[0, n]], int(v), 0, allow_small_or_imprecise_dtypes=True)])}
+        return add([alts[e] for e in engs], [z[:3]], [a], pri=pri)
+
     def zero(a, v=0):
-        return iota(a, [[0, sz(a)]], v, 0)
+        return fill(a, v, "gs")
 
-    def dma(pairs, rd, wr, nbytes, after=(), q="y", pri=0.0):
+    def copy(out, a):
+        return gp(sz(a), lambda q, T, r: [q.affine_select(r(out), r(a), [[0, sz(a)]], OP.is_ge, 0.0, 0, 0)], [a], [out])
+
+    def either(a, b):
+        return add(copy(a, b)["alts"] + flex(a, b)["alts"], [b], [a], drop=2)
+
+    def reset(h):
+        return either(("LW", h, 1024, 2), ("LT", h, 1024, 2))
+
+    def named(nm, *calls):
+        for o in calls:
+            o["nm"] = nm
+        return list(calls)
+
+    def dma(pairs, rd, wr, nbytes, after=(), q="y", pri=0.0, rows=128):
         return add([(q, 100.0 * len(pairs), lambda e, T, r: [e.dma_start(a(T), b(T)) for a, b in pairs])], rd, wr, after,
-                   lat=c["dma"] + nbytes / c["bw"], kind="d", pri=pri)
+                   lat=c["dma"], move=nbytes / c["bw"] + rows * len(pairs) * c["row"], kind="d", pri=pri)
 
-    def send(src, dst, k):
-        s = add([("g", 300.0, (src, dst, k))], [src], [], kind="s")
-        return add([("n", 0.0, k)], [], [dst], [s], lat=200.0 + c["dma"] + sz(src) * 256 / c["bw"], kind="r")
+    def send(src, dst, k, after=()):
+        s = add([("g", c["call"] + c["once"] * (k == 0), (src, dst, k))], [src], [], after, kind="s")
+        return add([("n", 0.0, k)], [], [dst], [s], lat=500.0 + c["dma"], move=sz(src) * 256 / c["bw"] + 128 * c["row"], kind="r")
 
     def sel(buf, base, r):
         return (buf, base + 15 - r, base + 143 - r)
@@ -195,12 +227,12 @@ def build(par, c):
     IBM = lambda i: ("IB", 128 * i, 128 * i + 128)
     IP, IN, KP, KN = [("IF", 128 * i, 128 * i + 128) for i in range(4)]
     DUM, LDUM, UF = b32("ST", 0, 2), b32("ST", 2), b32("ST", 3)
-    LN = [b32("ST", 4), b32("ST", 5)]
     PC = lambda i: ("PF", i, i + 1)
     BA, M1, M2, B2 = PC(1), PC(2), PC(3), PC(4)
-    CE, CV, CG = ("CR", 512, 864), ("CR", 864, 1024), ("CR", 1024, 1280)
+    CV, CG, CW, CQ = ("CR", 448, 608), ("CR", 608, 864), ("CR", 864, 992), ("CR", 928, 992)
     NE = lambda h, i, n=1: b32("NE", 6 * h + i, n)
-    R = lambda h: b32("R", h)
+    SR = lambda h, n=1: b32("R", 3 * h, n)
+    R = lambda h, n=1: b32("R", 3 * h + 1, n)
     EM = lambda h: b32("EM", h)
     UW = lambda h, i, n=1: b32("UB", 5 * h + i, n)
 
@@ -212,25 +244,31 @@ def build(par, c):
         return ("K%d" % (h + (2 if t == 2 else 0)), o, o + 64 * blk(t) - blk(t) + 1, blk(t))
 
     def Uu(t, h, k):
-        o = (2 * t + h) * 384 + 64 * (2 if k == 0 else k - 1 if k < 3 else k)
+        o = (2 * (t % 2) + h) * 384 + 64 * (2 if k == 0 else k - 1 if k < 3 else k)
         return ("U", o, o + 64)
 
-    def key(t, h, k, src, out=None):
-        return flex(out or Kk(t, h, k), src, WT[k] * KEY, "sv", KEY)
+    def key(t, h, k, src, out=None, less=0.0):
+        return flex(out or Kk(t, h, k), src, (WT[k] + less) * KEY, "sv", KEY)
+
+    def spare(t, h):
+        return t > 0 or h == 1
+
+    def Uw(t, h):
+        return Uu(t + 1, h, 0 if spare(t, h) else 1)
 
     dma([(lambda T: T.NS[:], lambda T: T.nsum[:])], [], [("NS", 0, 512)], 262144, pri=9.5e5)
     dma([(lambda T: T.RN[:, 0:64], lambda T: T.rho[:]), (lambda T: T.RN[:, 64:192], lambda T: T.nei[:])], [], [("RN", 0, 192)], 98304, q="s", pri=9e5)
-    lx = dma([(lambda T: T.X[:], lambda T: T.x[:])], [], [("X", 0, W)], 2400000, pri=8e5)
-    ld = dma([(lambda T, i=i: T.D0[:, 1024 * i:1024 * i + 1024], lambda T: T.dem[:, 0:1024]) for i in range(2)], [], [("D0", 0, 2048)], 600000, q="s", pri=8e5)
-    dma([(lambda T: T.KD[:], lambda T: T.kid[:])], [], [("KD", 0, 512)], 800000, q="s", pri=7e5)
-    ms(("ZN", 0, 256), 0.0, 9e5)
+    dma([(lambda T: T.D0[:, 0:1024], lambda T: T.dem[:, 0:1024])], [], [("D0", 0, 1024)], 262144, pri=8.5e5)
+    dma([(lambda T: T.X[:, 0:2560], lambda T: T.x[:, 0:2560])], [], [("X", 0, 2560)], 655360, pri=8e5)
+    for i in range(4):
+        ops[i]["turn"] = i
+    dma([(lambda T: T.X[:, 2560:W], lambda T: T.x[:, 2560:W])], [], [("X", 2560, W)], 1441792, pri=8e5)["turn"] = 3.6
+    dma([(lambda T: T.D0[:, 1024:2048], lambda T: T.dem[:, 0:1024])], [], [("D0", 1024, 2048)], 262144)["turn"] = 3.7
+    ms(("ZN", 0, 768), 0.0, 9e5)
     ms(("ONE", 0, 128), 1.0, 9e5)
     ms(("ZP", 0, 1008), 0.0, 9e5)
-    nv = par["fill"]
-    for i in range(0, nv, 2):
-        ms(("A0", 512 * i, 512 * i + 1024), 32768.0, 5e5)
-    for i in range(2 * nv, 32):
-        flex(("A0", 256 * i, 256 * i + 256), ("ZN", 0, 256), 32768.0, "s")["pri"] = 5e5
+    for i in range(16):
+        fill(("A0", 512 * i, 512 * i + 512), 32768, "vs" if i < par["fill"] else "sv", 7.5e5)
 
     def diag(out, src, pat, fill, base, cm=1):
         return gp(sz(out), lambda q, T, r: [q.affine_select(r(out), r(src), pat, OP.not_equal, fill, base, cm)], [src], [out])
@@ -238,75 +276,87 @@ def build(par, c):
     def band(out, src, pat, base, cm):
         return gp(sz(out), lambda q, T, r: [q.affine_select(r(out), r(src), pat, OP.is_ge, 0.0, base, cm)], [src], [out])
 
-    ts(("NH", 0, 512), ("NS", 0, 512), 64.0, None, OP.add)["pri"] = 6e5
-    tt(("CK", 0, 512), ("NS", 0, 512), ("NH", 0, 512), OP.subtract)["pri"] = 6e5
-    flex(("NM", 0, 512), ("CK", 0, 512), 128.0)["pri"] = 6e5
-    wa = dma([(lambda T: T.A0[0:128:16, :], lambda T: T.NH[:]), (lambda T: T.A0[1:128:16, :], lambda T: T.NM[:])],
-             [("NH", 0, 512), ("NM", 0, 512)], [("A0", 0, W)], 262144, pri=6e5)
-    late_loads = [lx, ld, wa]
-
     z128 = ("ZN", 0, 128)
+    diag(IP, z128, [[-1, 128]], 1.0, 0)
+    diag(IBM(8), z128, [[-1, 128]], -1.0, 0)
+    ts(("NH", 0, 512), ("NS", 0, 512), 64.0, None, OP.add)["pri"] = 6e5
+    tt(("NM", 0, 512), ("NS", 0, 512), ("NH", 0, 512), OP.subtract)["pri"] = 6e5
+    gp(1, lambda q, T, r: [q.iota(r(("PI", 0, 1)), [[0, 1]], 0, 1)], [], [("PI", 0, 1)])
+    ts(("PI", 1, 2), ("PI", 0, 1), 15, None, OP.bitwise_and)
+    cp(PC(0), ("PI", 1, 2))
+    ts(PC(5), PC(0), 1.0, 128.0, OP.is_equal, OP.mult)
+    ts(PC(11), PC(0), 2.0, 32768.0, OP.is_equal, OP.mult)
+    flex(BA, PC(5), PC(11))
+    for i in range(3):
+        fill(("ZS", 768 * i, 768 * i + 768), 0, "vgs")
+    zs = ("ZS", 15, 2304, 16)
+    diag(zs, zs, [[-1, 16], [-16, 9]], 1.0, 0)
+    flex(("NM", 0, 512), ("NM", 0, 512), 128.0)["pri"] = 7e5
+    dma([(lambda T: T.A0[0:128:16, 0:W], lambda T: T.NH[:]), (lambda T: T.A0[1:128:16, 0:W], lambda T: T.NM[:])],
+        [("NH", 0, 512), ("NM", 0, 512)], [("A0", 0, W)], 262144, pri=6e5)["turn"] = 3.5
+
     for h in range(2):
         for b in range(2):
-            diag(("DN2", 128 * (2 * h + b), 128 * (2 * h + b + 1)), z128, [[-16, 8], [1024, 2], [-2, 8]], 1.0, -h - 1024 * b)
-    diag(IP, z128, [[-1, 128]], 1.0, 0)
+            diag(("DN2", 128 * (2 * h + b), 128 * (2 * h + b + 1)), z128, [[-16, 8], [1024, 2], [-2, 8]], 1.0, -h - 1024 * b)["pri"] = 6.5e5
     zp6, zp0, zpa = ("ZP", 15, 864, 16), ("ZP", 15, 144, 16), ("ZP", 879, 1008, 16)
     band(zp6, ("ONE", 0, 54), [[-2, 6], [-16, 9]], 0, 1)
     band(zp6, zp6, [[2, 6], [16, 9]], 1, -1)
     diag(zp0, zp0, [[-16, 9]], -2.0 ** -8, -2)
+    for i, row, s in ((2, 10, -BIG), (4, 10, -BIG), (1, 1, 1.0)):
+        a = ("ZP", 144 * i + 15, 144 * i + 144, 16)
+        diag(a, a, [[-16, 9]], s, -row)
     ms(("EM", 0, 9), 2.0)
     band(zpa, ("EM", 0, 9), [[-16, 9]], 0, 1)
     band(zpa, zpa, [[16, 9]], 15, -1)
     for i, s in ((1, -1.0), (2, 1 / KEY), (3, -1 / KEY)):
-        flex(("IF", 128 * i, 128 * i + 128), IP, 0.0, "s", s)
-    for i, s in enumerate((-64.0, -BIG, BIG, -4096.0, -1024.0)):
-        flex(IBM(i), IP, 0.0, "s", s)
-    flex(("IB", 640 + 16, 768), ("IF", 0, 112), 0.0, "s", -2048.0)
-    flex(("IB", 640, 640 + 16), ("IF", 112, 128), 0.0, "s", -2048.0)
-    ms(("ONE", 128, 256), 65536.0)
+        flex(("IF", 128 * i, 128 * i + 128), IP, 0.0, "sv", s)
+    for i, s in ((1, -BIG), (2, BIG), (4, -1024.0), (6, -8 * 65536.0), (7, 1.0)):
+        flex(IBM(i), IP, 0.0, "sv", s)
+    flex(("IB", 640 + 16, 768), ("IF", 0, 112), 0.0, "sv", -2048.0)
+    flex(("IB", 640, 640 + 16), ("IF", 112, 128), 0.0, "sv", -2048.0)
+    fill(("ONE", 128, 256, 1, 1), 65536, "gsv")
     iota(("CR", 0, 256), [[-1, 4], [0, 64]], 4, 0)
     iota(("CR", 256, 448), [[16, 3], [0, 64]], -17, 0)
-    iota(("CR", 512, 768), [[0, 2], [1, 2], [0, 64]], -4, 0)
-    ms(("CR", 768, 992), 0.0)
-    ms(("CR", 992, 1024), -128.0 / 65536.0)
-    iota(CG, [[0, 256]], int(MAGIC) // 65536, 0)
+    fill(("CR", 448, 576, 1, 1), 0, "gsv")
+    fill(("CR", 576, 608, 1, 1), -128.0 / 65536.0)
+    fill(("CR", 864, 928, 1, 1), 0, "gsv")
+    fill(CQ + (1, 1), 0.25)
+    for o, n_, v in ((0, 128, 0.25), (128, 64, -4.0), (192, 64, -3.0), (256, 64, 0.0), (352, 32, 0.4375),
+                     (384, 64, 0.25), (448, 64, -1 / 64), (512, 64, -4.0), (576, 64, 1.0), (640, 96, 0.0), (736, 32, 0.4375)):
+        fill(("CE", o, o + n_, 1, 1), v)
+    fill(CG + (1, 1), int(MAGIC) // 65536, "gsv")
     for h in range(2):
-        ms(("K%d" % h, 0, 386, 385), 0.0)
-        ms(("K%d" % (2 + h), 0, 450, 7), 0.0)
-        ms(("K%d" % (2 + h), 1, 450, 7), WT[6] * KEY)
-    gp(1, lambda q, T, r: [q.iota(r(("PI", 0, 1)), [[0, 1]], 0, 1)], [], [("PI", 0, 1)])
-    iota(b32("ST", 6), [[16, 32]], 0, 0)
-    ts(("PI", 1, 2), ("PI", 0, 1), 15, None, OP.bitwise_and)
-    cp(PC(0), ("PI", 1, 2))
-    ts(PC(5), PC(0), 1.0, 128.0, OP.is_equal, OP.mult)
-    ts(PC(6), PC(0), 2.0, 32768.0, OP.is_ge, OP.mult)
-    ts(PC(7), PC(0), 4.0, -32768.0, OP.is_ge, OP.mult)
-    ts(BA, PC(5), PC(6), PC(7), OP.add, OP.add)
+        fill(("K%d" % h, 0, 386, 385), 0, "gsv")
+        fill(("K%d" % (2 + h), 0, 450, 7), 0, "gsv")
+        fill(("K%d" % (2 + h), 1, 450, 7), WT[6] * KEY)
+    iota(b32("ST", 4), [[16, 32]], 0, 0)
     ts(M1, PC(0), 6.0, None, OP.is_lt)
     ts(PC(9), PC(0), 6.0, None, OP.is_ge)
     ts(M2, PC(0), 10.0, PC(9), OP.is_lt, OP.mult)
     ts(B2, PC(0), 10.0, -1.0, OP.is_equal, OP.mult)
     ts(PC(8), ("PI", 0, 1), PC(0), -512.0, OP.subtract, OP.mult)
-    ts(UF, b32("ST", 6), PC(0), None, OP.add)
-    for s in range(2):
-        ts(sub(DUM, s), UF, float(W), None, OP.add)
-    ts(LDUM, UF, 1024.0 - 4096.0, None, OP.add)
+    flex(UF, b32("ST", 4), PC(0))
+    flex(("CE", 320, 352, 1, 1), b32("ST", 4) + (1, 1), 0.0, "sv", 1 / 32768)
     for h in range(2):
-        ts(LN[h], UF, 2.0, float(h + 1024 * (h + 1)), OP.mult, OP.add)
+        flex(PC(6 + h), PC(0), float(h + 1024 * (h + 1)), "sv", 2.0)
+    for s in range(2):
+        flex(sub(DUM, s), UF, float(W))
+    flex(LDUM, UF, 1024.0 - BIG)
+    iota(PC(10), [[0, 1]], 1, 0)
+    gp(1, lambda q, T, r: [q.affine_select(r(PC(10)), r(PC(10)), [[0, 1]], OP.is_ge, -1.0, 31, -1)], [PC(10)], [PC(10)])
 
-    cp(("TM", 0, 192), ("RN", 0, 192))
+    cp(("TM", 0, 192), ("RN", 0, 192))["pri"] = 6.5e5
     for h in range(2):
         bk = "P%d" % (4 + h)
-        pe([[((bk, 0, 96), ("DN2", 128 * (2 * h + b), 128 * (2 * h + b + 1)), ("TM", b, 192, 2)) for b in range(2)]])
-        cp(Uu(0, h, 1), (bk, 32, 96))
-        key(0, h, 1, (bk, 32, 96))
-        flex(R(h), (bk, 0, 32))
-        flex(b32("NI", 2 * h, 2), (bk, 32, 96))
-    cp(("RU", 0, 64), ("R", 0, 64))
-    for h in range(2):
-        for s in range(2):
-            key(2, h, 0, R(h), sub(Kk(2, h, 0), s))
-    send(("D0", 0, 1024), ("ZW1", 1024, 2048), 0)
+        mv = lambda o, a, n: [((bk, o, o + n), ("DN2", 128 * (2 * h + b), 128 * (2 * h + b + 1)), ("TM", a + b, a + 2 * n, 2)) for b in range(2)]
+        pe([mv(64, 0, 96)])["pri"] = 6.5e5
+        pe([mv(32, 0, 32), mv(0, 64, 32) + mv(0, 128, 32)])
+        cp(Uu(0, h, 1), (bk, 96, 160))
+        key(0, h, 1, (bk, 96, 160))
+        flex(SR(h, 3), (bk, 0, 96))
+        cp(b32("RU", h), R(h))
+        key(2, h, 0, R(h, 2))
+    send(("D0", 0, 1024), ("ZW1", 1024, 2048), 0)["turn"] = 8
 
     def rotate(z):
         dma([(lambda T: T[z][16:128, 2048:3072], lambda T: T[z][0:112, 1024:2048]), (lambda T: T[z][0:16, 2048:3072], lambda T: T[z][112:128, 1024:2048])],
@@ -314,45 +364,48 @@ def build(par, c):
     rotate("ZW1")
 
     tag[0] = 22
-    if par["kwd"]:
-        dma([(lambda T, i=i: T.KW[i:128:16, :], lambda T, i=i: T.A0[i:128:16, :]) for i in (0, 1, 10, 11, 12, 13, 14, 15)],
-            [("A0", 0, W)], [("KW", 0, 1)], 1048576, late_loads)
-    for i in range(0 if par["kwd"] else par["kwv"]):
-        ms(("KW", 1024 * i, 1024 * i + 1024), 0.0)
-    for i in range(16 if par["kwd"] else 2 * par["kwv"], 16):
-        flex(("KW", 512 * i, 512 * i + 512), ("ZP", 0, 512), 0.0, "s", 0.0)
-    ts(("KD", 0, 512), ("KD", 0, 512), 2047, None, OP.bitwise_and)
-    cp(("G1", 0, 512), ("KD", 0, 512))
-    tt(("G2", 0, 512), ("KD", 0, 512), ("G1", 0, 512), OP.subtract)
-    iota(("NHF", 0, 512), [[32, 16], [0, 32]], 0, 512)
-    flex(("GR", 0, 512), ("NHF", 0, 512), PC(8))
+    dma([(lambda T: T.KD[:], lambda T: T.kid[:])], [], [("KD", 0, 512)], 262144)["turn"] = 4
+    cp(("WS", 0, 512), ("KD", 0, 512))
+    flex(("G1", 0, 512), ("WS", 0, 512))
+    pe([[(("P7", 0, 512), IP, ("WS", 0, 512)), (("P7", 0, 512), IBM(8), ("G1", 0, 512))]])
+    flex(("G2", 0, 512), ("P7", 0, 512))
+    add([("s", 15.0 + vc(512), lambda q, T, r: [q.activation(T.LW[:, 1024:1536], T.WS[:, 0:512], AF.Relu, bias=0.0, scale=-2048.0)])],
+        [("WS", 0, 512)], [("LW", 1024, 1536)])
+    iota(("WS", 512, 1024), [[32, 16], [0, 32]], 0, 512)
+    flex(("GR", 0, 512), ("WS", 512, 1024), PC(8))
     iota(("GX", 0, 512), [[0, 16], [1, 32]], 0, 0)
-    rows = [(2, "G1"), (3, "G2"), (4, "GR"), (5, "GX"), (8, "GR"), (9, "GX"), (6, "NH"), (7, "NM")]
-    dma([(lambda T, i=i: T.KW[i:128:16, :], lambda T, n=n: T[n][:]) for i, n in rows], [(n, 0, 512) for _, n in rows],
-        [("KW", par["kwd"], W)], 1048576 * (1 + par["kwd"]), late_loads)
-    dma([(lambda T: T.ZW1[:, 0:1024], lambda T: T.dem[:, 1024:2048]), (lambda T: T.ZW2[:, 0:1024], lambda T: T.dem[:, 2048:3072])],
-        [], [("ZW1", 0, 1024), ("ZW2", 0, 1024)], 1500000, late_loads)
-    for i in range(2):
-        ms(("ZS", 1152 * i, 1152 * i + 1152), 0.0)
-    zs = ("ZS", 15, 2304, 16)
-    diag(zs, zs, [[-1, 16], [-16, 9]], 1.0, 0)
-    zero(("LW", 0, 1024))
+    dma([(lambda T, i=i: T.KW[i:128:16, :], lambda T, j=j: T.A0[j:128:16, 0:W]) for i, j in ((6, 0), (7, 1), (0, 2), (11, 3), (12, 4), (13, 5), (14, 6), (15, 7))],
+        [("A0", 0, W)], [("KW", 2, 3)], 1048576, rows=16)["turn"] = par["kw"][2]
+    for j, rows in enumerate(([(4, "GR", 0), (5, "GX", 0), (8, "GR", 0), (9, "GX", 0), (10, "ZN", 0)], [(1, "LW", 1024), (2, "G1", 0), (3, "G2", 0)])):
+        dma([(lambda T, i=i: T.KW[i:128:16, :], lambda T, n=n, o=o: T[n][:, o:o + 512]) for i, n, o in rows], [(n, o, o + 512) for _, n, o in rows],
+            [("KW", j, j + 1)], 131072 * len(rows))["turn"] = par["kw"][j]
+    for i in (1, 2):
+        dma([(lambda T, i=i: T["ZW%d" % i][:, 0:1024], lambda T, i=i: T.dem[:, 1024 * i:1024 * i + 1024])], [], [("ZW%d" % i, 0, 1024)], 262144)["turn"] = 8 + i
+    hh, ll = b32("H5", 0, 2), b32("L5", 0, 2)
+    flex(hh, ("TM", 0, 64))
+    tt(ll, ("TM", 0, 64), hh, OP.subtract)
+    for b in range(2):
+        bk = "P%d" % (2 + b)
+        for j in range(0, 8, 4):
+            pe([[((bk, i, 512, 8), sel("ZS", 144 * (2 * i + b), row), a) for a, row in ((hh, 4), (ll, 5), (hh, 8), (ll, 9))] for i in range(j, j + 4)])
+        flex(("LT", b, 1024, 2), (bk, 0, 512))
+    reset(1)
     tag[0] = 24
-    ia = []
-    for i in range(8):
-        a, b = ("A", 1024 * i, 1024 * i + 1024), ("A0", 1024 * i, 1024 * i + 1024)
-        ia.append(gp(1024, lambda q, T, r, a=a, b=b: [q.affine_select(r(a), r(b), [[0, 1024]], OP.is_ge, 0.0, 0, 0)], [b], [a]))
+    ia = [either(("A", 512 * i, 512 * i + 512), ("A0", 512 * i, 512 * i + 512)) for i in range(16)]
     for i in range(3):
         zero(("RW", 512 * i, 512 * i + 512))
     tag[0] = 23
-    zero(("DN1", 0, 512), -int(MAGIC) - 32896)
-    idl = dma([(lambda T: T.D1[0:128:16, 0:W], lambda T: T.DN1[:])], [("DN1", 0, 512)], [("D1", 0, W)], 262144, late_loads)
-    for h in range(2):
-        diag(("EO", 256 * h, 256 * h + 256), ("ZN", 0, 256), [[-16, 8], [-1, 16], [1024, 2]], 1.0, -1024 * h)
+    zero(("NLF", 0, 512), 32768)
+    idl = dma([(lambda T: T.D1[0:128:16, 0:W], lambda T: T.NLF[:])], [("NLF", 0, 512)], [("D1", 0, W)], 262144)
+    zero(("WT", 0, 768), 32768)
+    add([("s", 1400.0 + vc(256), lambda q, T, r: [q.activation(T.WT[:, 768:1024], T.ZN[:, 0:256], AF.Silu, bias=32768.0, scale=1.0)])],
+        [("ZN", 0, 256)], [("WT", 768, 1024)], pri=6e5)
+    zero(("TB", 0, 64), 64)
+    dma([(lambda T: T.WT[1:128:16, :], lambda T: T.TB[:, 0:64])], [("TB", 0, 64)], [("WT", 0, 1024)], 32768)
 
-    turn = [0, 0]
+    turn, staged = [0, 0], []
 
-    def write(lists, off, engs, after, stage=None, banks=None):
+    def write(nm, lists, off, win, after, stage=None, banks=None, behind=()):
         n = sz(lists[0][0]) // 32
         if stage is None:
             turn[1] ^= 1
@@ -364,22 +417,26 @@ def build(par, c):
             grp = [[((bk, i, 512, len(rs)), sel("ZS", 144 * r, row), a) for a, row in lists] for i, r in enumerate(rs)]
             per = 16 // len(lists)
             for i in range(0, len(grp), per):
-                pe(grp[i:i + per])
-            flex(stage if n == 1 else (stage[0], stage[1] + b, stage[2], 2), (bk, 0, 512), BA if engs[0] == "s" else -MAGIC - 32896.0)
-        return [scat(("A" if engs[0] == "s" else "D1", 0, WD), sub(off, b), stage if n == 1 else sub(stage, 16 * b, 16), engs[0], after) for b in range(n)]
+                staged.append(pe(grp[i:i + per]))
+                staged[-1]["dep"].update(x["n"] for x in behind)
+            named("s" + nm, flex(stage if n == 1 else (stage[0], stage[1] + b, stage[2], 2), (bk, 0, 512), {"A": BA, "D1": 32768.0, "A0": 0.0}[win]))
+        return [named("a%s%d" % (nm, b), scat((win, 0, WD), sub(off, b), stage if n == 1 else sub(stage, 16 * b, 16), "v" if win == "A0" else "s", after))[0]
+                for b in range(n)]
 
-    def pairs(hh, ll, rows, off, eng, after, banks=None):
-        if par["pair"] and sz(hh) == 64:
-            return write([(hh, rows[0]), (ll, rows[1])], off, eng, after, None, banks)
-        return [x for s in range(sz(hh) // 32) for x in write([(sub(hh, s), rows[0]), (sub(ll, s), rows[1])], sub(off, s), eng, after)]
+    def turned(terms, n, bias, scale, stage, row, bk):
+        o, tb = (bk, 0, 128, 1, n), ("TB", 128, 256, 1, n)
+        pe([[((bk, 0, 128, 1, sz(a)), a, m) for a, m in terms]])
+        flex(tb, o, bias, "sv", scale)
+        return dma([(lambda T, g_=g_: T[stage][16 * g_ + row, 0:16 * n], lambda T, g_=g_: T.TB[0:n, 128 + 16 * g_:144 + 16 * g_]) for g_ in range(8)],
+                   [tb], [(stage, 0, 16 * n)], 512 * n, rows=n)
 
-    aw, pw, ga, d1w, d2w, base = {-1: ia}, {-1: []}, [], [], [], []
+    aw, pw, d1w, d2w, clear = {-1: ia}, {-1: []}, [], [], []
 
-    def delta(hh, ll, off, eng, banks=None):
+    def delta(nm, hh, ll, off, eng, banks=None):
         if eng == "s":
-            d2w.extend(pairs(hh, ll, (3, 3), off, "s", base + ga, banks))
+            d2w.extend(write(nm, [(hh, 0), (ll, 0)], off, "D1", [idl], None, banks))
         else:
-            d1w.extend(pairs(hh, ll, (0, 0), off, "v", [idl], banks))
+            d1w.extend(write(nm, [(hh, 0), (ll, 1)], off, "A0", clear, None, banks))
 
     def walks(t, h):
         isp = h == t % 2
@@ -387,42 +444,46 @@ def build(par, c):
         win = ("A0", 0, W) if old else ("A", 0, W)
         after = [] if old else aw[0] if isp else aw[t - 1]
         sb, pb, n = "P%d" % h, "P%d" % (2 + h), blk(t)
-        z = ("Z%d" % t if t else "D0", h, 1024, 2)
+        zb = "Z1" if t == 1 else "D0"
         slot = lambda k: (pb, 6 - k, 64 * n, n)
+        nm = lambda k: "%d%s%d" % (t, "QP"[isp], k)
         for k in range(1, 6):
             if (k > 1 or t == 0) and (k < 5 or t < 2 or isp):
-                sides = [(0, 1)] if t == 2 and k == 5 else [(0, 1), (1, 1)] if par["split"] and t > 0 and not isp else [(0, 2)]
-                for s, m in sides:
-                    o_ = 2048 * h + 1024 * (k % 2) + 512 * s
-                    g_ = ("GS", o_, o_ + 512 * m)
-                    sp = (sb, 32 * s, 32 * (s + m))
-                    x = gat(g_, win, sub(Uu(t, h, k), s, m), "sv", after)
-                    if not old:
-                        ga.append(x)
-                    prev = [(sp, KN, sub(Kk(t, h, k - 1), s, m)), const(sp, k - 2)] if k > 1 else [(sub(sp, s), IN, R(h)) for s in range(2)]
-                    pe([to_list(sp, g_, 0) + prev])
-                    if k < 5:
-                        ts(sub(Uu(t, h, k + 1), s, m), sp, float(W - 1), None, OP.min)
-                    key(t, h, k + 1, sp, sub(Kk(t, h, k + 1), s, m))
-                    if t > 0 and k < 4 and s == 0:
-                        tt(b32("OV", 3 * h + k - 1), sub(sp, 0), NE(h, 1), OP.is_equal)
+                m = 1 if t == 2 and k == 5 else 2
+                o_ = 2048 * h + 1024 * (k % 2)
+                g_ = ("GS", o_, o_ + 512 * m)
+                sp = (sb, 448 * (k % 2), 448 * (k % 2) + 32 * m)
+                m_ = 1 if par["half"][2 * t + (not isp)] else m
+                for i in range(m // m_):
+                    named("w" + nm(k), gat(sub(g_, 16 * i, 16 * m_), win, sub(Uu(t, h, k), i, m_), "sv", after))
+                test = t > 0 and k < 4
+                less = WT[k - 1] if k > 1 and not test else 0.0
+                prev = [(sp, KN, sub(Kk(t, h, k - 1), 0, m))] + ([const(sp, k - 2)] if test else []) if k > 1 else [(sp, IN, R(h, 2))]
+                if t > 0 and k < 5:
+                    prev.append((sub(sp, 0), IBM(6), b32("OV", 3 * h + k - 2)))
+                pe([to_list(sp, g_, 0) + prev])
+                if k < 5:
+                    ts(Uu(t, h, k + 1), sp, less, float(W - 1), OP.add, OP.min)
+                key(t, h, k + 1, sp, sub(Kk(t, h, k + 1), 0, m), less)
+                if test:
+                    tt(b32("OV", 3 * h + k - 1), sub(sp, 0), NE(h, 1), OP.is_equal)
             c_ = 2048 * h + 1024 * (k % 2)
-            if t == 0:
-                cmpg(("CM", c_, c_ + 1024), Uu(t, h, k), ("D0", h, 2048, 2))
-            for s in range(2 if t else 0):
-                cmpg(("CM", c_ + 512 * s, c_ + 512 * s + 512), sub(Uu(t, h, k), s), z)
-            stop = [b32("OV", 3 * h + j - 2) for j in range(2, k)] if t else []
-            stop += [b32("SP", j) for j in range(t) if j % 2 != h]
+            if k > par["dup"]:
+                named("c" + nm(k), cmpg(("CM", c_, c_ + 1024), Uu(t, h, k), (zb, h, 2048, 2)))
+            else:
+                for s in range(2):
+                    named("c" + nm(k) + "ab"[s], cmpg(("CM", c_ + 512 * s, c_ + 512 * s + 512), sub(Uu(t, h, k), s), (zb, h, 1024, 2)))
+            stop = [b32("SP", j) for j in range(t) if j % 2 != h]
             ends = [[const(slot(6), 6)]] + ([[const(slot(0), 5)]] if t == 2 else []) if k == 1 else []
-            pe([to_list(slot(k), ("CM", c_, c_ + 1024), ALL) + [const(slot(k), 4)] + [(sub(slot(k), 0), IBM(0), a) for a in stop]] + ends)
+            pe([to_list(slot(k), ("CM", c_, c_ + 1024), ALL) + [const(slot(k), 4)] + [(sub(slot(k), 0), IBM(1), a) for a in stop]] + ends)
 
     def embed(t, h):
         isp = h == t % 2
         sb, pb, n = "P%d" % h, "P%d" % (2 + h), blk(t)
         kb, sc = Kk(t, h, 1)[0], "SC%d" % h
         lo, hi, lw, fs = (sb, 64, 192), (sb, 192, 320), (sb, 320, 384), (sb, 384, 416)
-        pe([[const((sb, 64, 416), CE)] + [(sub(a, 2 * i, 2), KP, Kk(t, h, 1 + i)) for a in (lo, hi) for i in range(2)]
-            + [(lw, IP, DUM), (fs, IP, LN[h])]], True, False, sb)
+        pe([[const((sb, 64, 448), ("CE", 384 * (t == 2), 384 * (t == 2) + 384))] + [(lw, IP, DUM)] * spare(t, h)
+            + [(sub(hi, 2 * i, 2), KP, Kk(t, h, 1 + i)) for i in range(2 if t < 2 else 1)]], True, False, sb)
         m = 64 * n
         scan((sc, 0, m), (pb, 0, m), (kb, 1, m + 1))
         o = 2 if t == 2 else 0
@@ -432,28 +493,36 @@ def build(par, c):
             scan((sc, 2 * m, 2 * m + m // 2), (pb, 0, m // 2), (kb, 0, m // 2))
             nf = 5
         fin = (sc, 5, 5 + 32 * nf * n - n + 1, n)
-        mn, wn = b32("MN", 5 * h, nf), b32("WN", 5 * h, nf)
+        wn = b32("MN", 5 * h, nf)
         tt(b32("E", 2 * h + 1), sub(fin, 0), sub(fin, 1), OP.min)
-        ts(mn, fin, 1 / KEY, None, OP.mult)
-        ts(wn, mn, W - 1, None, OP.bitwise_and)
-        cp(UW(h, 0, nf), wn)
+        for i, j in ((0, 2), (2, nf - 2)) if par["cut"][isp] else ((0, nf),):
+            ts(sub(wn, i, j), sub(fin, i, j), 1 / KEY, None, OP.mult)
+            ts(sub(wn, i, j), sub(wn, i, j), W - 1, None, OP.bitwise_and)
+        nu = nf if nf == 5 else 3 if isp else 2
+        cp(UW(h, 0, nu), sub(wn, 0, nu))
         tt(b32("E", 2 * h), sub(wn, 0), sub(wn, 1), OP.is_equal)
         tt(EM(h), b32("E", 2 * h), b32("E", 2 * h + 1), OP.is_le)
-        pe([[(fs, IBM(4 + h), EM(h))] + [(sub(a, i), IBM(j), EM(h)) for a, j in ((lo, 1), (hi, 2), (lw, 1)) for i in range(sz(a) // 32)]], False, True, sb)
+        ns, nw = 4 if t < 2 else 2, 2 if spare(t, h) else 0
+        parts = ((lo, 1, ns), (hi, 2, ns), (lw, 1, nw), ((sb, 416, 448), 1, not isp))
+        pe([[(fs, IBM(4 + h), EM(h))] * (t < 2) + [(sub(a, i), IBM(j), EM(h)) for a, j, n_ in parts for i in range(n_)]], False, True, sb)
         if t < 2:
-            cp(b32("FS", 2 * t + h), fs)
+            ts(b32("FS", 2 * t + h), fs, PC(6 + h), None, OP.add)
             send(b32("FS", 2 * t + h), b32("FO", 2 * t + h), 2 + 2 * t + h)
         tt(b32("TM", 4 * h, 4), lo, sub(wn, 0, 4), OP.max)
         tt(NE(h, 0, 4), hi, b32("TM", 4 * h, 4), OP.min)
-        tt(NE(h, 4, 2), lw, sub(wn, 0, 2), OP.max)
+        if nw:
+            tt(NE(h, 4, 2), lw, sub(wn, 0, 2), OP.max)
         u1 = Uu(t + 1, h, 1)
-        cp(("U", u1[1], u1[1] + 192), NE(h, 0, 6))
+        i, j = (4, 6) if t == 2 else (0, 6 if nw else 2)
+        cp(("U", u1[1] + 32 * i, u1[1] + 32 * j), NE(h, i, j - i))
         if t < 2:
             key(t + 1, h, 1, NE(h, 0, 2))
             if not isp:
                 key(t + 1, h, 2, NE(h, 2, 2))
                 tt(b32("OV", 3 * h), NE(h, 2), NE(h, 1), OP.is_equal)
-            gat(("Z%d" % (t + 1), h, 1024, 2), ("ZW%d" % (t + 1), 0, 3072), b32("FO", 2 * t + h))
+            za, zc = [("D0" if t else "Z1", o_ + h, o_ + 1024, 2) for o_ in (0, 1024)]
+            named("Z%d%s" % (t + 1, "PQ"[isp]), gat(za, ("ZW%d" % (t + 1), 0, 3072), b32("FO", 2 * t + h)))
+            copy(zc, za)
 
     def told(out, st, h):
         return [(out, sel("ZP", 144 * st, r), ("LW", 2 * r + h, 1024, 32)) for r in range(16)]
@@ -462,35 +531,27 @@ def build(par, c):
         flex(hh, src, 64.0)
         tt(ll, src, hh, OP.subtract)
 
-    def root(out, h):
-        return [(out, IP, NE(h, 0)), (out, IP, NE(h, 1)), (out, IN, b32("NI", 2 * h)), (out, IN, b32("NI", 2 * h + 1))]
-
     def parents(t):
         h = t % 2
         q_ = 1 - h
-        gat(("G1", 0, 512), ("KW", 0, W), UW(h, 0), scale=M1)
-        gat(("G2", 0, 512), ("KW", 0, W), UW(h, 2 if t < 2 else 4), scale=M2, bias=B2)
+        named("G%d" % t, gat(("G1", 0, 512), ("KW", 0, W), UW(h, 0), scale=M1),
+              gat(("G2", 0, 512), ("KW", 0, W), UW(h, 2 if t < 2 else 4), scale=M2, bias=B2))
         kb = ("P%d" % (2 + h), 448, 480)
         pe([to_list(kb, ("G1", 0, 512), 1)], True, False, kb[0])
-        pe([[(kb, IBM(3), EM(h))]], False, True, kb[0])
+        pe([[(kb, IBM(1), EM(h))]], False, True, kb[0])
         tt(b32("PT", 0), kb, LDUM, OP.min)
-        ts(b32("LO", t), b32("PT", 0), 4096.0, None, OP.add)
-        scat(("LW", 0, 1536), b32("LO", t), ("G1", 0, 512), "v", src2=("G2", 0, 512))
-        for i, st in enumerate((4, 2, 5)):
-            o = ("P4", 32 * i, 32 + 32 * i)
-            pe([told(o, st, q_) + ([(o, ("ONE", 0, 128, 1, 1), ("ONE", 0, 32, 1, 1))] if st == 5 else [])])
-        flex(b32("LI", 0, 3), ("P4", 0, 96))
-        tt(b32("Q", 0), b32("LI", 2), R(q_), OP.mult)
+        ts(b32("LO", t), b32("PT", 0), BIG, None, OP.add)
+        named("LW%d" % t, scat(("LW", 0, 1536), b32("LO", t), ("G1", 0, 512), "v", src2=("G2", 0, 512)))
+        for i, st in enumerate((4, 2)):
+            pe([told(("P4", 32 * i, 32 + 32 * i), st, q_)])
+        flex(b32("LI", 0, 2), ("P4", 0, 64))
         tag[0] += 1
         if t < 2:
             tt(b32("PT", 1), NE(h, 2), NE(h, 1), OP.is_equal)
         else:
-            sb = "P%d" % h
-            pe([[((sb, 0, 64), IN, NE(h, 2, 2))] + [((sb, 32 * s, 32 * s + 32), IP, R(h)) for s in range(2)], root((sb, 64, 96), h)])
-            digits(b32("HP", 0, 3), b32("LP", 0, 3), (sb, 0, 96))
-            delta(b32("HP", 0, 2), b32("LP", 0, 2), Uu(3, h, 0), par["last"][0])
-            if not par["roots"]:
-                delta(b32("HP", 2), b32("LP", 2), b32("RU", h), par["last"][1])
+            turned([(NE(h, 1, 3), IP), (NE(h, 0), IP), (SR(h, 3), IN)], 96, 32768.0, PC(10) + (1, 96), "RW", 0, "P%d" % h)
+            for i, off in enumerate((b32("RU", h), sub(Uw(2, h), 0), sub(Uw(2, h), 1))):
+                d2w.extend(named("d", scat(("D1", 0, WD), off, ("RW", 512 * i, 512 * i + 512), "s", [idl])))
 
     def children(t):
         h = 1 - t % 2
@@ -498,10 +559,10 @@ def build(par, c):
         Q = lambda i, n=1: b32("Q", i, n)
         li = lambda i, n=1: b32("LI", i, n)
         cb, spl = ("P%d" % (2 + h), 448, 480), b32("SP", t)
-        gat(("GX", 0, 512), ("X", 0, W), UW(h, 1))
-        cmpg(("CK", 0, 512), UW(h, 0), ("GX", 0, 512))
-        pe([to_list(cb, ("CK", 0, 512), ALL)])
-        tt(spl, EM(h), li(2), OP.is_gt)
+        named("GX%d" % t, gat(("GX", 0, 512), ("X", 0, W), UW(h, 1)))
+        named("CK%d" % t, cmpg(("GR", 0, 512), UW(h, 0), ("GX", 0, 512)))
+        tt(spl, li(0), ("P%d" % h, 416, 448), OP.is_gt)
+        pe([to_list(cb, ("GR", 0, 512), ALL) + [(cb, IBM(2), spl)]])
         t3 = lambda i, n=1: ("P4", 160 + 32 * i, 160 + 32 * (i + n))
         dif = lambda o, a, b: [(o, IP, a), (o, IN, b)]
         cross = lambda o: [(o, IP, NE(h, 0, 2)), (sub(o, 0), IN, li(1)), (sub(o, 1), IN, li(0))]
@@ -509,41 +570,40 @@ def build(par, c):
         pe([dif(t3(0), NE(h, 0), NE(h, 1))])
         pe([dif(t3(1), li(1), li(0))])
         if t < 2:
-            pe([cross(t3(2, 2))])
-        pe([[(t3(4, nq), IP, sub(DUM, 0, nq))] + [(t3(4 + i), IBM(1), spl) for i in range(nq)]])
+            pe([cross(t3(2, 2)) + [const(t3(2, 2), CQ)]])
+        pe([[(t3(4, nq), IP, sub(DUM, 0, nq)), const(t3(4, nq), sub(CQ, 0, nq))] + [(t3(4 + i), IBM(6), spl) for i in range(nq)]])
         tt(Q(1, nq), t3(4, nq), li(0, nq), OP.max)
-        cp(b32("QO", 0, nq), Q(1, nq))
+        ts(b32("QO", 0, nq), Q(1, nq), -BIG, None, OP.add)
         v = lambda i, n=1: ("P5", 32 * i, 32 * (i + n))
-        pe([[const(v(0, 5), CV)] + (told(v(4), 3, h) if t < 2 else [])], True, False, "P5")
-        pe([[(v(0), IP, Q(0)), (v(1), IP, Q(0)), (v(0, 2), IP, li(0, 2))]], False, False, "P5")
+        pe([[const(v(0, 5), CV)] + told(v(4), 3, h) if t < 2 else [const(v(0, 4), CW)]], True, False, "P5")
+        pe([[(v(0, 2), IP, li(0, 2)), (v(0), IBM(1), spl), (v(1), IBM(1), spl)]], False, False, "P5")
         if t < 2:
-            for i in range(2):
-                zero(("LW", 512 * i, 512 * i + 512))
-            for i, j in ((3, 0), (4, 2), (5, 3)):
+            reset(p_)
+            for i, j in ((4, 2), (5, 3)):
                 tt(Q(i), t3(j), spl, OP.mult)
             pe([[(v(0, 2), IP, NE(h, 2, 2)), (v(2, 2), IP, Q(4, 2)), (v(4), IP, Q(4))]], False, False, "P5")
         else:
             pe([[(v(0, 2), IN, NE(h, 2, 2))] + cross(v(2, 2))], False, False, "P5")
-        ts(Q(6), cb, 17.0, None, OP.is_ge)
+        ts(Q(6), cb, 17.0 + BIG, None, OP.is_ge)
         tt(Q(7), t3(1), Q(6), OP.mult)
-        tt(Q(8), Q(3) if t < 2 else t3(0), Q(6), OP.mult)
+        tt(Q(8), t3(0), Q(6), OP.mult)
         pe([[(v(0), IP, Q(7)), (v(1, 2), IN, Q(7, 2)), (v(3), IP, Q(8))] + ([(v(4), IN, Q(8))] if t < 2 else [])], False, True, "P5")
         nv_ = 5 if t < 2 else 4
         digits(b32("H5", 0, nv_), b32("L5", 0, nv_), v(0, nv_))
         hl = lambda i, row: [(b32("H5", i), row), (b32("L5", i), row + 1)]
         if t == 2:
-            delta(b32("H5", 2, 2), b32("L5", 2, 2), ("QO", 0, 64), "v" if par["last"][0] == "s" else "s")
-            delta(b32("H5", 0, 2), b32("L5", 0, 2), Uu(3, h, 0), par["last"][3], ("P5", "P4"))
+            delta("3b", b32("H5", 2, 2), b32("L5", 2, 2), ("QO", 0, 64), "v")
+            delta("3n", b32("H5", 0, 2), b32("L5", 0, 2), Uw(2, h), par["last"][1], ("P5", "P4"))
             ts(b32("LV", 0), b32("SP", 1), 0.0, None, OP.is_equal)
             tt(b32("LV", 1), b32("SP", 0), spl, OP.is_equal)
             return
         aft = aw[-1] + pw[t - 1]
-        aw[t] = pairs(b32("H5", 0, 2), b32("L5", 0, 2), (0, 1), Uu(t + 1, h, 0), "s", aft)
-        wb = write(hl(4, 0) + hl(3, 4) + hl(2, 6), b32("QO", 0), "s", aft, ("RW", h, 1024, 2), ("P5",))
+        aw[t] = write("%dn" % (t + 1), [(b32("H5", 0, 2), 0), (b32("L5", 0, 2), 1)], Uw(t, h), "A", aft)
+        wb = write("%db" % (t + 1), hl(4, 0) + hl(3, 4) + hl(2, 6), b32("QO", 0), "A", aft, ("RW", h, 1024, 2), ("P5",), staged[-2:])
         aw[t] += wb
         tag[0] += 1
         sb = "P%d" % p_
-        gat(("GR", 0, 512), ("RW", 0, 1536), b32("LO", t))
+        named("GR%d" % (t + 1), gat(("GR", 0, 512), ("RW", 0, 1536), b32("LO", t)))
         if t == 0:
             zero(("RW", h, 1024, 2))
         pe([to_list((sb, 128, 160), ("GR", 0, 512), 3)])
@@ -554,10 +614,8 @@ def build(par, c):
         key(t + 1, p_, 2, (sb, 0, 64))
         tt(b32("OV", 3 * p_), (sb, 0, 32), NE(p_, 1), OP.is_equal)
         tag[0] = 25
-        vb = ("P4", 448, 512)
-        pe([[(vb, KP, Kk(t + 1, p_, 2)), const(vb, ("CR", 576, 640))] + [(sub(vb, s), IP, R(p_)) for s in range(2)]])
-        digits(b32("HP", 0, 2), b32("LP", 0, 2), vb)
-        pw[t] = pairs(b32("HP", 0, 2), b32("LP", 0, 2), (0, 1), Uu(t + 1, p_, 0), "s", wb)
+        turned([(Kk(t + 1, p_, 2), KP), (R(p_, 2), IP)], 64, 64.0 - WT[2], 1.0, "WT", 0, "P4")
+        pw[t] = named("p%d" % (t + 1), *[scat(("A", 0, WD), sub(Uw(t, p_), i), ("WT", 512 * i, 512 * i + 512), "s", wb) for i in range(2)])
 
     fb = lambda i: ("P%d" % (2 * i), 256, 512)
     cs = lambda nm, i: (nm, 256 * i, 256 * i + 256)
@@ -570,8 +628,10 @@ def build(par, c):
         tag[0] += 1
         embed(t, p_)
         if t == 2:
-            base.append(dma([(lambda T: T.NHF[:], lambda T: T.A[0:128:16, 0:W]), (lambda T: T.NLF[:], lambda T: T.A[1:128:16, 0:W])],
-                            [("A", 0, W)], [("NHF", 0, 512), ("NLF", 0, 512)], 524288, aw[1] + pw[1]))
+            dma([(lambda T: T.NHF[:], lambda T: T.A[0:128:16, 0:W]), (lambda T: T.NLF[:], lambda T: T.A[1:128:16, 0:W])],
+                [("A", 0, W)], [("NHF", 0, 512), ("NLF", 0, 512)], 524288, aw[1] + pw[1])
+            zero(("NH", 0, 512))
+            clear.append(dma([(lambda T, i=i: T.A0[i:128:16, 0:W], lambda T: T.NH[:]) for i in range(2)], [("NH", 0, 512)], [("A0", 0, W)], 262144))
         parents(t)
         if t == 2:
             for i in range(2):
@@ -579,10 +639,10 @@ def build(par, c):
         tag[0] += 1
         embed(t, 1 - p_)
         if t == 2:
-            pe([root(("P1", 0, 32), 1)])
-            digits(b32("HP", 3), b32("LP", 3), ("P1", 0, 32))
-            i = 2 if par["roots"] else 3
-            delta(b32("HP", i, 4 - i), b32("LP", i, 4 - i), b32("RU", i - 2, 4 - i), par["last"][2])
+            o = ("P1", 0, 32)
+            pe([[(o, IP, NE(1, 0)), (o, IP, NE(1, 1)), (o, IN, SR(1))]])
+            digits(b32("H5", 4), b32("L5", 4), o)
+            delta("3r", b32("H5", 4), b32("L5", 4), b32("RU", 1), par["last"][0])
         tag[0] += 1
         children(t)
         if t == 0:
@@ -591,120 +651,24 @@ def build(par, c):
             rotate("ZW2")
 
     tag[0] = 21
-    for nm, n, bk, ob in (("yn", 64, "P1", "RW"), ("yl", 32, "P3", "TM")):
-        a = [NE(h, 0, 2) if nm == "yn" else b32("LV", h) for h in range(2)]
-        add([("t", 60.0 + 2048 * PCY, lambda q, T, r, a=a, n=n, bk=bk: [q.matmul(T[bk][0:n, 256:512], r(a[h]), T.EO[:, 256 * h:256 * h + 256], h == 0, h == 1) for h in range(2)])],
-            a + [("EO", 0, 512)], [(bk, 256, 512)])
-        add([("s", 15.0 + vc(256), lambda q, T, r, n=n, bk=bk, ob=ob: [q.activation(T[ob][0:n, 0:256], T[bk][0:n, 256:512], AF.Copy)]),
-             ("v", vc(256), lambda q, T, r, n=n, bk=bk, ob=ob: [q.tensor_copy(T[ob][0:n, 0:256], T[bk][0:n, 256:512])])], [(bk, 256, 512)], [(ob, 0, 256)])
-        dma([(lambda T, g_=g_, nm=nm: T[nm][g_, :], lambda T, g_=g_, n=n, ob=ob: T[ob][0:n, 32 * g_:32 * g_ + 32]) for g_ in range(8)], [(ob, 0, 256)], [], 65536)
-    dma([(lambda T: T.DN2[:], lambda T: T.A[3:128:16, 0:W])], [("A", 0, W)], [("DN2", 0, 512)], 262144, d2w, q="s")
-    dma([(lambda T: T.DN1[:], lambda T: T.D1[0:128:16, 0:W])], [("D1", 0, W)], [("DN1", 0, 512)], 262144, d1w)
+    for nm, n, bk, ob in (("yn", 64, "P1", "SC0"), ("yl", 32, "P3", "TM")):
+        for h in range(2):
+            o = (bk, 256 + 128 * h, 384 + 128 * h, 1, n)
+            pe([[(o, NE(h, 0, 2), IP) if nm == "yn" else (o, b32("LV", h), IBM(2))]])
+            flex((ob, h, 256, 2, n), o, 0.0, "sv", 1.0 if nm == "yn" else 1 / BIG)
+        dma([(lambda T, g_=g_, nm=nm: T[nm][g_, :], lambda T, g_=g_, n=n, ob=ob: T[ob][0:n, 32 * g_:32 * g_ + 32]) for g_ in range(8)], [(ob, 0, 256)], [], 1024 * n, rows=n)
+    dma([(lambda T: T.DN2[:], lambda T: T.D1[0:128:16, 0:W])], [("D1", 0, W)], [("DN2", 0, 512)], 262144, d2w, q="s")
+    dma([(lambda T: T.NH[:], lambda T: T.A0[0:128:16, 0:W]), (lambda T: T.NM[:], lambda T: T.A0[1:128:16, 0:W])],
+        [("A0", 0, W)], [("NH", 0, 512), ("NM", 0, 512)], 262144, d1w)
     for i in range(2):
-        pe([[(fb(i), IP, cs("DN2", i))]], False, True, fb(i)[0])
-        tt(cs("NLF", i), fb(i), cs("DN1", i), OP.add)
+        pe([[(fb(i), IP, cs("DN2", i))]], False, False, fb(i)[0])
+        pe([[(fb(i), IBM(7), cs("NH", i)), (fb(i), IBM(7), cs("NM", i))]], False, True, fb(i)[0])
+        flex(cs("NLF", i), fb(i), -MAGIC - 32896.0)
     dma([(lambda T: T.ys[:], lambda T: T.NLF[:])], [("NLF", 0, 512)], [], 262144)
     return ops
 
 
-def place(ops, pri, pred, succ, fixed, hop, par):
-    n = len(ops)
-    left = [len(p) for p in pred]
-    rdy = [0.0] * n
-    todo = sorted(range(n), key=lambda j: (pri[j], -j))
-    passed = [False] * n
-    late = []
-    busy = {e: [] for e in "vstgyn"}
-    lock, out = {}, []
-    while todo or late:
-        if late:
-            i = max(late, key=lambda j: (pri[j], -j))
-            late.remove(i)
-        else:
-            i = todo.pop()
-            if left[i]:
-                passed[i] = True
-                continue
-        o = ops[i]
-        lk, lat = o["lk"], o["lat"] + hop
-        best = None
-        for a in (o["alts"] if fixed is None else (fixed[i],)):
-            e, d = a[0], a[1]
-            s = rdy[i]
-            iv = busy[e]
-            k = len(iv)
-            while k and iv[k - 1][1] > s:
-                k -= 1
-            while True:
-                while k < len(iv) and iv[k][0] < s + d:
-                    if iv[k][1] > s:
-                        s = iv[k][1]
-                    k += 1
-                s0 = s
-                for nm, w, bank in lk:
-                    lv = lock.get(nm, ())
-                    m = len(lv)
-                    while m and lv[m - 1][0] > s - (2500.0 if bank else 9000.0):
-                        m -= 1
-                    while m < len(lv) and lv[m][0] < s + d + lat:
-                        x = lv[m]
-                        if x[1] > s and ((x[2] != e) if bank else (w or x[3])):
-                            s = x[1]
-                        m += 1
-                if s == s0:
-                    break
-            if fixed is not None:
-                best = (s, s, a, k)
-            else:
-                f = s + d + (par["flex0" if s + d < par["xl"] else "flexv"] * d if e == "v" else 0.0)
-                if best is None or f < best[0]:
-                    best = (f, s, a, k)
-        _, s, a, k = best
-        end = s + a[1] + lat
-        if a[0] != "n":
-            busy[a[0]].insert(k, (s, s + a[1]))
-        for nm, w, bank in lk:
-            lv = lock.setdefault(nm, [])
-            m = len(lv)
-            while m and lv[m - 1][0] > s:
-                m -= 1
-            lv.insert(m, (s, end, a[0], w))
-        out.append((i, a, s, end - hop))
-        for j in succ[i]:
-            if end > rdy[j]:
-                rdy[j] = end
-            left[j] -= 1
-            if left[j] == 0 and passed[j]:
-                late.append(j)
-    out.sort(key=lambda x: (x[2], x[0]))
-    return out
-
-
-def blocks(ops, plan, pred, hop):
-    at, last, before = {}, {}, {}
-    for (i, a, s, e) in plan:
-        at[i] = (a, s, e)
-        before[i] = [last.get(a[0])] + [last.get(nm) for nm, w, bank in ops[i]["lk"]]
-        for k in [a[0]] + [nm for nm, w, bank in ops[i]["lk"]]:
-            last[k] = i
-    i = max(at, key=lambda j: at[j][2])
-    out = []
-    while True:
-        s = at[i][1]
-        dep = [j for j in pred[i] if at[j][2] + hop >= s - 0.5]
-        if dep:
-            i = dep[0]
-            continue
-        cand = [j for j in before[i] if j is not None]
-        if s < 0.5 or not cand:
-            return out
-        j = max(cand, key=lambda k: at[k][1] + at[k][0][1] if at[k][0][0] == at[i][0][0] else at[k][2] + hop)
-        out.append((j, i))
-        i = j
-
-
-def schedule(ops, par, c):
-    n = len(ops)
+def links(ops):
     pred, above = [], []
     for o in ops:
         far = 0
@@ -714,90 +678,261 @@ def schedule(ops, par, c):
         for d in o["dep"]:
             far |= 1 << d
         above.append(far)
-    succ = [[] for _ in range(n)]
-    for o in ops:
-        lk = {}
+    succ = [[] for _ in ops]
+    for i, p in enumerate(pred):
+        for d in p:
+            succ[d].append(i)
+    return pred, succ
+
+
+def queues(par):
+    v = ["c0P1a", "c0P1b", "c0Q1a", "c0Q1b", "c0P2", "c0P3", "c0P4", "c0Q2", "c0P5", "c0Q3", "c0Q4", "c0Q5", "LW0"]
+    s = ["w0%s%d" % (h, k) for k in range(1, 6) for h in "PQ"] + ["G0", "Z1Q", "GX0"]
+    for t in (1, 2):
+        v += ["c%dQ1a" % t] * (t > 1) + ["CK%d" % (t - 1)] + ["c%dQ1a" % t] * (t == 1)
+        v += [x % t for x in ("c%dQ1b", "c%dP1a", "c%dP1b", "c%dP2", "c%dP3", "c%dP4", "c%dP5", "c%dQ2", "c%dQ3", "LW%d", "c%dQ4", "c%dQ5")]
+        s += [x % t for x in ("w%dP2", "Z%dP", "w%dP3", "s%dn", "w%dP4", "a%dn0", "s%db", "GR%d", "a%dn1", "w%dP5", "a%db0", "w%dQ2", "w%dQ3", "G%d", "w%dQ4")]
+        s += ["Z2Q", "w1Q5", "p1", "GX1"] if t == 1 else ["p2", "GX2", "d", "s3r", "a3r0", "s3n", "a3n0", "a3n1"]
+    return {"v": v + ["CK2", "s3b", "a3b0", "a3b1"], "s": s}
+
+
+def first_order(ops, par, c):
+    n = len(ops)
+    pred, succ = links(ops)
+    early = sorted((o["turn"], o["n"]) for o in ops if "turn" in o)
+    tail = [0.0] * n
+    for i in reversed(range(n)):
+        tail[i] = ops[i]["alts"][0][1] + ops[i]["lat"] + ops[i]["move"] + c["hop"] + max([tail[j] for j in succ[i]] + [0.0])
+    line, turn, queue = {}, {}, {}
+    for e, names in queues(par).items():
+        line[e] = [o["n"] for nm in names for o in ops if o.get("nm") == nm]
+        turn[e] = 0
+        queue.update((i, e) for i in line[e])
+    left = [len(p) for p in pred]
+    rdy = [0.0] * n
+    free, lock, out = {e: 0.0 for e in "vstgyn"}, {}, []
+    ready = [i for i in range(n) if not left[i]]
+    while ready:
+        best = None
+        for i in ready:
+            o = ops[i]
+            if i in queue and line[queue[i]][turn[queue[i]]] != i or o["move"] and early and early[0][1] != i:
+                continue
+            for a in o["alts"]:
+                e = a[0]
+                if queue.get(i, e) != e or (e == "v" and a is not o["alts"][0] and i not in queue and rdy[i] > par["head"]):
+                    continue
+                s = max([rdy[i], free[e] * (e != "n")] + [lock.get((x[0], k), 0.0) for x in o["rd"] + o["wr"] if isps(x) for k in "vst" if k != e]
+                        + [lock.get((x[0], 1), 0.0) for x in o["rd"] + o["wr"] if window(x)] + [lock.get((x[0], 0), 0.0) for x in o["wr"] if window(x)])
+                f = (s - par["pull"] * (tail[i] + o["pri"]), i)
+                if best is None or f < best[0]:
+                    best = (f, i, a, s)
+        _, i, a, s = best
+        o, e = ops[i], a[0]
+        end = s + a[1]
+        if o["move"]:
+            end = free["n"] = max(end, free["n"]) + o["move"]
+        end += o["lat"] + c["hop"]
+        if e != "n":
+            free[e] = s + a[1]
         for x, w in [(x, 0) for x in o["rd"]] + [(x, 1) for x in o["wr"]]:
-            if isps(x) or x[0] in ("A", "D1"):
-                lk[x[0]] = max(lk.get(x[0], 0), w)
-        o["lk"] = [(k, v, k[0] == "P") for k, v in sorted(lk.items())]
-        for d in pred[o["n"]]:
-            succ[d].append(o["n"])
-    pri = [0.0] * n
-    for o in reversed(ops):
-        i = o["n"]
-        pri[i] = min(a[1] for a in o["alts"]) + o["lat"] + c["hop"] + max([pri[j] for j in succ[i]] + [0.0])
-    best = None
-    seed = par["seed"]
-    for _ in range(par["iters"]):
-        p = []
-        for i in range(n):
-            seed = (seed * 1103515245 + 12345) % 2147483648
-            p.append(pri[i] + ops[i]["pri"] + par["boost"][ops[i]["tag"]] + par["noise"] * seed / 2147483648.0)
-        fw = place(ops, p, pred, succ, None, c["hop"], par)
-        span = max(x[3] for x in fw)
-        if best is None or span < best[0]:
-            best = (span, fw)
-        fixed, back = {}, [0.0] * n
-        for (i, a, s_, e_) in fw:
-            fixed[i] = a
-            back[i] = e_
-        for (i, a, s_, e_) in place(ops, back, succ, pred, fixed, c["hop"], par):
-            pri[i] = e_
+            if isps(x) or window(x):
+                k = (x[0], e if isps(x) else w)
+                lock[k] = max(lock.get(k, 0.0), end)
+        if i in queue:
+            turn[e] += 1
+        out.append((i, a, s, end - c["hop"]))
+        ready.remove(i)
+        if "turn" in o:
+            early.pop(0)
+        for j in succ[i]:
+            rdy[j] = max(rdy[j], end)
+            left[j] -= 1
+            if not left[j]:
+                ready.append(j)
+    return out
+
+
+def anneal(sets, weights, hops, start, seed, moves, temp, lam, mu, lo=0.0, hi=1.0):
+    ops = sets[0]
+    n = len(ops)
+    pred, succ = links(ops)
+    eng = {e: k for k, e in enumerate("vstgyn")}
+    table = [[] for _ in sets]
+    for i, o in enumerate(ops):
+        rows = [[] for _ in sets]
+        for ai, a in enumerate(o["alts"]):
+            e = eng[a[0]]
+            need, mark = ([n + e] if e < 5 else []) + pred[i], []
+            for nm in sorted(set(x[0] for x in o["rd"] + o["wr"] if isps(x) or window(x))):
+                if isps((nm,)):
+                    b = n + 6 + 3 * int(nm[1:])
+                    need += [b + k for k in range(3) if k != e]
+                    mark.append(b + e)
+                else:
+                    b = n + 30 + 2 * ("A", "D1", "A0").index(nm)
+                    w = any(x[0] == nm for x in o["wr"])
+                    need += [b, b + 1] if w else [b + 1]
+                    mark.append(b + w)
+            for m, s in enumerate(sets):
+                rows[m].append((n + e, need, mark, s[i]["alts"][ai][1], s[i]["lat"] + hops[m], s[i]["move"]))
+        for m in range(len(sets)):
+            table[m].append(rows[m])
+    order = [x[0] for x in start]
+    alt = [[a[0] for a in ops[x[0]]["alts"]].index(x[1][0]) for x in sorted(start, key=lambda y: y[0])]
+    step = 25
+
+    def replay(order, alt, m, first, last, old):
+        c = first // step
+        tab = table[m]
+        if old:
+            st, saved, total = old[0][:n] + old[1][c], old[1][:c], old[2]
+        else:
+            st, saved, total = [0.0] * (n + 37), [], 0.0
+        moved, seen = [], set()
+        for p in range(c * step, n, step):
+            if p > last and st[n:] == old[1][p // step]:
+                moved = [i for i in moved if not seen.issuperset(succ[i])]
+                if not moved:
+                    return st, saved + old[1][p // step:], total
+            saved.append(st[n:])
+            part = order[p:p + step]
+            seen.update(part)
+            for i in part:
+                e, need, mark, d, lat, move = tab[i][alt[i]]
+                s = max([st[j] for j in need]) + d
+                st[e] = s
+                if move:
+                    s = st[n + 36] = max(s, st[n + 36]) + move
+                s += lat
+                if st[i] != s:
+                    total += s - st[i]
+                    st[i] = s
+                    moved.append(i)
+                for k in mark:
+                    if s > st[k]:
+                        st[k] = s
+            st[n + 5] = 0.0
+        return st, saved, total
+
     state = [seed]
 
     def rnd():
         state[0] = (state[0] * 1103515245 + 12345) % 2147483648
         return state[0] / 2147483648.0
-    span, cur = best
+
     either = [i for i in range(n) if len(ops[i]["alts"]) > 1]
-    fixed, tight = {}, []
-    for (i, a, s_, e_) in cur:
-        pri[i], fixed[i] = -s_, a
-    for it in range(par["moves"]):
-        p, f, x = list(pri), dict(fixed), rnd()
-        if x < 0.45:
-            if not tight:
-                tight.extend(blocks(ops, cur, pred, c["hop"]))
-            i, j = tight[int(rnd() * len(tight))]
-            if x < 0.15:
-                p[i] = p[j] - 1.0
-            elif x < 0.3:
-                p[j] = p[i] + 1.0
-                for k in pred[j]:
-                    p[k] = max(p[k], p[j] + 1.0)
+    sinks = [i for i in range(n) if not succ[i]]
+    fee = [[lam * x[3] * ((1.0, 0.6, 0, 0, 0, 0) if 0 < o["tag"] < 22 or o["tag"] == 25 else (0.1, 0.1, 0, 0, 0, 0))[x[0] - n] for x in row]
+           for o, row in zip(ops, table[0])]
+    before, behind = [list(x) for x in pred], [list(x) for x in succ]
+    for i in range(n):
+        for j in range(n if ops[i]["move"] else 0):
+            if ops[j].get("turn", 99) < ops[i].get("turn", 99):
+                before[i].append(j)
+                behind[j].append(i)
+
+    def value(order, alt, first, last, old):
+        v = sum([fee[i][alt[i]] for i in either])
+        new = [replay(order, alt, m, first, last, old and old[m]) for m in range(len(sets))]
+        for w, (st, _, total) in zip(weights, new):
+            v += w * (max([st[i] for i in sinks]) + mu * total / n)
+        return v, new
+
+    def tight(order, alt, clock):
+        m = int(rnd() * len(sets))
+        st, tab = clock[m][0], table[m]
+        who, last, at = {}, {}, {}
+        for i in order:
+            at[i] = len(at)
+            e, need, mark, d, lat, move = tab[i][alt[i]]
+            who[i] = [last.get(k, -1) if k >= n else k for k in need] + [last.get(n + 36, -1)]
+            last[e] = i
+            if move:
+                last[n + 36] = i
+            for k in mark:
+                if k not in last or st[i] >= st[last[k]]:
+                    last[k] = i
+        i = max(sinks, key=lambda j: st[j])
+        out = []
+        while True:
+            e, need, mark, d, lat, move = tab[i][alt[i]]
+            s = st[i] - d - lat - move - 30.0
+            c = [(j, k >= n) for j, k in zip(who[i], need + [n + 36] * (move > 0))
+                 if j >= 0 and st[j] - (tab[j][alt[j]][4] if k == n + 36 else sum(tab[j][alt[j]][4:]) if k == e else 0.0) >= s]
+            if not c:
+                return out
+            j, q = c[int(rnd() * len(c))]
+            if q and lo * n <= at[j] and at[i] <= hi * n:
+                out.append((j, i))
+            i = j
+
+    def shift(order, i, p):
+        q = order.index(i)
+        p = min(n - 1, max(0, p))
+        seg, near, take = (order[p:q][::-1], behind, {i}) if p < q else (order[q + 1:p + 1], before, {i})
+        for k in seg:
+            if not take.isdisjoint(near[k]):
+                take.add(k)
+        go, stay = [k for k in seg if k in take], [k for k in seg if k not in take]
+        if p < q:
+            return order[:p] + go[::-1] + [i] + stay[::-1] + order[q + 1:], p, q
+        return order[:q] + stay + [i] + go + order[p + 1:], q, p
+
+    def other(alt, k):
+        a = list(alt)
+        a[k] = (a[k] + 1 + int(rnd() * (len(ops[k]["alts"]) - 1))) % len(ops[k]["alts"])
+        return a
+
+    cur, clock = value(order, alt, 0, n, None)
+    best = (cur, order, alt, clock)
+    pairs, stale = tight(order, alt, clock), 0
+    for it in range(moves):
+        x = rnd()
+        o2, a2 = order, alt
+        if x < 0.7 and pairs:
+            j, i = pairs[int(rnd() * len(pairs))]
+            more = int(rnd() * rnd() * 12)
+            if x < 0.27:
+                o2, first, last = shift(order, i, order.index(j) - more)
+            elif x < 0.54:
+                o2, first, last = shift(order, j, order.index(i) + more)
             else:
-                for k in (i, j):
-                    if len(ops[k]["alts"]) > 1 and rnd() < 0.7:
-                        f[k] = [a for a in ops[k]["alts"] if a is not f[k]][0]
-        elif x < 0.55:
-            i = either[int(rnd() * len(either))]
-            f[i] = [a for a in ops[i]["alts"] if a is not f[i]][0]
+                k = i if rnd() < 0.5 else j
+                if len(ops[k]["alts"]) < 2:
+                    continue
+                a2 = other(alt, k)
+                first = last = order.index(k)
+                if rnd() < 0.5:
+                    o2, first, last = shift(order, k, first + int((rnd() - 0.5) * 24))
         elif x < 0.8:
-            i, d, up = int(rnd() * n), rnd() * rnd() * 8000.0, rnd() < 0.5
-            seen, edge = {i}, [i]
-            for _ in range(1 + int(rnd() * 8)):
-                edge = [k for j in edge for k in (pred[j] if up else succ[j]) if k not in seen and abs(p[k] - p[i]) < 9000.0]
-                seen.update(edge)
-            for k in seen:
-                p[k] += d if up else -d
-        elif x < 0.9:
-            tg, lo, d = 1 + int(rnd() * 25), -rnd() * span, (rnd() + rnd() - 1) * 6000.0
-            for i in range(n):
-                if ops[i]["tag"] == tg and lo - 6000.0 < p[i] < lo:
-                    p[i] += d
+            k = order[int((lo + (hi - lo) * rnd()) * n)]
+            if len(ops[k]["alts"]) < 2:
+                continue
+            a2 = other(alt, k)
+            first = last = order.index(k)
         else:
-            for _ in range(1 + int(rnd() * rnd() * 8)):
-                p[int(rnd() * n)] += (rnd() + rnd() - 1) * 3500.0
-        new = place(ops, p, pred, succ, f, c["hop"], par)
-        s = max(y[3] for y in new)
-        if s <= span + 300.0 * rnd() * rnd() * (1.0 - it / par["moves"]):
-            span, fixed, cur, tight = s, f, new, []
-            for (i, a, s_, e_) in new:
-                pri[i] = -s_
-            if s < best[0]:
-                best = (s, new)
-    return best[1]
+            k = order[int((lo + (hi - lo) * rnd()) * n)]
+            o2, first, last = shift(order, k, order.index(k) + int((rnd() + rnd() - 1) * 50))
+        v, c2 = value(o2, a2, first, last, clock)
+        if v <= cur + temp * rnd() * rnd() * (1.0 - it / moves):
+            cur, order, alt, clock = v, o2, a2, c2
+            if it - stale > 40:
+                pairs, stale = tight(order, alt, clock), it
+            if v < best[0]:
+                best = (v, o2, a2, c2)
+    _, order, alt, clock = best
+    st = clock[0][0]
+    return [(i, ops[i]["alts"][alt[i]], st[i] - sum(table[0][i][alt[i]][3:]), st[i] - hops[0]) for i in order]
+
+
+def schedule(par, costs):
+    sets = [build(par, c) for c in costs]
+    plan = first_order(sets[0], par, costs[0])
+    for moves, temp, lam, mu, weights, lo, hi in par["search"]:
+        use = [m for m, w in enumerate(weights) if w]
+        plan = anneal([sets[m] for m in use], [weights[m] for m in use], [costs[m]["hop"] for m in use], plan, par["seed"], moves, temp, lam, mu, lo, hi)
+    return sets[0], plan
 
 
 PLAN = []
@@ -808,9 +943,7 @@ def rank_program(g, core, T, topo):
     if rank is None:
         return
     if not PLAN:
-        ops = build(PARAM, COST)
-        PLAN.append(ops)
-        PLAN.append(schedule(ops, PARAM, COST))
+        PLAN.extend(schedule(PARAM, [COST, SLOW]))
     ops, order = PLAN
     nxt = T.cores[(rank + 1) % len(T.cores)]
     rid, pid = topo.addr(nxt)[0:2]
@@ -827,7 +960,7 @@ def rank_program(g, core, T, topo):
 
     def r(a):
         if len(a) > 4:
-            return T[a[0]][0:a[4], a[1]:a[2]]
+            return T[a[0]][0:a[4], a[1]:a[2] - (a[2] - a[1] - 1) % a[3]:a[3]]
         return T[a[0]][:, a[1]:a[2] - (a[2] - a[1] - 1) % a[3]:a[3]] if len(a) > 3 else T[a[0]][:, a[1]:a[2]]
 
     def wait(e, sem, val):
@@ -860,9 +993,9 @@ def rank_program(g, core, T, topo):
         known[i] = [(k[1], v) for k, v in waited.items() if k[0] == e]
         if o["kind"] == "s":
             src, dst, k = a[2]
-            g.remote_dma(r(dst), r(src), T.sem["a%d" % k], T.sem.sent, pid, rid, mask)
-            count["sent"] = count.get("sent", 0) + nen
-            token[i] = None
+            g.remote_dma(r(dst), r(src), T.sem["a%d" % k], T.sem["l%d" % k], pid, rid, mask)
+            token[i] = ("l%d" % k, nen)
+            count[token[i][0]] = nen
             continue
         ins = a[2](queue[e], T, r)
         if o["kind"] == "d":

from concourse.mybir import AluOpType as OP, ActivationFunctionType as AF

W = 8192
WD = W + 512
BF, F32, I32, U16 = "bfloat16", "float32", "int32", "uint16"
SB = {
    "X": (W, BF), "A0": (WD, BF), "KW": (W, BF), "A": (WD, F32), "D1": (WD, F32),
    "D0": (2048, BF), "ZW1": (3072, BF), "ZW2": (3072, BF), "Z1": (2048, BF),
    "NS": (512, I32), "KD": (512, I32), "NH": (512, BF), "NM": (512, BF),
    "NHF": (512, F32), "NLF": (512, F32), "DN2": (512, F32),
    "RN": (192, I32), "WT": (1024, F32), "TB": (256, F32), "IF": (512, F32), "ZN": (768, BF),
    "IB": (128 * 9, BF), "CE": (2 * 384, BF), "LT": (1024, BF), "ZS": (16 * 144, BF), "ZP": (7 * 144, BF), "ONE": (256, BF),
    "CR": (64 * 7 + 160 + 256 + 128, BF),
    "PI": (2, I32), "PF": (12, F32), "ST": (32 * 5, F32),
    "K0": (386, F32), "K1": (386, F32), "K2": (450, F32), "K3": (450, F32), "SC0": (1120, F32), "SC1": (896, F32),
    "U": (4 * 384, U16), "R": (192, F32), "RU": (64, U16),
    "GS": (4096, BF), "CM": (4096, BF), "OV": (192, BF), "SP": (96, BF),
    "MN": (320, I32), "E": (128, F32), "EM": (64, BF), "TM": (256, F32), "NE": (384, F32),
    "FS": (128, U16), "FO": (128, U16), "UB": (320, U16), "G1": (512, BF), "G2": (512, BF), "GR": (512, BF),
    "PT": (128, F32), "LO": (96, U16), "LW": (1536, BF), "LI": (128, F32),
    "RW": (1536, F32), "WS": (2048, F32),
    "Q": (32 * 9, F32), "QO": (64, U16), "GX": (512, BF), "H5": (160, BF), "L5": (160, BF),
    "LV": (64, BF),
}
SCRATCH = {k: ("sbuf", [128, v[0]], v[1]) for k, v in SB.items()}
for _i in range(8):
    SCRATCH["P%d" % _i] = ("psum", [128, 512], "float32")
SEMAPHORES = ["ev", "es", "et", "eg"] + ["d%d" % i for i in range(40)] + [s + str(i) for s in "al" for i in range(6)]

COST = {"cy": 0.85, "pe": 0.43, "ga": 1.4, "sc": 3.3, "hop": 80.0, "dma": 1300.0, "bw": 380.0, "call": 700.0, "once": 3500.0,
        "mm": 0.0, "row": 3.0, "f": 1.0}
SLOW = dict(COST, ga=1.6, sc=3.8, f=1.2, hop=160.0, dma=1700.0, bw=280.0, row=6.0, call=1200.0, once=6000.0)
PARAM = {"head": 10000.0, "pull": 0.01, "seed": 5, "last": "ss",
         "dup": 1, "fill": 7, "kw": [5, 7, 6], "cut": [0, 0], "half": [0, 0, 0, 0, 1, 0],
         "search": [(20000, 500.0, 0.3, 2.0, (1.0, 0.0), 0.0, 0.4), (100000, 900.0, 0.3, 0.3, (1.0, 0.0), 0.0, 1.0),
                    (15000, 500.0, 0.1, 0.05, (0.6, 0.45), 0.55, 1.0), (45000, 450.0, 0.1, 0.05, (0.6, 0.45), 0.0, 1.0),
                    (30000, 400.0, 0.05, 0.03, (0.6, 0.45), 0.2, 0.65), (35000, 400.0, 0.05, 0.03, (0.6, 0.45), 0.6, 1.0)]}
KEY = 2.0 ** -20
WT = [(5 - k) * 65536.0 for k in range(7)]
MAGIC = 1.5 * 2 ** 23
BIG = 16384.0


def meet(a, b):
    if len(a) > 3 and len(b) > 3 and a[3] == b[3] and (a[1] - b[1]) % a[3]:
        return False
    return a[1] < b[2] and b[1] < a[2]


def isps(a):
    return a[0][0] == "P" and a[0][1:].isdigit()


def window(a):
    return a[0] in ("A", "D1") or a == ("A0", 0, WD)


def build(par, c):
    ops = []
    acc = {}
    tag = [0]
    CY, PCY, GA, SC = c["cy"], c["pe"], c["ga"], c["sc"]

    def sz(a):
        return (a[2] - a[1] + (a[3] if len(a) > 3 else 1) - 1) // (a[3] if len(a) > 3 else 1)

    def add(alts, rd, wr, after=(), lat=0.0, kind="c", pri=0.0, drop=0, move=0.0):
        if drop:
            del ops[-drop:]
            for lst in acc.values():
                while lst and lst[-1][0] >= len(ops):
                    lst.pop()
        else:
            alts = [(e, d * (c["f"] if kind == "c" else 1.0), em) for e, d, em in alts]
        o = {"n": len(ops), "alts": alts, "rd": rd, "wr": wr, "lat": lat, "move": move, "kind": kind, "pri": pri, "tag": tag[0]}
        dep = set(x["n"] for x in after)
        for a, w in [(a, 0) for a in rd] + [(a, 1) for a in wr]:
            if window(a):
                continue
            for (n, a2, w2) in acc.get(a[0], ()):
                if (w or w2) and meet(a, a2):
                    dep.add(n)
        for a, w in [(a, 0) for a in rd] + [(a, 1) for a in wr]:
            acc.setdefault(a[0], []).append((o["n"], a, w))
        o["dep"] = dep
        ops.append(o)
        return o

    def two(*aps):
        return all((not isps(a)) and SB[a[0]][1] in (BF, U16) for a in aps)

    def vc(n):
        return 50.0 + max(64, n) * CY

    def val(r, x):
        return r(x) if isinstance(x, tuple) else x

    def cols(*xs):
        return [x for x in xs if isinstance(x, tuple)]

    def tt(out, a, b, op):
        n = sz(out) * (1 if isps(a) or isps(b) else 2)
        return add([("v", vc(n), lambda q, T, r: [q.tensor_tensor(r(out), r(a), r(b), op)])], [a, b], [out])

    def ts(out, a, s1, s2, op0, op1=None):
        n = sz(out) * (0.5 if two(out, a) else 1)

        def em(q, T, r):
            if op1 is None:
                return [q.tensor_scalar(r(out), r(a), val(r, s1), None, op0)]
            return [q.tensor_scalar(r(out), r(a), val(r, s1), val(r, s2), op0, op1)]
        return add([("v", vc(n), em)], [a] + cols(s1, s2), [out])

    def cp(out, a):
        n = sz(out) * (0.5 if two(out, a) else 1)
        return add([("v", vc(n), lambda q, T, r: [q.tensor_copy(r(out), r(a))])], [a], [out])

    def ms(out, v, pri=0.0):
        n = sz(out) * (0.5 if two(out) else 1)
        return add([("v", vc(n), lambda q, T, r: [q.memset(r(out), v)])], [], [out], pri=pri)

    def scan(out, p, k):
        return add([("v", vc(sz(out)), lambda q, T, r: [q.tensor_tensor_scan(r(out), r(p), r(k), 0.0, OP.max, OP.min)])], [p, k], [out])

    def flex(out, a, bias=0.0, engs="sv", scale=1.0):
        n = sz(out)
        alts = {"s": ("s", 15.0 + vc(n), lambda q, T, r: [q.activation(r(out), r(a), AF.Identity, bias=val(r, bias), scale=val(r, scale))]),
                "v": ("v", vc(n), lambda q, T, r: [q.tensor_scalar(r(out), r(a), val(r, scale), val(r, bias), OP.mult, OP.add)])}
        return add([alts[e] for e in engs], [a] + cols(bias, scale), [out])

    def gat(out, win, off, engs="sv", after=(), scale=None, bias=0.0):
        n = sz(out)
        if scale is None:
            es = lambda q, T, r: [q.activation(r(out), r(win).indirect(r(off)), AF.Copy)]
            ev = lambda q, T, r: [q.tensor_copy(r(out), r(win).indirect(r(off)))]
        else:
            es = lambda q, T, r: [q.activation(r(out), r(win).indirect(r(off)), AF.Identity, bias=val(r, bias), scale=r(scale))]
            ev = lambda q, T, r: [q.tensor_scalar(r(out), r(win).indirect(r(off)), r(scale), val(r, bias), OP.mult, OP.add)]
        alts = [x for x in (("s", 65.0 + n * GA * CY, es), ("v", 50.0 + n * GA * CY, ev)) if x[0] in engs]
        return add(alts, [win, off] + cols(scale, bias), [out], after)

    def cmpg(out, off, z):
        return add([("v", 50.0 + sz(out) * GA * CY, lambda q, T, r: [q.tensor_tensor(r(out), r(("X", 0, W)).indirect(r(off)), r(z), OP.is_ge)])],
                   [("X", 0, W), off, z], [out])

    def scat(win, off, src, eng, after=(), src2=None):
        em = {"s": lambda q, T, r: [q.activation(r(win).indirect(r(off)), r(src), AF.Silu)],
              "v": lambda q, T, r: [q.tensor_copy(r(win).indirect(r(off)), r(src))]}
        if src2 is not None:
            em["v"] = lambda q, T, r: [q.tensor_tensor(r(win).indirect(r(off)), r(src), r(src2), OP.add)]
        return add([(e, 60.0 + sz(src) * SC * CY, em[e]) for e in ("sv" if eng == "s" else "v")], [off, src] + cols(src2), [win], after)

    def pe(groups, first=True, last=True, hold=None):
        cost, rd, wr = 60.0, [], [(hold, 0, 512)] if hold else []
        for grp in groups:
            for (o, l, x) in grp:
                cost += max(64, sz(x)) * PCY * (4 if SB[x[0]][1] == F32 else 1) + c["mm"]
                for lst, a in ((rd, l), (rd, x if x[0][0] == "K" else x[:3]), (wr, o[:4])):
                    if a not in lst:
                        lst.append(a)

        def em(q, T, r):
            res = []
            for grp in groups:
                for i, (o, l, x) in enumerate(grp):
                    res.append(q.matmul(r(o), r(l), r(x), first and i == 0, last and i == len(grp) - 1))
            return res
        return add([("t", cost, em)], rd, wr)

    def gp(n, em, rd, wr, pri=0.0, after=()):
        return add([("g", 200.0 + 2.3 * n * CY, em)], rd, wr, after, pri=pri)

    def iota(a, pat, base, cm, pri=0.0):
        return gp(sz(a), lambda q, T, r: [q.iota(r(a), pat, base, cm, allow_small_or_imprecise_dtypes=True)], [], [a], pri)

    def fill(a, v=0, engs="sv", pri=0.0):
        n, z = sz(a), ("ZN", 0, sz(a), 1) + a[4:]
        alts = {"s": ("s", 15.0 + vc(n), lambda q, T, r: [q.activation(r(a), r(z), AF.Identity, bias=float(v), scale=1.0)]),
                "v": ("v", vc(n * (0.5 if two(a) else 1)), lambda q, T, r: [q.memset(r(a), float(v))]),
                "g": ("g", 160.0 + 2.3 * n * CY, lambda q, T, r: [q.iota(r(a), [[0, n]], int(v), 0, allow_small_or_imprecise_dtypes=True)])}
        return add([alts[e] for e in engs], [z[:3]], [a], pri=pri)

    def zero(a, v=0):
        return fill(a, v, "gs")

    def copy(out, a):
        return gp(sz(a), lambda q, T, r: [q.affine_select(r(out), r(a), [[0, sz(a)]], OP.is_ge, 0.0, 0, 0)], [a], [out])

    def either(a, b):
        return add(copy(a, b)["alts"] + flex(a, b)["alts"], [b], [a], drop=2)

    def reset(h):
        return either(("LW", h, 1024, 2), ("LT", h, 1024, 2))

    def named(nm, *calls):
        for o in calls:
            o["nm"] = nm
        return list(calls)

    def dma(pairs, rd, wr, nbytes, after=(), q="y", pri=0.0, rows=128):
        return add([(q, 100.0 * len(pairs), lambda e, T, r: [e.dma_start(a(T), b(T)) for a, b in pairs])], rd, wr, after,
                   lat=c["dma"], move=nbytes / c["bw"] + rows * len(pairs) * c["row"], kind="d", pri=pri)

    def send(src, dst, k, after=()):
        s = add([("g", c["call"] + c["once"] * (k == 0), (src, dst, k))], [src], [], after, kind="s")
        return add([("n", 0.0, k)], [], [dst], [s], lat=500.0 + c["dma"], move=sz(src) * 256 / c["bw"] + 128 * c["row"], kind="r")

    def sel(buf, base, r):
        return (buf, base + 15 - r, base + 143 - r)

    def to_list(out, wide, zset):
        return [(out, sel("ZP", 144 * zset, r), (wide[0], wide[1] + r, wide[2], 16)) for r in range(16)]

    def b32(name, i, n=1):
        return (name, 32 * i, 32 * (i + n))

    def sub(a, i, n=1):
        s = a[3] if len(a) > 3 else 1
        return (a[0], a[1] + 32 * i * s, a[1] + 32 * (i + n) * s) + a[3:]

    def const(out, i):
        a = i if isinstance(i, tuple) else ("CR", 64 * i, 64 * i + sz(out))
        o = 0 if i in (4, 5, 6) else 128
        return (out, ("ONE", o, o + 128, 1, 1), a + (1, 1))

    ALL = 6
    IBM = lambda i: ("IB", 128 * i, 128 * i + 128)
    IP, IN, KP, KN = [("IF", 128 * i, 128 * i + 128) for i in range(4)]
    DUM, LDUM, UF = b32("ST", 0, 2), b32("ST", 2), b32("ST", 3)
    PC = lambda i: ("PF", i, i + 1)
    BA, M1, M2, B2 = PC(1), PC(2), PC(3), PC(4)
    CV, CG, CW, CQ = ("CR", 448, 608), ("CR", 608, 864), ("CR", 864, 992), ("CR", 928, 992)
    NE = lambda h, i, n=1: b32("NE", 6 * h + i, n)
    SR = lambda h, n=1: b32("R", 3 * h, n)
    R = lambda h, n=1: b32("R", 3 * h + 1, n)
    EM = lambda h: b32("EM", h)
    UW = lambda h, i, n=1: b32("UB", 5 * h + i, n)

    def blk(t):
        return 7 if t == 2 else 6

    def Kk(t, h, k):
        o = 7 - k
        return ("K%d" % (h + (2 if t == 2 else 0)), o, o + 64 * blk(t) - blk(t) + 1, blk(t))

    def Uu(t, h, k):
        o = (2 * (t % 2) + h) * 384 + 64 * (2 if k == 0 else k - 1 if k < 3 else k)
        return ("U", o, o + 64)

    def key(t, h, k, src, out=None, less=0.0):
        return flex(out or Kk(t, h, k), src, (WT[k] + less) * KEY, "sv", KEY)

    def spare(t, h):
        return t > 0 or h == 1

    def Uw(t, h):
        return Uu(t + 1, h, 0 if spare(t, h) else 1)

    dma([(lambda T: T.NS[:], lambda T: T.nsum[:])], [], [("NS", 0, 512)], 262144, pri=9.5e5)
    dma([(lambda T: T.RN[:, 0:64], lambda T: T.rho[:]), (lambda T: T.RN[:, 64:192], lambda T: T.nei[:])], [], [("RN", 0, 192)], 98304, q="s", pri=9e5)
    dma([(lambda T: T.D0[:, 0:1024], lambda T: T.dem[:, 0:1024])], [], [("D0", 0, 1024)], 262144, pri=8.5e5)
    dma([(lambda T: T.X[:, 0:2560], lambda T: T.x[:, 0:2560])], [], [("X", 0, 2560)], 655360, pri=8e5)
    for i in range(4):
        ops[i]["turn"] = i
    dma([(lambda T: T.X[:, 2560:W], lambda T: T.x[:, 2560:W])], [], [("X", 2560, W)], 1441792, pri=8e5)["turn"] = 3.6
    dma([(lambda T: T.D0[:, 1024:2048], lambda T: T.dem[:, 0:1024])], [], [("D0", 1024, 2048)], 262144)["turn"] = 3.7
    ms(("ZN", 0, 768), 0.0, 9e5)
    ms(("ONE", 0, 128), 1.0, 9e5)
    ms(("ZP", 0, 1008), 0.0, 9e5)
    for i in range(16):
        fill(("A0", 512 * i, 512 * i + 512), 32768, "vs" if i < par["fill"] else "sv", 7.5e5)

    def diag(out, src, pat, fill, base, cm=1):
        return gp(sz(out), lambda q, T, r: [q.affine_select(r(out), r(src), pat, OP.not_equal, fill, base, cm)], [src], [out])

    def band(out, src, pat, base, cm):
        return gp(sz(out), lambda q, T, r: [q.affine_select(r(out), r(src), pat, OP.is_ge, 0.0, base, cm)], [src], [out])

    z128 = ("ZN", 0, 128)
    diag(IP, z128, [[-1, 128]], 1.0, 0)
    diag(IBM(8), z128, [[-1, 128]], -1.0, 0)
    ts(("NH", 0, 512), ("NS", 0, 512), 64.0, None, OP.add)["pri"] = 6e5
    tt(("NM", 0, 512), ("NS", 0, 512), ("NH", 0, 512), OP.subtract)["pri"] = 6e5
    gp(1, lambda q, T, r: [q.iota(r(("PI", 0, 1)), [[0, 1]], 0, 1)], [], [("PI", 0, 1)])
    ts(("PI", 1, 2), ("PI", 0, 1), 15, None, OP.bitwise_and)
    cp(PC(0), ("PI", 1, 2))
    ts(PC(5), PC(0), 1.0, 128.0, OP.is_equal, OP.mult)
    ts(PC(11), PC(0), 2.0, 32768.0, OP.is_equal, OP.mult)
    flex(BA, PC(5), PC(11))
    for i in range(3):
        fill(("ZS", 768 * i, 768 * i + 768), 0, "vgs")
    zs = ("ZS", 15, 2304, 16)
    diag(zs, zs, [[-1, 16], [-16, 9]], 1.0, 0)
    flex(("NM", 0, 512), ("NM", 0, 512), 128.0)["pri"] = 7e5
    dma([(lambda T: T.A0[0:128:16, 0:W], lambda T: T.NH[:]), (lambda T: T.A0[1:128:16, 0:W], lambda T: T.NM[:])],
        [("NH", 0, 512), ("NM", 0, 512)], [("A0", 0, W)], 262144, pri=6e5)["turn"] = 3.5

    for h in range(2):
        for b in range(2):
            diag(("DN2", 128 * (2 * h + b), 128 * (2 * h + b + 1)), z128, [[-16, 8], [1024, 2], [-2, 8]], 1.0, -h - 1024 * b)["pri"] = 6.5e5
    zp6, zp0, zpa = ("ZP", 15, 864, 16), ("ZP", 15, 144, 16), ("ZP", 879, 1008, 16)
    band(zp6, ("ONE", 0, 54), [[-2, 6], [-16, 9]], 0, 1)
    band(zp6, zp6, [[2, 6], [16, 9]], 1, -1)
    diag(zp0, zp0, [[-16, 9]], -2.0 ** -8, -2)
    for i, row, s in ((2, 10, -BIG), (4, 10, -BIG), (1, 1, 1.0)):
        a = ("ZP", 144 * i + 15, 144 * i + 144, 16)
        diag(a, a, [[-16, 9]], s, -row)
    ms(("EM", 0, 9), 2.0)
    band(zpa, ("EM", 0, 9), [[-16, 9]], 0, 1)
    band(zpa, zpa, [[16, 9]], 15, -1)
    for i, s in ((1, -1.0), (2, 1 / KEY), (3, -1 / KEY)):
        flex(("IF", 128 * i, 128 * i + 128), IP, 0.0, "sv", s)
    for i, s in ((1, -BIG), (2, BIG), (4, -1024.0), (6, -8 * 65536.0), (7, 1.0)):
        flex(IBM(i), IP, 0.0, "sv", s)
    flex(("IB", 640 + 16, 768), ("IF", 0, 112), 0.0, "sv", -2048.0)
    flex(("IB", 640, 640 + 16), ("IF", 112, 128), 0.0, "sv", -2048.0)
    fill(("ONE", 128, 256, 1, 1), 65536, "gsv")
    iota(("CR", 0, 256), [[-1, 4], [0, 64]], 4, 0)
    iota(("CR", 256, 448), [[16, 3], [0, 64]], -17, 0)
    fill(("CR", 448, 576, 1, 1), 0, "gsv")
    fill(("CR", 576, 608, 1, 1), -128.0 / 65536.0)
    fill(("CR", 864, 928, 1, 1), 0, "gsv")
    fill(CQ + (1, 1), 0.25)
    for o, n_, v in ((0, 128, 0.25), (128, 64, -4.0), (192, 64, -3.0), (256, 64, 0.0), (352, 32, 0.4375),
                     (384, 64, 0.25), (448, 64, -1 / 64), (512, 64, -4.0), (576, 64, 1.0), (640, 96, 0.0), (736, 32, 0.4375)):
        fill(("CE", o, o + n_, 1, 1), v)
    fill(CG + (1, 1), int(MAGIC) // 65536, "gsv")
    for h in range(2):
        fill(("K%d" % h, 0, 386, 385), 0, "gsv")
        fill(("K%d" % (2 + h), 0, 450, 7), 0, "gsv")
        fill(("K%d" % (2 + h), 1, 450, 7), WT[6] * KEY)
    iota(b32("ST", 4), [[16, 32]], 0, 0)
    ts(M1, PC(0), 6.0, None, OP.is_lt)
    ts(PC(9), PC(0), 6.0, None, OP.is_ge)
    ts(M2, PC(0), 10.0, PC(9), OP.is_lt, OP.mult)
    ts(B2, PC(0), 10.0, -1.0, OP.is_equal, OP.mult)
    ts(PC(8), ("PI", 0, 1), PC(0), -512.0, OP.subtract, OP.mult)
    flex(UF, b32("ST", 4), PC(0))
    flex(("CE", 320, 352, 1, 1), b32("ST", 4) + (1, 1), 0.0, "sv", 1 / 32768)
    for h in range(2):
        flex(PC(6 + h), PC(0), float(h + 1024 * (h + 1)), "sv", 2.0)
    for s in range(2):
        flex(sub(DUM, s), UF, float(W))
    flex(LDUM, UF, 1024.0 - BIG)
    iota(PC(10), [[0, 1]], 1, 0)
    gp(1, lambda q, T, r: [q.affine_select(r(PC(10)), r(PC(10)), [[0, 1]], OP.is_ge, -1.0, 31, -1)], [PC(10)], [PC(10)])

    cp(("TM", 0, 192), ("RN", 0, 192))["pri"] = 6.5e5
    for h in range(2):
        bk = "P%d" % (4 + h)
        mv = lambda o, a, n: [((bk, o, o + n), ("DN2", 128 * (2 * h + b), 128 * (2 * h + b + 1)), ("TM", a + b, a + 2 * n, 2)) for b in range(2)]
        pe([mv(64, 0, 96)])["pri"] = 6.5e5
        pe([mv(32, 0, 32), mv(0, 64, 32) + mv(0, 128, 32)])
        cp(Uu(0, h, 1), (bk, 96, 160))
        key(0, h, 1, (bk, 96, 160))
        flex(SR(h, 3), (bk, 0, 96))
        cp(b32("RU", h), R(h))
        key(2, h, 0, R(h, 2))
    send(("D0", 0, 1024), ("ZW1", 1024, 2048), 0)["turn"] = 8

    def rotate(z):
        dma([(lambda T: T[z][16:128, 2048:3072], lambda T: T[z][0:112, 1024:2048]), (lambda T: T[z][0:16, 2048:3072], lambda T: T[z][112:128, 1024:2048])],
            [(z, 1024, 2048)], [(z, 2048, 3072)], 262144)
    rotate("ZW1")

    tag[0] = 22
    dma([(lambda T: T.KD[:], lambda T: T.kid[:])], [], [("KD", 0, 512)], 262144)["turn"] = 4
    cp(("WS", 0, 512), ("KD", 0, 512))
    flex(("G1", 0, 512), ("WS", 0, 512))
    pe([[(("P7", 0, 512), IP, ("WS", 0, 512)), (("P7", 0, 512), IBM(8), ("G1", 0, 512))]])
    flex(("G2", 0, 512), ("P7", 0, 512))
    add([("s", 15.0 + vc(512), lambda q, T, r: [q.activation(T.LW[:, 1024:1536], T.WS[:, 0:512], AF.Relu, bias=0.0, scale=-2048.0)])],
        [("WS", 0, 512)], [("LW", 1024, 1536)])
    iota(("WS", 512, 1024), [[32, 16], [0, 32]], 0, 512)
    flex(("GR", 0, 512), ("WS", 512, 1024), PC(8))
    iota(("GX", 0, 512), [[0, 16], [1, 32]], 0, 0)
    dma([(lambda T, i=i: T.KW[i:128:16, :], lambda T, j=j: T.A0[j:128:16, 0:W]) for i, j in ((6, 0), (7, 1), (0, 2), (11, 3), (12, 4), (13, 5), (14, 6), (15, 7))],
        [("A0", 0, W)], [("KW", 2, 3)], 1048576, rows=16)["turn"] = par["kw"][2]
    for j, rows in enumerate(([(4, "GR", 0), (5, "GX", 0), (8, "GR", 0), (9, "GX", 0), (10, "ZN", 0)], [(1, "LW", 1024), (2, "G1", 0), (3, "G2", 0)])):
        dma([(lambda T, i=i: T.KW[i:128:16, :], lambda T, n=n, o=o: T[n][:, o:o + 512]) for i, n, o in rows], [(n, o, o + 512) for _, n, o in rows],
            [("KW", j, j + 1)], 131072 * len(rows))["turn"] = par["kw"][j]
    for i in (1, 2):
        dma([(lambda T, i=i: T["ZW%d" % i][:, 0:1024], lambda T, i=i: T.dem[:, 1024 * i:1024 * i + 1024])], [], [("ZW%d" % i, 0, 1024)], 262144)["turn"] = 8 + i
    hh, ll = b32("H5", 0, 2), b32("L5", 0, 2)
    flex(hh, ("TM", 0, 64))
    tt(ll, ("TM", 0, 64), hh, OP.subtract)
    for b in range(2):
        bk = "P%d" % (2 + b)
        for j in range(0, 8, 4):
            pe([[((bk, i, 512, 8), sel("ZS", 144 * (2 * i + b), row), a) for a, row in ((hh, 4), (ll, 5), (hh, 8), (ll, 9))] for i in range(j, j + 4)])
        flex(("LT", b, 1024, 2), (bk, 0, 512))
    reset(1)
    tag[0] = 24
    ia = [either(("A", 512 * i, 512 * i + 512), ("A0", 512 * i, 512 * i + 512)) for i in range(16)]
    for i in range(3):
        zero(("RW", 512 * i, 512 * i + 512))
    tag[0] = 23
    zero(("NLF", 0, 512), 32768)
    idl = dma([(lambda T: T.D1[0:128:16, 0:W], lambda T: T.NLF[:])], [("NLF", 0, 512)], [("D1", 0, W)], 262144)
    zero(("WT", 0, 768), 32768)
    add([("s", 1400.0 + vc(256), lambda q, T, r: [q.activation(T.WT[:, 768:1024], T.ZN[:, 0:256], AF.Silu, bias=32768.0, scale=1.0)])],
        [("ZN", 0, 256)], [("WT", 768, 1024)], pri=6e5)
    zero(("TB", 0, 64), 64)
    dma([(lambda T: T.WT[1:128:16, :], lambda T: T.TB[:, 0:64])], [("TB", 0, 64)], [("WT", 0, 1024)], 32768)

    turn, staged = [0, 0], []

    def write(nm, lists, off, win, after, stage=None, banks=None, behind=()):
        n = sz(lists[0][0]) // 32
        if stage is None:
            turn[1] ^= 1
            stage = ("WS", 1024 * turn[1], 1024 * turn[1] + 512 * n)
        for b in range(n):
            turn[0] ^= 1
            bk = banks[b] if banks else "P%d" % (6 + turn[0])
            rs = list(range(b, 16, n))
            grp = [[((bk, i, 512, len(rs)), sel("ZS", 144 * r, row), a) for a, row in lists] for i, r in enumerate(rs)]
            per = 16 // len(lists)
            for i in range(0, len(grp), per):
                staged.append(pe(grp[i:i + per]))
                staged[-1]["dep"].update(x["n"] for x in behind)
            named("s" + nm, flex(stage if n == 1 else (stage[0], stage[1] + b, stage[2], 2), (bk, 0, 512), {"A": BA, "D1": 32768.0, "A0": 0.0}[win]))
        return [named("a%s%d" % (nm, b), scat((win, 0, WD), sub(off, b), stage if n == 1 else sub(stage, 16 * b, 16), "v" if win == "A0" else "s", after))[0]
                for b in range(n)]

    def turned(terms, n, bias, scale, stage, row, bk):
        o, tb = (bk, 0, 128, 1, n), ("TB", 128, 256, 1, n)
        pe([[((bk, 0, 128, 1, sz(a)), a, m) for a, m in terms]])
        flex(tb, o, bias, "sv", scale)
        return dma([(lambda T, g_=g_: T[stage][16 * g_ + row, 0:16 * n], lambda T, g_=g_: T.TB[0:n, 128 + 16 * g_:144 + 16 * g_]) for g_ in range(8)],
                   [tb], [(stage, 0, 16 * n)], 512 * n, rows=n)

    aw, pw, d1w, d2w, clear = {-1: ia}, {-1: []}, [], [], []

    def delta(nm, hh, ll, off, eng, banks=None):
        if eng == "s":
            d2w.extend(write(nm, [(hh, 0), (ll, 0)], off, "D1", [idl], None, banks))
        else:
            d1w.extend(write(nm, [(hh, 0), (ll, 1)], off, "A0", clear, None, banks))

    def walks(t, h):
        isp = h == t % 2
        old = t == 0 or (t == 1 and isp)
        win = ("A0", 0, W) if old else ("A", 0, W)
        after = [] if old else aw[0] if isp else aw[t - 1]
        sb, pb, n = "P%d" % h, "P%d" % (2 + h), blk(t)
        zb = "Z1" if t == 1 else "D0"
        slot = lambda k: (pb, 6 - k, 64 * n, n)
        nm = lambda k: "%d%s%d" % (t, "QP"[isp], k)
        for k in range(1, 6):
            if (k > 1 or t == 0) and (k < 5 or t < 2 or isp):
                m = 1 if t == 2 and k == 5 else 2
                o_ = 2048 * h + 1024 * (k % 2)
                g_ = ("GS", o_, o_ + 512 * m)
                sp = (sb, 448 * (k % 2), 448 * (k % 2) + 32 * m)
                m_ = 1 if par["half"][2 * t + (not isp)] else m
                for i in range(m // m_):
                    named("w" + nm(k), gat(sub(g_, 16 * i, 16 * m_), win, sub(Uu(t, h, k), i, m_), "sv", after))
                test = t > 0 and k < 4
                less = WT[k - 1] if k > 1 and not test else 0.0
                prev = [(sp, KN, sub(Kk(t, h, k - 1), 0, m))] + ([const(sp, k - 2)] if test else []) if k > 1 else [(sp, IN, R(h, 2))]
                if t > 0 and k < 5:
                    prev.append((sub(sp, 0), IBM(6), b32("OV", 3 * h + k - 2)))
                pe([to_list(sp, g_, 0) + prev])
                if k < 5:
                    ts(Uu(t, h, k + 1), sp, less, float(W - 1), OP.add, OP.min)
                key(t, h, k + 1, sp, sub(Kk(t, h, k + 1), 0, m), less)
                if test:
                    tt(b32("OV", 3 * h + k - 1), sub(sp, 0), NE(h, 1), OP.is_equal)
            c_ = 2048 * h + 1024 * (k % 2)
            if k > par["dup"]:
                named("c" + nm(k), cmpg(("CM", c_, c_ + 1024), Uu(t, h, k), (zb, h, 2048, 2)))
            else:
                for s in range(2):
                    named("c" + nm(k) + "ab"[s], cmpg(("CM", c_ + 512 * s, c_ + 512 * s + 512), sub(Uu(t, h, k), s), (zb, h, 1024, 2)))
            stop = [b32("SP", j) for j in range(t) if j % 2 != h]
            ends = [[const(slot(6), 6)]] + ([[const(slot(0), 5)]] if t == 2 else []) if k == 1 else []
            pe([to_list(slot(k), ("CM", c_, c_ + 1024), ALL) + [const(slot(k), 4)] + [(sub(slot(k), 0), IBM(1), a) for a in stop]] + ends)

    def embed(t, h):
        isp = h == t % 2
        sb, pb, n = "P%d" % h, "P%d" % (2 + h), blk(t)
        kb, sc = Kk(t, h, 1)[0], "SC%d" % h
        lo, hi, lw, fs = (sb, 64, 192), (sb, 192, 320), (sb, 320, 384), (sb, 384, 416)
        pe([[const((sb, 64, 448), ("CE", 384 * (t == 2), 384 * (t == 2) + 384))] + [(lw, IP, DUM)] * spare(t, h)
            + [(sub(hi, 2 * i, 2), KP, Kk(t, h, 1 + i)) for i in range(2 if t < 2 else 1)]], True, False, sb)
        m = 64 * n
        scan((sc, 0, m), (pb, 0, m), (kb, 1, m + 1))
        o = 2 if t == 2 else 0
        scan((sc, m, 2 * m), (pb, 0, m), (kb, o, m + o))
        nf = 4
        if t == 2 and isp:
            scan((sc, 2 * m, 2 * m + m // 2), (pb, 0, m // 2), (kb, 0, m // 2))
            nf = 5
        fin = (sc, 5, 5 + 32 * nf * n - n + 1, n)
        wn = b32("MN", 5 * h, nf)
        tt(b32("E", 2 * h + 1), sub(fin, 0), sub(fin, 1), OP.min)
        for i, j in ((0, 2), (2, nf - 2)) if par["cut"][isp] else ((0, nf),):
            ts(sub(wn, i, j), sub(fin, i, j), 1 / KEY, None, OP.mult)
            ts(sub(wn, i, j), sub(wn, i, j), W - 1, None, OP.bitwise_and)
        nu = nf if nf == 5 else 3 if isp else 2
        cp(UW(h, 0, nu), sub(wn, 0, nu))
        tt(b32("E", 2 * h), sub(wn, 0), sub(wn, 1), OP.is_equal)
        tt(EM(h), b32("E", 2 * h), b32("E", 2 * h + 1), OP.is_le)
        ns, nw = 4 if t < 2 else 2, 2 if spare(t, h) else 0
        parts = ((lo, 1, ns), (hi, 2, ns), (lw, 1, nw), ((sb, 416, 448), 1, not isp))
        pe([[(fs, IBM(4 + h), EM(h))] * (t < 2) + [(sub(a, i), IBM(j), EM(h)) for a, j, n_ in parts for i in range(n_)]], False, True, sb)
        if t < 2:
            ts(b32("FS", 2 * t + h), fs, PC(6 + h), None, OP.add)
            send(b32("FS", 2 * t + h), b32("FO", 2 * t + h), 2 + 2 * t + h)
        tt(b32("TM", 4 * h, 4), lo, sub(wn, 0, 4), OP.max)
        tt(NE(h, 0, 4), hi, b32("TM", 4 * h, 4), OP.min)
        if nw:
            tt(NE(h, 4, 2), lw, sub(wn, 0, 2), OP.max)
        u1 = Uu(t + 1, h, 1)
        i, j = (4, 6) if t == 2 else (0, 6 if nw else 2)
        cp(("U", u1[1] + 32 * i, u1[1] + 32 * j), NE(h, i, j - i))
        if t < 2:
            key(t + 1, h, 1, NE(h, 0, 2))
            if not isp:
                key(t + 1, h, 2, NE(h, 2, 2))
                tt(b32("OV", 3 * h), NE(h, 2), NE(h, 1), OP.is_equal)
            za, zc = [("D0" if t else "Z1", o_ + h, o_ + 1024, 2) for o_ in (0, 1024)]
            named("Z%d%s" % (t + 1, "PQ"[isp]), gat(za, ("ZW%d" % (t + 1), 0, 3072), b32("FO", 2 * t + h)))
            copy(zc, za)

    def told(out, st, h):
        return [(out, sel("ZP", 144 * st, r), ("LW", 2 * r + h, 1024, 32)) for r in range(16)]

    def digits(hh, ll, src):
        flex(hh, src, 64.0)
        tt(ll, src, hh, OP.subtract)

    def parents(t):
        h = t % 2
        q_ = 1 - h
        named("G%d" % t, gat(("G1", 0, 512), ("KW", 0, W), UW(h, 0), scale=M1),
              gat(("G2", 0, 512), ("KW", 0, W), UW(h, 2 if t < 2 else 4), scale=M2, bias=B2))
        kb = ("P%d" % (2 + h), 448, 480)
        pe([to_list(kb, ("G1", 0, 512), 1)], True, False, kb[0])
        pe([[(kb, IBM(1), EM(h))]], False, True, kb[0])
        tt(b32("PT", 0), kb, LDUM, OP.min)
        ts(b32("LO", t), b32("PT", 0), BIG, None, OP.add)
        named("LW%d" % t, scat(("LW", 0, 1536), b32("LO", t), ("G1", 0, 512), "v", src2=("G2", 0, 512)))
        for i, st in enumerate((4, 2)):
            pe([told(("P4", 32 * i, 32 + 32 * i), st, q_)])
        flex(b32("LI", 0, 2), ("P4", 0, 64))
        tag[0] += 1
        if t < 2:
            tt(b32("PT", 1), NE(h, 2), NE(h, 1), OP.is_equal)
        else:
            turned([(NE(h, 1, 3), IP), (NE(h, 0), IP), (SR(h, 3), IN)], 96, 32768.0, PC(10) + (1, 96), "RW", 0, "P%d" % h)
            for i, off in enumerate((b32("RU", h), sub(Uw(2, h), 0), sub(Uw(2, h), 1))):
                d2w.extend(named("d", scat(("D1", 0, WD), off, ("RW", 512 * i, 512 * i + 512), "s", [idl])))

    def children(t):
        h = 1 - t % 2
        p_ = 1 - h
        Q = lambda i, n=1: b32("Q", i, n)
        li = lambda i, n=1: b32("LI", i, n)
        cb, spl = ("P%d" % (2 + h), 448, 480), b32("SP", t)
        named("GX%d" % t, gat(("GX", 0, 512), ("X", 0, W), UW(h, 1)))
        named("CK%d" % t, cmpg(("GR", 0, 512), UW(h, 0), ("GX", 0, 512)))
        tt(spl, li(0), ("P%d" % h, 416, 448), OP.is_gt)
        pe([to_list(cb, ("GR", 0, 512), ALL) + [(cb, IBM(2), spl)]])
        t3 = lambda i, n=1: ("P4", 160 + 32 * i, 160 + 32 * (i + n))
        dif = lambda o, a, b: [(o, IP, a), (o, IN, b)]
        cross = lambda o: [(o, IP, NE(h, 0, 2)), (sub(o, 0), IN, li(1)), (sub(o, 1), IN, li(0))]
        nq = 1 if t < 2 else 2
        pe([dif(t3(0), NE(h, 0), NE(h, 1))])
        pe([dif(t3(1), li(1), li(0))])
        if t < 2:
            pe([cross(t3(2, 2)) + [const(t3(2, 2), CQ)]])
        pe([[(t3(4, nq), IP, sub(DUM, 0, nq)), const(t3(4, nq), sub(CQ, 0, nq))] + [(t3(4 + i), IBM(6), spl) for i in range(nq)]])
        tt(Q(1, nq), t3(4, nq), li(0, nq), OP.max)
        ts(b32("QO", 0, nq), Q(1, nq), -BIG, None, OP.add)
        v = lambda i, n=1: ("P5", 32 * i, 32 * (i + n))
        pe([[const(v(0, 5), CV)] + told(v(4), 3, h) if t < 2 else [const(v(0, 4), CW)]], True, False, "P5")
        pe([[(v(0, 2), IP, li(0, 2)), (v(0), IBM(1), spl), (v(1), IBM(1), spl)]], False, False, "P5")
        if t < 2:
            reset(p_)
            for i, j in ((4, 2), (5, 3)):
                tt(Q(i), t3(j), spl, OP.mult)
            pe([[(v(0, 2), IP, NE(h, 2, 2)), (v(2, 2), IP, Q(4, 2)), (v(4), IP, Q(4))]], False, False, "P5")
        else:
            pe([[(v(0, 2), IN, NE(h, 2, 2))] + cross(v(2, 2))], False, False, "P5")
        ts(Q(6), cb, 17.0 + BIG, None, OP.is_ge)
        tt(Q(7), t3(1), Q(6), OP.mult)
        tt(Q(8), t3(0), Q(6), OP.mult)
        pe([[(v(0), IP, Q(7)), (v(1, 2), IN, Q(7, 2)), (v(3), IP, Q(8))] + ([(v(4), IN, Q(8))] if t < 2 else [])], False, True, "P5")
        nv_ = 5 if t < 2 else 4
        digits(b32("H5", 0, nv_), b32("L5", 0, nv_), v(0, nv_))
        hl = lambda i, row: [(b32("H5", i), row), (b32("L5", i), row + 1)]
        if t == 2:
            delta("3b", b32("H5", 2, 2), b32("L5", 2, 2), ("QO", 0, 64), "v")
            delta("3n", b32("H5", 0, 2), b32("L5", 0, 2), Uw(2, h), par["last"][1], ("P5", "P4"))
            ts(b32("LV", 0), b32("SP", 1), 0.0, None, OP.is_equal)
            tt(b32("LV", 1), b32("SP", 0), spl, OP.is_equal)
            return
        aft = aw[-1] + pw[t - 1]
        aw[t] = write("%dn" % (t + 1), [(b32("H5", 0, 2), 0), (b32("L5", 0, 2), 1)], Uw(t, h), "A", aft)
        wb = write("%db" % (t + 1), hl(4, 0) + hl(3, 4) + hl(2, 6), b32("QO", 0), "A", aft, ("RW", h, 1024, 2), ("P5",), staged[-2:])
        aw[t] += wb
        tag[0] += 1
        sb = "P%d" % p_
        named("GR%d" % (t + 1), gat(("GR", 0, 512), ("RW", 0, 1536), b32("LO", t)))
        if t == 0:
            zero(("RW", h, 1024, 2))
        pe([to_list((sb, 128, 160), ("GR", 0, 512), 3)])
        tt(b32("PT", 2), (sb, 128, 160), b32("PT", 1), OP.mult)
        pe([[((sb, 0, 64), IP, NE(p_, 2, 2))] + to_list((sb, 0, 32), ("GR", 0, 512), 2)], True, False, sb)
        pe([[((sb, 32, 64), IP, b32("PT", 2))]], False, True, sb)
        ts(Uu(t + 1, p_, 2), (sb, 0, 64), float(W - 1), None, OP.min)
        key(t + 1, p_, 2, (sb, 0, 64))
        tt(b32("OV", 3 * p_), (sb, 0, 32), NE(p_, 1), OP.is_equal)
        tag[0] = 25
        turned([(Kk(t + 1, p_, 2), KP), (R(p_, 2), IP)], 64, 64.0 - WT[2], 1.0, "WT", 0, "P4")
        pw[t] = named("p%d" % (t + 1), *[scat(("A", 0, WD), sub(Uw(t, p_), i), ("WT", 512 * i, 512 * i + 512), "s", wb) for i in range(2)])

    fb = lambda i: ("P%d" % (2 * i), 256, 512)
    cs = lambda nm, i: (nm, 256 * i, 256 * i + 256)
    for t in range(3):
        p_ = t % 2
        tag[0] = 1 + 7 * t
        walks(t, p_)
        tag[0] += 1
        walks(t, 1 - p_)
        tag[0] += 1
        embed(t, p_)
        if t == 2:
            dma([(lambda T: T.NHF[:], lambda T: T.A[0:128:16, 0:W]), (lambda T: T.NLF[:], lambda T: T.A[1:128:16, 0:W])],
                [("A", 0, W)], [("NHF", 0, 512), ("NLF", 0, 512)], 524288, aw[1] + pw[1])
            zero(("NH", 0, 512))
            clear.append(dma([(lambda T, i=i: T.A0[i:128:16, 0:W], lambda T: T.NH[:]) for i in range(2)], [("NH", 0, 512)], [("A0", 0, W)], 262144))
        parents(t)
        if t == 2:
            for i in range(2):
                pe([[(fb(i), IP, cs("NHF", i)), (fb(i), IP, cs("NLF", i)), const(fb(i), CG)]], True, False, fb(i)[0])
        tag[0] += 1
        embed(t, 1 - p_)
        if t == 2:
            o = ("P1", 0, 32)
            pe([[(o, IP, NE(1, 0)), (o, IP, NE(1, 1)), (o, IN, SR(1))]])
            digits(b32("H5", 4), b32("L5", 4), o)
            delta("3r", b32("H5", 4), b32("L5", 4), b32("RU", 1), par["last"][0])
        tag[0] += 1
        children(t)
        if t == 0:
            tag[0] = 23
            send(("Z1", 0, 1024), ("ZW2", 1024, 2048), 1)
            rotate("ZW2")

    tag[0] = 21
    for nm, n, bk, ob in (("yn", 64, "P1", "SC0"), ("yl", 32, "P3", "TM")):
        for h in range(2):
            o = (bk, 256 + 128 * h, 384 + 128 * h, 1, n)
            pe([[(o, NE(h, 0, 2), IP) if nm == "yn" else (o, b32("LV", h), IBM(2))]])
            flex((ob, h, 256, 2, n), o, 0.0, "sv", 1.0 if nm == "yn" else 1 / BIG)
        dma([(lambda T, g_=g_, nm=nm: T[nm][g_, :], lambda T, g_=g_, n=n, ob=ob: T[ob][0:n, 32 * g_:32 * g_ + 32]) for g_ in range(8)], [(ob, 0, 256)], [], 1024 * n, rows=n)
    dma([(lambda T: T.DN2[:], lambda T: T.D1[0:128:16, 0:W])], [("D1", 0, W)], [("DN2", 0, 512)], 262144, d2w, q="s")
    dma([(lambda T: T.NH[:], lambda T: T.A0[0:128:16, 0:W]), (lambda T: T.NM[:], lambda T: T.A0[1:128:16, 0:W])],
        [("A0", 0, W)], [("NH", 0, 512), ("NM", 0, 512)], 262144, d1w)
    for i in range(2):
        pe([[(fb(i), IP, cs("DN2", i))]], False, False, fb(i)[0])
        pe([[(fb(i), IBM(7), cs("NH", i)), (fb(i), IBM(7), cs("NM", i))]], False, True, fb(i)[0])
        flex(cs("NLF", i), fb(i), -MAGIC - 32896.0)
    dma([(lambda T: T.ys[:], lambda T: T.NLF[:])], [("NLF", 0, 512)], [], 262144)
    return ops


def links(ops):
    pred, above = [], []
    for o in ops:
        far = 0
        for d in o["dep"]:
            far |= above[d]
        pred.append(sorted(d for d in o["dep"] if not far >> d & 1))
        for d in o["dep"]:
            far |= 1 << d
        above.append(far)
    succ = [[] for _ in ops]
    for i, p in enumerate(pred):
        for d in p:
            succ[d].append(i)
    return pred, succ


def queues(par):
    v = ["c0P1a", "c0P1b", "c0Q1a", "c0Q1b", "c0P2", "c0P3", "c0P4", "c0Q2", "c0P5", "c0Q3", "c0Q4", "c0Q5", "LW0"]
    s = ["w0%s%d" % (h, k) for k in range(1, 6) for h in "PQ"] + ["G0", "Z1Q", "GX0"]
    for t in (1, 2):
        v += ["c%dQ1a" % t] * (t > 1) + ["CK%d" % (t - 1)] + ["c%dQ1a" % t] * (t == 1)
        v += [x % t for x in ("c%dQ1b", "c%dP1a", "c%dP1b", "c%dP2", "c%dP3", "c%dP4", "c%dP5", "c%dQ2", "c%dQ3", "LW%d", "c%dQ4", "c%dQ5")]
        s += [x % t for x in ("w%dP2", "Z%dP", "w%dP3", "s%dn", "w%dP4", "a%dn0", "s%db", "GR%d", "a%dn1", "w%dP5", "a%db0", "w%dQ2", "w%dQ3", "G%d", "w%dQ4")]
        s += ["Z2Q", "w1Q5", "p1", "GX1"] if t == 1 else ["p2", "GX2", "d", "s3r", "a3r0", "s3n", "a3n0", "a3n1"]
    return {"v": v + ["CK2", "s3b", "a3b0", "a3b1"], "s": s}


def first_order(ops, par, c):
    n = len(ops)
    pred, succ = links(ops)
    early = sorted((o["turn"], o["n"]) for o in ops if "turn" in o)
    tail = [0.0] * n
    for i in reversed(range(n)):
        tail[i] = ops[i]["alts"][0][1] + ops[i]["lat"] + ops[i]["move"] + c["hop"] + max([tail[j] for j in succ[i]] + [0.0])
    line, turn, queue = {}, {}, {}
    for e, names in queues(par).items():
        line[e] = [o["n"] for nm in names for o in ops if o.get("nm") == nm]
        turn[e] = 0
        queue.update((i, e) for i in line[e])
    left = [len(p) for p in pred]
    rdy = [0.0] * n
    free, lock, out = {e: 0.0 for e in "vstgyn"}, {}, []
    ready = [i for i in range(n) if not left[i]]
    while ready:
        best = None
        for i in ready:
            o = ops[i]
            if i in queue and line[queue[i]][turn[queue[i]]] != i or o["move"] and early and early[0][1] != i:
                continue
            for a in o["alts"]:
                e = a[0]
                if queue.get(i, e) != e or (e == "v" and a is not o["alts"][0] and i not in queue and rdy[i] > par["head"]):
                    continue
                s = max([rdy[i], free[e] * (e != "n")] + [lock.get((x[0], k), 0.0) for x in o["rd"] + o["wr"] if isps(x) for k in "vst" if k != e]
                        + [lock.get((x[0], 1), 0.0) for x in o["rd"] + o["wr"] if window(x)] + [lock.get((x[0], 0), 0.0) for x in o["wr"] if window(x)])
                f = (s - par["pull"] * (tail[i] + o["pri"]), i)
                if best is None or f < best[0]:
                    best = (f, i, a, s)
        _, i, a, s = best
        o, e = ops[i], a[0]
        end = s + a[1]
        if o["move"]:
            end = free["n"] = max(end, free["n"]) + o["move"]
        end += o["lat"] + c["hop"]
        if e != "n":
            free[e] = s + a[1]
        for x, w in [(x, 0) for x in o["rd"]] + [(x, 1) for x in o["wr"]]:
            if isps(x) or window(x):
                k = (x[0], e if isps(x) else w)
                lock[k] = max(lock.get(k, 0.0), end)
        if i in queue:
            turn[e] += 1
        out.append((i, a, s, end - c["hop"]))
        ready.remove(i)
        if "turn" in o:
            early.pop(0)
        for j in succ[i]:
            rdy[j] = max(rdy[j], end)
            left[j] -= 1
            if not left[j]:
                ready.append(j)
    return out


def anneal(sets, weights, hops, start, seed, moves, temp, lam, mu, lo=0.0, hi=1.0):
    ops = sets[0]
    n = len(ops)
    pred, succ = links(ops)
    eng = {e: k for k, e in enumerate("vstgyn")}
    table = [[] for _ in sets]
    for i, o in enumerate(ops):
        rows = [[] for _ in sets]
        for ai, a in enumerate(o["alts"]):
            e = eng[a[0]]
            need, mark = ([n + e] if e < 5 else []) + pred[i], []
            for nm in sorted(set(x[0] for x in o["rd"] + o["wr"] if isps(x) or window(x))):
                if isps((nm,)):
                    b = n + 6 + 3 * int(nm[1:])
                    need += [b + k for k in range(3) if k != e]
                    mark.append(b + e)
                else:
                    b = n + 30 + 2 * ("A", "D1", "A0").index(nm)
                    w = any(x[0] == nm for x in o["wr"])
                    need += [b, b + 1] if w else [b + 1]
                    mark.append(b + w)
            for m, s in enumerate(sets):
                rows[m].append((n + e, need, mark, s[i]["alts"][ai][1], s[i]["lat"] + hops[m], s[i]["move"]))
        for m in range(len(sets)):
            table[m].append(rows[m])
    order = [x[0] for x in start]
    alt = [[a[0] for a in ops[x[0]]["alts"]].index(x[1][0]) for x in sorted(start, key=lambda y: y[0])]
    step = 25

    def replay(order, alt, m, first, last, old):
        c = first // step
        tab = table[m]
        if old:
            st, saved, total = old[0][:n] + old[1][c], old[1][:c], old[2]
        else:
            st, saved, total = [0.0] * (n + 37), [], 0.0
        moved, seen = [], set()
        for p in range(c * step, n, step):
            if p > last and st[n:] == old[1][p // step]:
                moved = [i for i in moved if not seen.issuperset(succ[i])]
                if not moved:
                    return st, saved + old[1][p // step:], total
            saved.append(st[n:])
            part = order[p:p + step]
            seen.update(part)
            for i in part:
                e, need, mark, d, lat, move = tab[i][alt[i]]
                s = max([st[j] for j in need]) + d
                st[e] = s
                if move:
                    s = st[n + 36] = max(s, st[n + 36]) + move
                s += lat
                if st[i] != s:
                    total += s - st[i]
                    st[i] = s
                    moved.append(i)
                for k in mark:
                    if s > st[k]:
                        st[k] = s
            st[n + 5] = 0.0
        return st, saved, total

    state = [seed]

    def rnd():
        state[0] = (state[0] * 1103515245 + 12345) % 2147483648
        return state[0] / 2147483648.0

    either = [i for i in range(n) if len(ops[i]["alts"]) > 1]
    sinks = [i for i in range(n) if not succ[i]]
    fee = [[lam * x[3] * ((1.0, 0.6, 0, 0, 0, 0) if 0 < o["tag"] < 22 or o["tag"] == 25 else (0.1, 0.1, 0, 0, 0, 0))[x[0] - n] for x in row]
           for o, row in zip(ops, table[0])]
    before, behind = [list(x) for x in pred], [list(x) for x in succ]
    for i in range(n):
        for j in range(n if ops[i]["move"] else 0):
            if ops[j].get("turn", 99) < ops[i].get("turn", 99):
                before[i].append(j)
                behind[j].append(i)

    def value(order, alt, first, last, old):
        v = sum([fee[i][alt[i]] for i in either])
        new = [replay(order, alt, m, first, last, old and old[m]) for m in range(len(sets))]
        for w, (st, _, total) in zip(weights, new):
            v += w * (max([st[i] for i in sinks]) + mu * total / n)
        return v, new

    def tight(order, alt, clock):
        m = int(rnd() * len(sets))
        st, tab = clock[m][0], table[m]
        who, last, at = {}, {}, {}
        for i in order:
            at[i] = len(at)
            e, need, mark, d, lat, move = tab[i][alt[i]]
            who[i] = [last.get(k, -1) if k >= n else k for k in need] + [last.get(n + 36, -1)]
            last[e] = i
            if move:
                last[n + 36] = i
            for k in mark:
                if k not in last or st[i] >= st[last[k]]:
                    last[k] = i
        i = max(sinks, key=lambda j: st[j])
        out = []
        while True:
            e, need, mark, d, lat, move = tab[i][alt[i]]
            s = st[i] - d - lat - move - 30.0
            c = [(j, k >= n) for j, k in zip(who[i], need + [n + 36] * (move > 0))
                 if j >= 0 and st[j] - (tab[j][alt[j]][4] if k == n + 36 else sum(tab[j][alt[j]][4:]) if k == e else 0.0) >= s]
            if not c:
                return out
            j, q = c[int(rnd() * len(c))]
            if q and lo * n <= at[j] and at[i] <= hi * n:
                out.append((j, i))
            i = j

    def shift(order, i, p):
        q = order.index(i)
        p = min(n - 1, max(0, p))
        seg, near, take = (order[p:q][::-1], behind, {i}) if p < q else (order[q + 1:p + 1], before, {i})
        for k in seg:
            if not take.isdisjoint(near[k]):
                take.add(k)
        go, stay = [k for k in seg if k in take], [k for k in seg if k not in take]
        if p < q:
            return order[:p] + go[::-1] + [i] + stay[::-1] + order[q + 1:], p, q
        return order[:q] + stay + [i] + go + order[p + 1:], q, p

    def other(alt, k):
        a = list(alt)
        a[k] = (a[k] + 1 + int(rnd() * (len(ops[k]["alts"]) - 1))) % len(ops[k]["alts"])
        return a

    cur, clock = value(order, alt, 0, n, None)
    best = (cur, order, alt, clock)
    pairs, stale = tight(order, alt, clock), 0
    for it in range(moves):
        x = rnd()
        o2, a2 = order, alt
        if x < 0.7 and pairs:
            j, i = pairs[int(rnd() * len(pairs))]
            more = int(rnd() * rnd() * 12)
            if x < 0.27:
                o2, first, last = shift(order, i, order.index(j) - more)
            elif x < 0.54:
                o2, first, last = shift(order, j, order.index(i) + more)
            else:
                k = i if rnd() < 0.5 else j
                if len(ops[k]["alts"]) < 2:
                    continue
                a2 = other(alt, k)
                first = last = order.index(k)
                if rnd() < 0.5:
                    o2, first, last = shift(order, k, first + int((rnd() - 0.5) * 24))
        elif x < 0.8:
            k = order[int((lo + (hi - lo) * rnd()) * n)]
            if len(ops[k]["alts"]) < 2:
                continue
            a2 = other(alt, k)
            first = last = order.index(k)
        else:
            k = order[int((lo + (hi - lo) * rnd()) * n)]
            o2, first, last = shift(order, k, order.index(k) + int((rnd() + rnd() - 1) * 50))
        v, c2 = value(o2, a2, first, last, clock)
        if v <= cur + temp * rnd() * rnd() * (1.0 - it / moves):
            cur, order, alt, clock = v, o2, a2, c2
            if it - stale > 40:
                pairs, stale = tight(order, alt, clock), it
            if v < best[0]:
                best = (v, o2, a2, c2)
    _, order, alt, clock = best
    st = clock[0][0]
    return [(i, ops[i]["alts"][alt[i]], st[i] - sum(table[0][i][alt[i]][3:]), st[i] - hops[0]) for i in order]


def schedule(par, costs):
    sets = [build(par, c) for c in costs]
    plan = first_order(sets[0], par, costs[0])
    for moves, temp, lam, mu, weights, lo, hi in par["search"]:
        use = [m for m, w in enumerate(weights) if w]
        plan = anneal([sets[m] for m in use], [weights[m] for m in use], [costs[m]["hop"] for m in use], plan, par["seed"], moves, temp, lam, mu, lo, hi)
    return sets[0], plan


PLAN = []


def rank_program(g, core, T, topo):
    rank = T.rank_of(core)
    if rank is None:
        return
    if not PLAN:
        PLAN.extend(schedule(PARAM, [COST, SLOW]))
    ops, order = PLAN
    nxt = T.cores[(rank + 1) % len(T.cores)]
    rid, pid = topo.addr(nxt)[0:2]
    mask = topo.mask(core, nxt)
    nen = len(topo.engines(core, nxt))
    queue = {"v": g.vector, "s": g.scalar, "t": g.tensor, "g": g, "y": g.sync}
    count = {}
    token = {}
    waited = {}
    hist = {}
    place_ = {}
    known = {}
    nd = [0]

    def r(a):
        if len(a) > 4:
            return T[a[0]][0:a[4], a[1]:a[2] - (a[2] - a[1] - 1) % a[3]:a[3]]
        return T[a[0]][:, a[1]:a[2] - (a[2] - a[1] - 1) % a[3]:a[3]] if len(a) > 3 else T[a[0]][:, a[1]:a[2]]

    def wait(e, sem, val):
        if waited.get((e, sem), 0) < val:
            queue[e].wait_ge(T.sem[sem], val)
            waited[(e, sem)] = val

    for (i, a, _, _) in order:
        o = ops[i]
        e = a[0]
        place_[i] = len(place_)
        accs = [(x, 0) for x in o["rd"]] + [(x, 1) for x in o["wr"]]
        prev = set(o["dep"])
        for x, w in accs:
            bank = isps(x)
            for (j, e2, x2, w2) in hist.get(x[0], ()):
                if ((w or w2) and meet(x, x2)) or (bank and e2 != e):
                    prev.add(j)
        for x, w in accs:
            hist.setdefault(x[0], []).append((i, e, x, w))
        if o["kind"] == "r":
            token[i] = ("a%d" % a[2], nen)
            count[token[i][0]] = nen
            continue
        for j in sorted(prev, key=lambda j: -place_[j]):
            if token[j] is not None and waited.get((e, token[j][0]), 0) < token[j][1]:
                wait(e, token[j][0], token[j][1])
                for sem, val in known.get(j, ()):
                    waited[(e, sem)] = max(waited.get((e, sem), 0), val)
        known[i] = [(k[1], v) for k, v in waited.items() if k[0] == e]
        if o["kind"] == "s":
            src, dst, k = a[2]
            g.remote_dma(r(dst), r(src), T.sem["a%d" % k], T.sem["l%d" % k], pid, rid, mask)
            token[i] = ("l%d" % k, nen)
            count[token[i][0]] = nen
            continue
        ins = a[2](queue[e], T, r)
        if o["kind"] == "d":
            sem, inc = "d%d" % nd[0], 16
            nd[0] += 1
        else:
            sem, inc = "e" + e, 1
        for x in ins:
            x.then_inc(T.sem[sem], inc)
            count[sem] = count.get(sem, 0) + inc
        token[i] = (sem, count[sem])
    for sem in sorted(count):
        g.wait_ge(T.sem[sem], count[sem])
